import numpy as np
import ml_dtypes


def mxq(x, axis, fmt="e4m3"):
    dtype, down = {"e4m3": (ml_dtypes.float8_e4m3fn, 7), "e5m2": (ml_dtypes.float8_e5m2, 14)}[fmt]
    v = np.moveaxis(np.asarray(x, np.float32).astype(ml_dtypes.bfloat16).astype(np.float64), axis, -1)
    blocks = v.reshape(v.shape[:-1] + (-1, 32))
    amax = np.abs(blocks).max(-1, keepdims=True)
    byte = np.maximum(np.where(amax > 0, np.frexp(amax)[1] - 1 + 127, 0) - down, 1)
    scale = np.exp2(byte - 127.0)
    codes = (blocks / scale).astype(np.float32).astype(dtype).astype(np.float64)
    return np.moveaxis((codes * scale).reshape(v.shape), -1, axis)


WIDE = False


def mx_kscale(k):
    if not WIDE:
        return np.ones(k)
    levels = np.array([10, -10, 5, -5, 0])
    if k % 512:
        return np.exp2(np.random.permutation(np.resize(levels, k // 32))).repeat(32)
    a = np.empty((k // 512, 16))
    for p in range(k // 512):
        a[p, :8] = np.random.permutation(np.resize(levels, 8))
        for g in range(8):
            far = levels[np.abs(levels - a[p, g]) >= 10]
            a[p, g + 8] = far[np.random.randint(len(far))]
    return np.exp2(a.ravel()).repeat(32)


def f64(x):
    return np.asarray(x).astype(np.float64)


def striped(idx):
    return np.tile(idx.reshape(-1, 16).T, (8, 1)).astype(np.uint16)


def unstriped(offs):
    return offs[:16].T.reshape(-1).astype(np.int64)


E2M1 = np.array([0.0, 0.5, 1.0, 1.5, 2.0, 3.0, 4.0, 6.0, -0.0, -0.5, -1.0, -1.5, -2.0, -3.0, -4.0, -6.0])


def pack_weight(w, fmt):
    k, n = w.shape
    w = f64(np.asarray(w, np.float32).astype(ml_dtypes.bfloat16)).reshape(k // 32, 32, n)
    amax = np.abs(w).max(1)
    if fmt == "e4m3":
        byte = np.frexp(amax)[1] - 1 + 127 - 7
    else:
        mant, ex = np.frexp(amax / 6.0)
        byte = np.where(mant > 0.5, ex, ex - 1) + 127
    byte = np.clip(np.where(amax > 0, byte, 1), 1, 254)
    scaled = (w * np.exp2(127.0 - byte)[:, None, :]).reshape(k, n).astype(np.float32)
    by_word = np.ascontiguousarray(scaled.reshape(k // 512, 128, 4, n).transpose(0, 1, 3, 2))
    if fmt == "e4m3":
        words = by_word.astype(ml_dtypes.float8_e4m3fn).view(np.uint8)
    else:
        c = by_word.astype(ml_dtypes.float4_e2m1fn).view(np.uint8) & 0xF
        words = (c[..., 0::2] | (c[..., 1::2] << 4)).reshape(k // 512, 128, 2 * n)
    return np.ascontiguousarray(words), np.ascontiguousarray(byte.astype(np.uint8).reshape(k // 512, 16, n))


def unpack_weight(words, scales, fmt):
    g, _, n = scales.shape
    words = np.ascontiguousarray(words).reshape(g, 128, n, -1)
    if fmt == "e4m3":
        vals = words.view(ml_dtypes.float8_e4m3fn).astype(np.float64)
    else:
        nib = np.empty((g, 128, n, 4), np.uint8)
        nib[..., 0::2] = words & 0xF
        nib[..., 1::2] = words >> 4
        vals = E2M1[nib]
    vals = vals * np.repeat(np.exp2(scales.astype(np.float64) - 127.0), 8, axis=1)[..., None]
    return vals.transpose(0, 1, 3, 2).reshape(g * 512, n)


def d_relu2(v):
    return 2.0 * np.maximum(v, 0.0)


K, T, E1, C1, E2, C2, H = 512, 768, 3, 256, 3, 256, 512
N = 512


def by_expert(wq, xq, E, C):
    return np.concatenate([wq[e].T @ xq[:, e * C:(e + 1) * C] for e in range(E)], axis=1)


def setup_inputs():
    n = np.random.standard_normal
    v = mx_kscale(N)
    u = mx_kscale(H)
    slots1, slots2 = np.random.permutation(T), np.random.permutation(T)
    dy = pack_weight(n((N, T)) * v[:, None], "e4m3")
    w2t = [pack_weight(m, "e4m3") for m in n((E2, N, H)) / np.sqrt(N) / v[None, :, None] * u]
    w1t = [pack_weight(m, "e2m1") for m in n((E1, H, K)) / np.sqrt(H) / u[None, :, None]]
    return {
        "dy_words": dy[0],
        "dy_scales": dy[1],
        "w2t_words": np.stack([m[0] for m in w2t]),
        "w2t_scales": np.stack([m[1] for m in w2t]),
        "w1t_words": np.stack([m[0] for m in w1t]),
        "w1t_scales": np.stack([m[1] for m in w1t]),
        "a": (n((H, T))).astype(np.float32),
        "gate1": (np.tile(np.random.uniform(0.2, 1.0, T), (128, 1))).astype(np.float32),
        "gate2": (np.tile(np.random.uniform(0.2, 1.0, T), (128, 1))).astype(np.float32),
        "offs": striped(slots1),
        "offs2": striped(slots2),
    }


def reference(dy_words, dy_scales, w2t_words, w2t_scales, w1t_words, w1t_scales, a, gate1, gate2, offs, offs2):
    w2t = np.stack([unpack_weight(w2t_words[e], w2t_scales[e], "e4m3") for e in range(E2)])
    w1t = np.stack([unpack_weight(w1t_words[e], w1t_scales[e], "e2m1") for e in range(E1)])
    idx, idx2 = unstriped(offs), unstriped(offs2)
    gq = unpack_weight(dy_words, dy_scales, "e4m3")[:, idx2]
    dc = np.zeros((H, T))
    dc[:, idx2] = f64(gate2[:1]) * by_expert(w2t, gq, E2, C2)
    da = f64(gate1[:1]) * dc[:, idx] * d_relu2(f64(a))
    out = np.zeros((K, T))
    out[:, idx] = by_expert(w1t, mxq(da, 0, "e4m3"), E1, C1)
    return out

@@ -1,0 +1,208 @@
+from contextlib import ExitStack
+
+import concourse.mybir as mybir
+
+F32 = mybir.dt.float32
+BF16 = mybir.dt.bfloat16
+I32 = mybir.dt.int32
+U32 = mybir.dt.uint32
+U16 = mybir.dt.uint16
+U8 = mybir.dt.uint8
+FP8X4 = mybir.dt.float8_e4m3fn_x4
+FP4X4 = mybir.dt.float4_e2m1fn_x4
+COPY = mybir.ActivationFunctionType.Copy
+RELU = mybir.ActivationFunctionType.Relu
+MULT = mybir.AluOpType.mult
+
+P = 128
+PACK = 4
+T = 768
+E = 3
+C = 256
+W = 512
+REST = T - C
+FLOPS = 2 * 2 * W * W * T
+
+
+def tile_moe_seb_relu2_kernel(
+    tc, dy_words, dy_scales, w2t_words, w2t_scales, w1t_words, w1t_scales, a, gate1, gate2, offs, offs2, out
+):
+    nc = tc.nc
+    with ExitStack() as ctx:
+        sb = ctx.enter_context(tc.tile_pool(name="sb", bufs=1))
+        ps = ctx.enter_context(tc.psum_pool(name="ps", bufs=1))
+
+        def bank(n):
+            return ps.tile([P, W], F32, name="bank%d" % n, tag="bank%d" % n)
+
+        def entries(lst, lo, hi):
+            return lst[:, lo // 16 : hi // 16]
+
+        dy_plane = sb.tile([P, T], U8, name="dy_plane", tag="dy_plane", align_bytes=64)
+        w2_plane = sb.tile([P, E, W], U8, name="w2_plane", align_bytes=64)
+        nc.gpsimd.memset(dy_plane[:].bitcast(I32), 0)
+        nc.gpsimd.memset(w2_plane[:].bitcast(I32), 0)
+        zeros = sb.tile([P, P], F32, name="zeros", tag="zeros", align_bytes=64)
+        nc.vector.memset(zeros[:], 0.0)
+        gate_rows = sb.tile([P, P], F32, name="gate_rows", tag="gate_rows", align_bytes=64)
+        nc.vector.memset(gate_rows[:], 0.0)
+        ident = sb.tile([P, P], F32, name="ident")
+        nc.gpsimd.affine_select(
+            out=ident[:], in_=zeros[:], compare_op=mybir.AluOpType.not_equal, fill=1.0, base=0, pattern=[[-1, P]], channel_multiplier=1
+        )
+        nc.gpsimd.dma_start(gate_rows[0 : T // P, :], gate2[0, :].rearrange("(b c) -> b c", c=P))
+
+        list2 = sb.tile([P, T // 16], U16, name="list2")
+        nc.sync.dma_start(list2[:], offs2)
+        list1 = sb.tile([P, T // 16], U16, name="list1")
+        nc.sync.dma_start(list1[:], offs)
+        dy_tile = sb.tile([P, T], I32, name="dy_tile", tag="dy_tile", align_bytes=64)
+        nc.sync.dma_start(dy_tile[:], dy_words[0].rearrange("p t d -> p (t d)").bitcast(I32))
+        w2_first = sb.tile([P, W], I32, name="w2_first", align_bytes=64)
+        nc.sync.dma_start(w2_first[:], w2t_words[0, 0].rearrange("p i d -> p (i d)").bitcast(I32))
+        for q in range(4):
+            nc.scalar.dma_start(dy_plane[:].bitcast(I32)[32 * q : 32 * q + 4, :], dy_scales[0, 4 * q : 4 * q + 4, :].bitcast(I32))
+        for q in range(4):
+            nc.sync.dma_start(
+                w2_plane[:].bitcast(I32)[32 * q : 32 * q + 4, :, :],
+                w2t_scales[:, 0, 4 * q : 4 * q + 4, :].rearrange("e r i -> r e i").bitcast(I32),
+            )
+        w2_rest = sb.tile([P, E - 1, W], I32, name="w2_rest", tag="zeros", align_bytes=64)
+        nc.sync.dma_start(w2_rest[:], w2t_words[1:E, 0].rearrange("e p i d -> p e (i d)").bitcast(I32))
+        w2 = [w2_first[:], w2_rest[:, 0, :], w2_rest[:, 1, :]]
+
+        warm = sb.tile([P, 1], F32, name="warm")
+        nc.scalar.activation(warm[:], ident[:, 0:1], COPY)
+
+        gate_ps = bank(0)
+        nc.tensor.transpose(gate_ps[:, 0:P], gate_rows[:], ident[:])
+        gate_col = sb.tile([P, 8], F32, name="gate_col")
+        nc.scalar.activation(gate_col[:], gate_ps[:, 0:8], COPY)
+
+        groups = ((0, C), (C, T))
+        runs = ((0, P), (P, 3 * P), (3 * P, T))
+        gw, gs = [], []
+        for n, (lo, hi) in enumerate(runs):
+            words = sb.tile([P, hi - lo], U32, name="gw_%d" % n, tag="gw_%d" % n, align_bytes=64)
+            nc.vector.tensor_copy(words[:], dy_tile[:].bitcast(U32).indirect(entries(list2, lo, hi)))
+            scal = sb.tile([P, hi - lo], U8, name="gs_%d" % n, tag="gs_%d" % n, align_bytes=64)
+            nc.vector.tensor_copy(scal[:], dy_plane[:].indirect(entries(list2, lo, hi)))
+            gw.append(words)
+            gs.append(scal)
+
+        dc = [sb.tile([P, T], F32, name="dc_%d" % d) for d in range(PACK)]
+
+        def second_layer(n, sum_banks, back_banks):
+            lo, hi = runs[n]
+            turned = []
+            for b in range((hi - lo) // P):
+                blk = lo // P + b
+                e = blk * P // C
+                acc = bank(sum_banks[b])
+                nc.tensor.matmul_mx(
+                    out=acc[:],
+                    lhsT=gw[n][:, b * P : (b + 1) * P].bitcast(FP8X4),
+                    lhsT_scale=gs[n][:, b * P : (b + 1) * P],
+                    rhs=w2[e].bitcast(FP8X4),
+                    rhs_scale=w2_plane[:, e, :],
+                    start=True,
+                    stop=True,
+                )
+                y = sb.tile([P, PACK, P], F32, name="y_%d" % blk, tag="y_%d" % blk, align_bytes=64)
+                by_plane = acc[:].rearrange("p (m d) -> p d m", d=PACK)
+                for d0, d1 in ((0, 1), (1, PACK)) if blk == 0 else ((0, PACK),):
+                    nc.scalar.activation(y[:, d0:d1, :], by_plane[:, d0:d1, :], COPY, scale=gate_col[:, blk : blk + 1])
+                turned.append(y)
+            for d in range(PACK):
+                back = bank(back_banks[d])
+                for b, y in enumerate(turned):
+                    nc.tensor.transpose(back[:, b * P : (b + 1) * P], y[:, d, :], ident[:])
+                src = sb.tile([P, hi - lo], F32, name="src_%d_%d" % (n, d), tag="src_%d_%d" % (n, d), align_bytes=64)
+                nc.scalar.activation(src[:], back[:, 0 : hi - lo], COPY)
+                nc.vector.tensor_copy(dc[d][:].indirect(entries(list2, lo, hi)), src[:])
+
+        second_layer(0, (0,), (1, 2, 3, 4))
+        second_layer(1, (0, 1), (5, 6, 7, 2))
+        second_layer(2, (5, 6, 7), (0, 1, 3, 4))
+
+        a_rows = a.rearrange("(p d) j -> p d j", d=PACK)
+        g1 = sb.tile([P, T], F32, name="g1", tag="y_0", align_bytes=64)
+        nc.sync.dma_start(g1[:], gate1)
+        a_sb = []
+        for d, tag in enumerate(("src_0_0", "src_0_1", "src_0_2", "src_0_3")):
+            rows = sb.tile([P, T], F32, name="a_%d" % d, tag=tag, align_bytes=64)
+            nc.sync.dma_start(rows[:], a_rows[:, d, :])
+            a_sb.append(rows)
+        w1 = sb.tile([P, E, 2 * W], U8, name="w1", tag="y_1", align_bytes=64)
+        nc.sync.dma_start(w1[:].bitcast(I32), w1t_words[:, 0].rearrange("e p b -> p e b").bitcast(I32))
+        w1_plane = sb.tile([P, E, W], U8, name="w1_plane", tag="gw_1", align_bytes=64)
+        nc.gpsimd.memset(w1_plane[:].bitcast(I32), 0)
+        for q in range(4):
+            nc.sync.dma_start(
+                w1_plane[:].bitcast(I32)[32 * q : 32 * q + 4, :, :],
+                w1t_scales[:, 0, 4 * q : 4 * q + 4, :].rearrange("e r i -> r e i").bitcast(I32),
+            )
+
+        m_first = sb.tile([P, PACK, C], F32, name="m_first", tag="m_first")
+        m_rest = sb.tile([P, PACK, REST], F32, name="m_rest")
+        relus = [sb.tile([P, 2, T], F32, name="relu_%d" % x, tag="y_%d" % (4 + x), align_bytes=64) for x in range(2)]
+        for d in range(PACK):
+            r = relus[d // 2][:, d % 2, :]
+            nc.scalar.activation(r, a_sb[d][:], RELU, scale=2.0)
+            nc.gpsimd.tensor_tensor(m_first[:, d, :], r[:, 0:C], g1[:, 0:C], MULT)
+            nc.gpsimd.tensor_tensor(m_rest[:, d, :], r[:, C:T], g1[:, C:T], MULT)
+
+        def round_interleave(dst, src):
+            nc.scalar.activation(
+                dst[:].rearrange("p (c i) d -> p c d i", i=4), src[:].rearrange("p d (c i) -> p c d i", i=4), COPY
+            )
+
+        def quantise(n, h):
+            lo, hi = groups[n]
+            codes = sb.tile([P, hi - lo], U32, name="codes_%d" % n, align_bytes=64)
+            plane = sb.tile([P, hi - lo], U8, name="plane_%d" % n, align_bytes=64)
+            nc.vector.quantize_mx(out=codes[:].bitcast(FP8X4), scales=plane[:], in_=h[:].rearrange("p j d -> p (j d)"))
+            return codes, plane
+
+        def first_layer(n, kb, codes, plane):
+            lo, hi = groups[n]
+            acc = bank(4 * (1 - n) + kb)
+            for x in range((hi - lo) // C):
+                e = lo // C + x
+                nc.tensor.matmul_mx(
+                    out=acc[:, x * C : (x + 1) * C],
+                    lhsT=w1[:, e, 2 * kb * P : 2 * (kb + 1) * P].bitcast(FP4X4),
+                    lhsT_scale=w1_plane[:, e, kb * P : (kb + 1) * P],
+                    rhs=codes[:, x * C : (x + 1) * C].bitcast(FP8X4),
+                    rhs_scale=plane[:, x * C : (x + 1) * C],
+                    start=True,
+                    stop=True,
+                )
+            res = sb.tile([P, hi - lo], F32, name="res_%d_%d" % (n, kb))
+            nc.scalar.activation(res[:], acc[:, 0 : hi - lo], COPY)
+            return res
+
+        da_first = sb.tile([P, PACK, C], F32, name="da_first", tag="src_2_3", align_bytes=64)
+        for d in range(PACK):
+            nc.vector.tensor_tensor(da_first[:, d, :], dc[d][:].indirect(entries(list1, 0, C)), m_first[:, d, :], MULT)
+        h_first = sb.tile([P, C, PACK], BF16, name="h_first", align_bytes=64)
+        round_interleave(h_first, da_first)
+        codes0, plane0 = quantise(0, h_first)
+        res0 = [first_layer(0, kb, codes0, plane0) for kb in range(W // P)]
+
+        da_rest = sb.tile([P, PACK, REST], F32, name="da_rest", tag="m_first")
+        for d in range(PACK):
+            nc.vector.tensor_tensor(da_rest[:, d, :], dc[d][:].indirect(entries(list1, C, T)), m_rest[:, d, :], MULT)
+        h_rest = sb.tile([P, REST, PACK], BF16, name="h_rest", tag="h_rest", align_bytes=64)
+        round_interleave(h_rest, da_rest)
+
+        dx = [sb.tile([P, T], F32, name="dx_%d" % kb) for kb in range(W // P - 1)]
+        for kb in range(W // P - 1):
+            nc.vector.tensor_copy(dx[kb][:].indirect(entries(list1, 0, C)), res0[kb][:])
+        codes1, plane1 = quantise(1, h_rest)
+        dx.append(sb.tile([P, T], F32, name="dx_last", tag="h_rest", align_bytes=64))
+        nc.vector.tensor_copy(dx[-1][:].indirect(entries(list1, 0, C)), res0[-1][:])
+        for kb in range(W // P):
+            res = first_layer(1, kb, codes1, plane1)
+            nc.vector.tensor_copy(dx[kb][:].indirect(entries(list1, C, T)), res[:])
+            nc.sync.dma_start(out[kb * P : (kb + 1) * P, :], dx[kb][:])

@@ -40,10 +40,10 @@ def tile_moe_seb_relu2_kernel(
 
         dy_plane = sb.tile([P, T], U8, name="dy_plane", tag="dy_plane", align_bytes=64)
         w2_plane = sb.tile([P, E, W], U8, name="w2_plane", align_bytes=64)
-        nc.gpsimd.memset(dy_plane[:].bitcast(I32), 0)
+        nc.vector.memset(dy_plane[:].bitcast(I32), 0)
         nc.gpsimd.memset(w2_plane[:].bitcast(I32), 0)
         zeros = sb.tile([P, P], F32, name="zeros", tag="zeros", align_bytes=64)
-        nc.vector.memset(zeros[:], 0.0)
+        nc.gpsimd.memset(zeros[:], 0.0)
         gate_rows = sb.tile([P, P], F32, name="gate_rows", tag="gate_rows", align_bytes=64)
         nc.vector.memset(gate_rows[:], 0.0)
         ident = sb.tile([P, P], F32, name="ident")
@@ -143,7 +143,7 @@ def tile_moe_seb_relu2_kernel(
                 w1t_scales[:, 0, 4 * q : 4 * q + 4, :].rearrange("e r i -> r e i").bitcast(I32),
             )
 
-        m_first = sb.tile([P, PACK, C], F32, name="m_first", tag="m_first")
+        m_first = sb.tile([P, PACK, C], F32, name="m_first", tag="m_first", align_bytes=64)
         m_rest = sb.tile([P, PACK, REST], F32, name="m_rest")
         relus = [sb.tile([P, 2, T], F32, name="relu_%d" % x, tag="y_%d" % (4 + x), align_bytes=64) for x in range(2)]
         for d in range(PACK):
@@ -157,52 +157,51 @@ def tile_moe_seb_relu2_kernel(
                 dst[:].rearrange("p (c i) d -> p c d i", i=4), src[:].rearrange("p d (c i) -> p c d i", i=4), COPY
             )
 
-        def quantise(n, h):
-            lo, hi = groups[n]
-            codes = sb.tile([P, hi - lo], U32, name="codes_%d" % n, align_bytes=64)
-            plane = sb.tile([P, hi - lo], U8, name="plane_%d" % n, align_bytes=64)
+        def gather_da(e, factor, tag):
+            da = sb.tile([P, PACK, C], F32, name="da_%d" % e, tag=tag, align_bytes=64)
+            for d in range(PACK):
+                nc.vector.tensor_tensor(da[:, d, :], dc[d][:].indirect(entries(list1, e * C, (e + 1) * C)), factor(d), MULT)
+            h = sb.tile([P, C, PACK], BF16, name="h_%d" % e, tag="h_%d" % e, align_bytes=64)
+            round_interleave(h, da)
+            return h
+
+        def quantise(e, h):
+            codes = sb.tile([P, C], U32, name="codes_%d" % e, align_bytes=64)
+            plane = sb.tile([P, C], U8, name="plane_%d" % e, align_bytes=64)
             nc.vector.quantize_mx(out=codes[:].bitcast(FP8X4), scales=plane[:], in_=h[:].rearrange("p j d -> p (j d)"))
             return codes, plane
 
-        def first_layer(n, kb, codes, plane):
-            lo, hi = groups[n]
-            acc = bank(4 * (1 - n) + kb)
-            for x in range((hi - lo) // C):
-                e = lo // C + x
+        def first_layer(kb, experts, quantised, bank_no):
+            acc = bank(bank_no)
+            for x, e in enumerate(experts):
+                codes, plane = quantised[e]
                 nc.tensor.matmul_mx(
                     out=acc[:, x * C : (x + 1) * C],
                     lhsT=w1[:, e, 2 * kb * P : 2 * (kb + 1) * P].bitcast(FP4X4),
                     lhsT_scale=w1_plane[:, e, kb * P : (kb + 1) * P],
-                    rhs=codes[:, x * C : (x + 1) * C].bitcast(FP8X4),
-                    rhs_scale=plane[:, x * C : (x + 1) * C],
+                    rhs=codes[:].bitcast(FP8X4),
+                    rhs_scale=plane[:],
                     start=True,
                     stop=True,
                 )
-            res = sb.tile([P, hi - lo], F32, name="res_%d_%d" % (n, kb))
-            nc.scalar.activation(res[:], acc[:, 0 : hi - lo], COPY)
+            res = sb.tile([P, len(experts) * C], F32, name="res_%d_%d" % (experts[0], kb))
+            nc.scalar.activation(res[:], acc[:, 0 : len(experts) * C], COPY)
             return res
 
-        da_first = sb.tile([P, PACK, C], F32, name="da_first", tag="src_2_3", align_bytes=64)
-        for d in range(PACK):
-            nc.vector.tensor_tensor(da_first[:, d, :], dc[d][:].indirect(entries(list1, 0, C)), m_first[:, d, :], MULT)
-        h_first = sb.tile([P, C, PACK], BF16, name="h_first", align_bytes=64)
-        round_interleave(h_first, da_first)
-        codes0, plane0 = quantise(0, h_first)
-        res0 = [first_layer(0, kb, codes0, plane0) for kb in range(W // P)]
-
-        da_rest = sb.tile([P, PACK, REST], F32, name="da_rest", tag="m_first")
-        for d in range(PACK):
-            nc.vector.tensor_tensor(da_rest[:, d, :], dc[d][:].indirect(entries(list1, C, T)), m_rest[:, d, :], MULT)
-        h_rest = sb.tile([P, REST, PACK], BF16, name="h_rest", tag="h_rest", align_bytes=64)
-        round_interleave(h_rest, da_rest)
+        h0 = gather_da(0, lambda d: m_first[:, d, :], "da_0")
+        h1 = gather_da(1, lambda d: m_rest[:, d, 0:C], "m_first")
+        quantised = [quantise(0, h0)]
+        res0 = [first_layer(kb, (0,), quantised, 4 + kb) for kb in range(W // P)]
+        h2 = gather_da(2, lambda d: m_rest[:, d, C:REST], "h_0")
+        quantised.append(quantise(1, h1))
 
         dx = [sb.tile([P, T], F32, name="dx_%d" % kb) for kb in range(W // P - 1)]
         for kb in range(W // P - 1):
             nc.vector.tensor_copy(dx[kb][:].indirect(entries(list1, 0, C)), res0[kb][:])
-        codes1, plane1 = quantise(1, h_rest)
-        dx.append(sb.tile([P, T], F32, name="dx_last", tag="h_rest", align_bytes=64))
+        quantised.append(quantise(2, h2))
+        dx.append(sb.tile([P, T], F32, name="dx_last", tag="h_2", align_bytes=64))
         nc.vector.tensor_copy(dx[-1][:].indirect(entries(list1, 0, C)), res0[-1][:])
         for kb in range(W // P):
-            res = first_layer(1, kb, codes1, plane1)
+            res = first_layer(kb, (1, 2), quantised, kb)
             nc.vector.tensor_copy(dx[kb][:].indirect(entries(list1, C, T)), res[:])
             nc.sync.dma_start(out[kb * P : (kb + 1) * P, :], dx[kb][:])

@@ -20,7 +20,7 @@ T = 768
 E = 3
 C = 256
 W = 512
-REST = T - C
+WIDE = 1024
 FLOPS = 2 * 2 * W * W * T
 
 
@@ -30,178 +30,188 @@ def tile_moe_seb_relu2_kernel(
     nc = tc.nc
     with ExitStack() as ctx:
         sb = ctx.enter_context(tc.tile_pool(name="sb", bufs=1))
+        shared = ctx.enter_context(tc.tile_pool(name="shared", bufs=1))
         ps = ctx.enter_context(tc.psum_pool(name="ps", bufs=1))
 
         def bank(n):
             return ps.tile([P, W], F32, name="bank%d" % n, tag="bank%d" % n)
 
+        def placed(name, shape, dtype, offset):
+            return shared.tile(shape, dtype, name=name, offset=offset, align_bytes=64)
+
         def entries(lst, lo, hi):
             return lst[:, lo // 16 : hi // 16]
 
-        dy_plane = sb.tile([P, T], U8, name="dy_plane", tag="dy_plane", align_bytes=64)
-        w2_plane = sb.tile([P, E, W], U8, name="w2_plane", align_bytes=64)
-        nc.vector.memset(dy_plane[:].bitcast(I32), 0)
-        nc.gpsimd.memset(w2_plane[:].bitcast(I32), 0)
-        zeros = sb.tile([P, P], F32, name="zeros", tag="zeros", align_bytes=64)
-        nc.gpsimd.memset(zeros[:], 0.0)
-        gate_rows = sb.tile([P, P], F32, name="gate_rows", tag="gate_rows", align_bytes=64)
-        nc.vector.memset(gate_rows[:], 0.0)
+        def scale_rows(engine, plane, rows, q):
+            engine.dma_start(
+                plane[:].bitcast(I32)[32 * q : 32 * q + 4, :, :],
+                rows[:, 0, 4 * q : 4 * q + 4, :].rearrange("e r i -> r e i").bitcast(I32),
+            )
+
+        dy_plane = placed("dy_plane", [P, WIDE], U8, 960)
+        w2_plane = placed("w2_plane", [P, E, W], U8, 22528)
         ident = sb.tile([P, P], F32, name="ident")
-        nc.gpsimd.affine_select(
-            out=ident[:], in_=zeros[:], compare_op=mybir.AluOpType.not_equal, fill=1.0, base=0, pattern=[[-1, P]], channel_multiplier=1
-        )
-        nc.gpsimd.dma_start(gate_rows[0 : T // P, :], gate2[0, :].rearrange("(b c) -> b c", c=P))
+
+        def identity_half(x, offset, span):
+            zeros = placed("zeros_%d" % x, [P, span // 4], F32, offset)[:, 0 : P // 2]
+            nc.gpsimd.memset(zeros, 0.0)
+            nc.gpsimd.affine_select(
+                out=ident[:, x * P // 2 : (x + 1) * P // 2],
+                in_=zeros,
+                compare_op=mybir.AluOpType.not_equal,
+                fill=1.0,
+                base=-x * P // 2,
+                pattern=[[-1, P // 2]],
+                channel_multiplier=1,
+            )
+
+        nc.gpsimd.memset(dy_plane[:].bitcast(I32), 0)
+        identity_half(0, 22400, 26176 - 22400)
+        nc.gpsimd.memset(w2_plane[:].bitcast(I32), 0)
+        identity_half(1, 26112, 29312 - 26112)
 
         list2 = sb.tile([P, T // 16], U16, name="list2")
         nc.sync.dma_start(list2[:], offs2)
         list1 = sb.tile([P, T // 16], U16, name="list1")
         nc.sync.dma_start(list1[:], offs)
-        dy_tile = sb.tile([P, T], I32, name="dy_tile", tag="dy_tile", align_bytes=64)
+        dy_tile = placed("dy_tile", [P, T], I32, 19392)
         nc.sync.dma_start(dy_tile[:], dy_words[0].rearrange("p t d -> p (t d)").bitcast(I32))
-        w2_first = sb.tile([P, W], I32, name="w2_first", align_bytes=64)
+        w2_first = placed("w2_first", [P, W], I32, 24064)
         nc.sync.dma_start(w2_first[:], w2t_words[0, 0].rearrange("p i d -> p (i d)").bitcast(I32))
         for q in range(4):
-            nc.scalar.dma_start(dy_plane[:].bitcast(I32)[32 * q : 32 * q + 4, :], dy_scales[0, 4 * q : 4 * q + 4, :].bitcast(I32))
+            (nc.scalar if q < 2 else nc.sync).dma_start(dy_plane[:, 0:T].bitcast(I32)[32 * q : 32 * q + 4, :], dy_scales[0, 4 * q : 4 * q + 4, :].bitcast(I32))
         for q in range(4):
-            nc.sync.dma_start(
-                w2_plane[:].bitcast(I32)[32 * q : 32 * q + 4, :, :],
-                w2t_scales[:, 0, 4 * q : 4 * q + 4, :].rearrange("e r i -> r e i").bitcast(I32),
-            )
-        w2_rest = sb.tile([P, E - 1, W], I32, name="w2_rest", tag="zeros", align_bytes=64)
+            scale_rows(nc.sync if q % 2 == 0 else nc.scalar, w2_plane, w2t_scales, q)
+        g2 = placed("g2", [P, T], F32, 26176)
+        nc.sync.dma_start(g2[:, 0:C], gate2[:, 0:C])
+        w2_rest = placed("w2_rest", [P, E - 1, W], I32, 29248)
         nc.sync.dma_start(w2_rest[:], w2t_words[1:E, 0].rearrange("e p i d -> p e (i d)").bitcast(I32))
+        nc.sync.dma_start(g2[:, C:T], gate2[:, C:T])
         w2 = [w2_first[:], w2_rest[:, 0, :], w2_rest[:, 1, :]]
 
-        warm = sb.tile([P, 1], F32, name="warm")
-        nc.scalar.activation(warm[:], ident[:, 0:1], COPY)
-
-        gate_ps = bank(0)
-        nc.tensor.transpose(gate_ps[:, 0:P], gate_rows[:], ident[:])
-        gate_col = sb.tile([P, 8], F32, name="gate_col")
-        nc.scalar.activation(gate_col[:], gate_ps[:, 0:8], COPY)
-
+        gs = sb.tile([P, T], U8, name="gs", tag="gs", align_bytes=64)
+        nc.vector.tensor_copy(gs[:], dy_plane[:].indirect(list2[:]))
         groups = ((0, C), (C, T))
-        runs = ((0, P), (P, 3 * P), (3 * P, T))
-        gw, gs = [], []
-        for n, (lo, hi) in enumerate(runs):
-            words = sb.tile([P, hi - lo], U32, name="gw_%d" % n, tag="gw_%d" % n, align_bytes=64)
+        gw = []
+        for lo, hi in groups:
+            words = placed("gw_%d" % lo, [P, hi - lo], U32, 4 * lo)
             nc.vector.tensor_copy(words[:], dy_tile[:].bitcast(U32).indirect(entries(list2, lo, hi)))
-            scal = sb.tile([P, hi - lo], U8, name="gs_%d" % n, tag="gs_%d" % n, align_bytes=64)
-            nc.vector.tensor_copy(scal[:], dy_plane[:].indirect(entries(list2, lo, hi)))
             gw.append(words)
-            gs.append(scal)
 
-        dc = [sb.tile([P, T], F32, name="dc_%d" % d) for d in range(PACK)]
+        dc = [sb.tile([P, WIDE], F32, name="dc_%d" % c) for c in range(PACK)]
+        for n, (lo, hi) in enumerate(groups):
+            for c in range(PACK):
+                acc = bank(PACK * n + c)
+                for e in range(lo // C, hi // C):
+                    nc.tensor.matmul_mx(
+                        out=acc[:, e * C - lo : (e + 1) * C - lo],
+                        lhsT=w2[e][:, c * P : (c + 1) * P].bitcast(FP8X4),
+                        lhsT_scale=w2_plane[:, e, c * P : (c + 1) * P],
+                        rhs=gw[n][:, e * C - lo : (e + 1) * C - lo].bitcast(FP8X4),
+                        rhs_scale=gs[:, e * C : (e + 1) * C],
+                        start=True,
+                        stop=True,
+                    )
+                src = sb.tile([P, hi - lo], F32, name="src_%d_%d" % (n, c), tag="src_%d_%d" % (n, c), align_bytes=64)
+                nc.scalar.activation(src[:], acc[:, 0 : hi - lo], COPY)
+                nc.vector.tensor_tensor(dc[c][:].indirect(entries(list2, lo, hi)), src[:], g2[:, lo:hi], MULT)
 
-        def second_layer(n, sum_banks, back_banks):
-            lo, hi = runs[n]
-            turned = []
-            for b in range((hi - lo) // P):
-                blk = lo // P + b
-                e = blk * P // C
-                acc = bank(sum_banks[b])
-                nc.tensor.matmul_mx(
-                    out=acc[:],
-                    lhsT=gw[n][:, b * P : (b + 1) * P].bitcast(FP8X4),
-                    lhsT_scale=gs[n][:, b * P : (b + 1) * P],
-                    rhs=w2[e].bitcast(FP8X4),
-                    rhs_scale=w2_plane[:, e, :],
-                    start=True,
-                    stop=True,
-                )
-                y = sb.tile([P, PACK, P], F32, name="y_%d" % blk, tag="y_%d" % blk, align_bytes=64)
-                by_plane = acc[:].rearrange("p (m d) -> p d m", d=PACK)
-                for d0, d1 in ((0, 1), (1, PACK)) if blk == 0 else ((0, PACK),):
-                    nc.scalar.activation(y[:, d0:d1, :], by_plane[:, d0:d1, :], COPY, scale=gate_col[:, blk : blk + 1])
-                turned.append(y)
-            for d in range(PACK):
-                back = bank(back_banks[d])
-                for b, y in enumerate(turned):
-                    nc.tensor.transpose(back[:, b * P : (b + 1) * P], y[:, d, :], ident[:])
-                src = sb.tile([P, hi - lo], F32, name="src_%d_%d" % (n, d), tag="src_%d_%d" % (n, d), align_bytes=64)
-                nc.scalar.activation(src[:], back[:, 0 : hi - lo], COPY)
-                nc.vector.tensor_copy(dc[d][:].indirect(entries(list2, lo, hi)), src[:])
-
-        second_layer(0, (0,), (1, 2, 3, 4))
-        second_layer(1, (0, 1), (5, 6, 7, 2))
-        second_layer(2, (5, 6, 7), (0, 1, 3, 4))
-
-        a_rows = a.rearrange("(p d) j -> p d j", d=PACK)
-        g1 = sb.tile([P, T], F32, name="g1", tag="y_0", align_bytes=64)
-        nc.sync.dma_start(g1[:], gate1)
-        a_sb = []
-        for d, tag in enumerate(("src_0_0", "src_0_1", "src_0_2", "src_0_3")):
-            rows = sb.tile([P, T], F32, name="a_%d" % d, tag=tag, align_bytes=64)
-            nc.sync.dma_start(rows[:], a_rows[:, d, :])
-            a_sb.append(rows)
-        w1 = sb.tile([P, E, 2 * W], U8, name="w1", tag="y_1", align_bytes=64)
+        a_sb = placed("a_sb", [P, PACK, T], F32, 7168)
+        nc.sync.dma_start(a_sb[:], a.rearrange("(c p) j -> p c j", p=P))
+        w1 = placed("w1", [P, E, 2 * W], U8, 19456)
         nc.sync.dma_start(w1[:].bitcast(I32), w1t_words[:, 0].rearrange("e p b -> p e b").bitcast(I32))
-        w1_plane = sb.tile([P, E, W], U8, name="w1_plane", tag="gw_1", align_bytes=64)
+        g1 = sb.tile([P, T // P], F32, name="g1", tag="src_0_0", align_bytes=64)
+        with nc.allow_non_contiguous_dma(reason="one gate value a partition"):
+            nc.sync.dma_start(g1[:], gate1[0, :].rearrange("(b p) -> p b", p=P))
+        w1_plane = sb.tile([P, E, W], U8, name="w1_plane", tag="gs", align_bytes=64)
         nc.gpsimd.memset(w1_plane[:].bitcast(I32), 0)
         for q in range(4):
-            nc.sync.dma_start(
-                w1_plane[:].bitcast(I32)[32 * q : 32 * q + 4, :, :],
-                w1t_scales[:, 0, 4 * q : 4 * q + 4, :].rearrange("e r i -> r e i").bitcast(I32),
-            )
+            scale_rows(nc.sync, w1_plane, w1t_scales, q)
 
-        m_first = sb.tile([P, PACK, C], F32, name="m_first", tag="m_first", align_bytes=64)
-        m_rest = sb.tile([P, PACK, REST], F32, name="m_rest")
-        relus = [sb.tile([P, 2, T], F32, name="relu_%d" % x, tag="y_%d" % (4 + x), align_bytes=64) for x in range(2)]
-        for d in range(PACK):
-            r = relus[d // 2][:, d % 2, :]
-            nc.scalar.activation(r, a_sb[d][:], RELU, scale=2.0)
-            nc.gpsimd.tensor_tensor(m_first[:, d, :], r[:, 0:C], g1[:, 0:C], MULT)
-            nc.gpsimd.tensor_tensor(m_rest[:, d, :], r[:, C:T], g1[:, C:T], MULT)
+        slope = []
+        for e in range(E):
+            r = sb.tile([P, PACK, C], F32, name="slope_%d" % e, tag="slope_%d" % e, align_bytes=64)
+            nc.scalar.activation(r[:], a_sb[:, :, e * C : (e + 1) * C], RELU, scale=2.0)
+            slope.append(r)
 
-        def round_interleave(dst, src):
-            nc.scalar.activation(
-                dst[:].rearrange("p (c i) d -> p c d i", i=4), src[:].rearrange("p d (c i) -> p c d i", i=4), COPY
-            )
+        def gather(e, dst, planes):
+            for x, c in enumerate(planes):
+                nc.vector.tensor_tensor(dst[:, x, :], dc[c][:].indirect(entries(list1, e * C, (e + 1) * C)), slope[e][:, c, :], MULT)
+            return [dst[:, x, :] for x in range(len(planes))]
 
-        def gather_da(e, factor, tag):
-            da = sb.tile([P, PACK, C], F32, name="da_%d" % e, tag=tag, align_bytes=64)
-            for d in range(PACK):
-                nc.vector.tensor_tensor(da[:, d, :], dc[d][:].indirect(entries(list1, e * C, (e + 1) * C)), factor(d), MULT)
-            h = sb.tile([P, C, PACK], BF16, name="h_%d" % e, tag="h_%d" % e, align_bytes=64)
-            round_interleave(h, da)
-            return h
+        def regroup(e, da, h, slot_banks, word_banks):
+            pairs = []
+            for b in range(C // P):
+                by_slot = bank(slot_banks[b])
+                for c in range(PACK):
+                    nc.tensor.transpose(by_slot[:, c * P : (c + 1) * P], da[c][:, b * P : (b + 1) * P], ident[:])
+                blk = e * C // P + b
+                rounded = sb.tile([P, W], BF16, name="rounded_%d" % blk, align_bytes=64)
+                nc.scalar.activation(
+                    rounded[:].rearrange("j (u p x) -> j u p x", u=2, x=2),
+                    by_slot[:].rearrange("j (p u x) -> j u p x", u=2, x=2),
+                    COPY,
+                    scale=g1[:, blk : blk + 1],
+                )
+                pairs.append(rounded[:].bitcast(F32))
+            for b in range(C // P):
+                back = bank(word_banks[b])
+                for u in range(2):
+                    nc.tensor.transpose(back[:, u * P : (u + 1) * P], pairs[b][:, u * P : (u + 1) * P], ident[:])
+                nc.scalar.copy(
+                    h.bitcast(F32)[:, 2 * b * P : 2 * (b + 1) * P].rearrange("p (j u) -> p j u", u=2),
+                    back[:, 0 : 2 * P].rearrange("p (u j) -> p j u", u=2),
+                )
 
-        def quantise(e, h):
-            codes = sb.tile([P, C], U32, name="codes_%d" % e, align_bytes=64)
-            plane = sb.tile([P, C], U8, name="plane_%d" % e, align_bytes=64)
-            nc.vector.quantize_mx(out=codes[:].bitcast(FP8X4), scales=plane[:], in_=h[:].rearrange("p j d -> p (j d)"))
+        def quantise(name, h, slots):
+            codes = sb.tile([P, slots], U32, name="codes_" + name, align_bytes=64)
+            plane = sb.tile([P, slots], U8, name="plane_" + name, align_bytes=64)
+            nc.vector.quantize_mx(out=codes[:].bitcast(FP8X4), scales=plane[:], in_=h)
             return codes, plane
 
-        def first_layer(kb, experts, quantised, bank_no):
-            acc = bank(bank_no)
-            for x, e in enumerate(experts):
-                codes, plane = quantised[e]
+        def first_layer(kb, lo, hi, quantised):
+            codes, plane = quantised
+            acc = bank(PACK + kb)
+            for e in range(lo // C, hi // C):
+                cols = slice(e * C - lo, (e + 1) * C - lo)
                 nc.tensor.matmul_mx(
-                    out=acc[:, x * C : (x + 1) * C],
+                    out=acc[:, cols],
                     lhsT=w1[:, e, 2 * kb * P : 2 * (kb + 1) * P].bitcast(FP4X4),
                     lhsT_scale=w1_plane[:, e, kb * P : (kb + 1) * P],
-                    rhs=codes[:].bitcast(FP8X4),
-                    rhs_scale=plane[:],
+                    rhs=codes[:, cols].bitcast(FP8X4),
+                    rhs_scale=plane[:, cols],
                     start=True,
                     stop=True,
                 )
-            res = sb.tile([P, len(experts) * C], F32, name="res_%d_%d" % (experts[0], kb))
-            nc.scalar.activation(res[:], acc[:, 0 : len(experts) * C], COPY)
+            res = sb.tile([P, hi - lo], F32, name="res_%d_%d" % (lo, kb))
+            nc.scalar.activation(res[:], acc[:, 0 : hi - lo], COPY)
             return res
 
-        h0 = gather_da(0, lambda d: m_first[:, d, :], "da_0")
-        h1 = gather_da(1, lambda d: m_rest[:, d, 0:C], "m_first")
-        quantised = [quantise(0, h0)]
-        res0 = [first_layer(kb, (0,), quantised, 4 + kb) for kb in range(W // P)]
-        h2 = gather_da(2, lambda d: m_rest[:, d, C:REST], "h_0")
-        quantised.append(quantise(1, h1))
+        da0 = sb.tile([P, PACK, C], F32, name="da_0", align_bytes=64)
+        planes0 = gather(0, da0, (0, 1, 2, 3))
+        h_first = sb.tile([P, PACK * C], BF16, name="h_first", tag="h_first", align_bytes=64)
+        regroup(0, planes0, h_first[:], (0, 1), (2, 3))
+        da1 = sb.tile([P, PACK, C], F32, name="da_1", tag="slope_0", align_bytes=64)
+        planes1 = gather(1, da1, (0, 1, 2, 3))
+        da2a = sb.tile([P, 1, C], F32, name="da_2a", tag="slope_1", align_bytes=64)
+        planes2 = gather(2, da2a, (0,))
+        first = quantise("first", h_first[:], C)
+        h_rest = placed("h_rest", [P, PACK * (T - C)], BF16, 34368)
+        regroup(1, planes1, h_rest[:, 0 : PACK * C], (2, 3), (0, 1))
+        res0 = [first_layer(kb, 0, C, first) for kb in range(W // P)]
+        da2b = sb.tile([P, PACK - 1, C], F32, name="da_2b", tag="h_first", align_bytes=64)
+        planes2 = planes2 + gather(2, da2b, (1, 2, 3))
+        regroup(2, planes2, h_rest[:, PACK * C : 2 * PACK * C], (0, 1), (2, 3))
 
-        dx = [sb.tile([P, T], F32, name="dx_%d" % kb) for kb in range(W // P - 1)]
-        for kb in range(W // P - 1):
+        dx = [sb.tile([P, T], F32, name="dx_%d" % kb) for kb in range(2)]
+        for kb in range(2):
             nc.vector.tensor_copy(dx[kb][:].indirect(entries(list1, 0, C)), res0[kb][:])
-        quantised.append(quantise(2, h2))
-        dx.append(sb.tile([P, T], F32, name="dx_last", tag="h_2", align_bytes=64))
-        nc.vector.tensor_copy(dx[-1][:].indirect(entries(list1, 0, C)), res0[-1][:])
+        rest = quantise("rest", h_rest[:], T - C)
+        dx.append(placed("dx_2", [P, T], F32, 33344))
+        dx.append(placed("dx_3", [P, T], F32, 36416))
+        for kb in range(2, W // P):
+            nc.vector.tensor_copy(dx[kb][:].indirect(entries(list1, 0, C)), res0[kb][:])
         for kb in range(W // P):
-            res = first_layer(kb, (1, 2), quantised, kb)
+            res = first_layer(kb, C, T, rest)
             nc.vector.tensor_copy(dx[kb][:].indirect(entries(list1, C, T)), res[:])
             nc.sync.dma_start(out[kb * P : (kb + 1) * P, :], dx[kb][:])

@@ -1,6 +1,7 @@
 from contextlib import ExitStack
 
 import concourse.mybir as mybir
+from concourse.masks import make_identity
 
 F32 = mybir.dt.float32
 BF16 = mybir.dt.bfloat16
@@ -42,91 +43,95 @@ def tile_moe_seb_relu2_kernel(
         def entries(lst, lo, hi):
             return lst[:, lo // 16 : hi // 16]
 
-        def scale_rows(engine, plane, rows, q):
+        def scale_rows(engine, plane, rows, q, e0, e1):
             engine.dma_start(
                 plane[:].bitcast(I32)[32 * q : 32 * q + 4, :, :],
-                rows[:, 0, 4 * q : 4 * q + 4, :].rearrange("e r i -> r e i").bitcast(I32),
+                rows[e0:e1, 0, 4 * q : 4 * q + 4, :].rearrange("e r i -> r e i").bitcast(I32),
             )
 
-        dy_plane = placed("dy_plane", [P, WIDE], U8, 960)
-        w2_plane = placed("w2_plane", [P, E, W], U8, 22528)
+        dy_plane = placed("dy_plane", [P, T], U8, 3072)
+        w2_plane = placed("w2_plane", [P, 1, W], U8, 22528)
         ident = sb.tile([P, P], F32, name="ident")
 
-        def identity_half(x, offset, span):
-            zeros = placed("zeros_%d" % x, [P, span // 4], F32, offset)[:, 0 : P // 2]
-            nc.gpsimd.memset(zeros, 0.0)
-            nc.gpsimd.affine_select(
-                out=ident[:, x * P // 2 : (x + 1) * P // 2],
-                in_=zeros,
-                compare_op=mybir.AluOpType.not_equal,
-                fill=1.0,
-                base=-x * P // 2,
-                pattern=[[-1, P // 2]],
-                channel_multiplier=1,
-            )
-
         nc.gpsimd.memset(dy_plane[:].bitcast(I32), 0)
-        identity_half(0, 22400, 26176 - 22400)
         nc.gpsimd.memset(w2_plane[:].bitcast(I32), 0)
-        identity_half(1, 26112, 29312 - 26112)
+        make_identity(nc, ident[:])
 
         list2 = sb.tile([P, T // 16], U16, name="list2")
         nc.sync.dma_start(list2[:], offs2)
-        list1 = sb.tile([P, T // 16], U16, name="list1")
-        nc.sync.dma_start(list1[:], offs)
+        for q in range(4):
+            (nc.scalar if q < 2 else nc.sync).dma_start(dy_plane[:].bitcast(I32)[32 * q : 32 * q + 4, :], dy_scales[0, 4 * q : 4 * q + 4, :].bitcast(I32))
         dy_tile = placed("dy_tile", [P, T], I32, 19392)
         nc.sync.dma_start(dy_tile[:], dy_words[0].rearrange("p t d -> p (t d)").bitcast(I32))
-        w2_first = placed("w2_first", [P, W], I32, 24064)
+        w2_first = placed("w2_first", [P, W], I32, 24064 + 64)
         nc.sync.dma_start(w2_first[:], w2t_words[0, 0].rearrange("p i d -> p (i d)").bitcast(I32))
         for q in range(4):
-            (nc.scalar if q < 2 else nc.sync).dma_start(dy_plane[:, 0:T].bitcast(I32)[32 * q : 32 * q + 4, :], dy_scales[0, 4 * q : 4 * q + 4, :].bitcast(I32))
-        for q in range(4):
-            scale_rows(nc.sync if q % 2 == 0 else nc.scalar, w2_plane, w2t_scales, q)
-        g2 = placed("g2", [P, T], F32, 26176)
-        nc.sync.dma_start(g2[:, 0:C], gate2[:, 0:C])
-        w2_rest = placed("w2_rest", [P, E - 1, W], I32, 29248)
-        nc.sync.dma_start(w2_rest[:], w2t_words[1:E, 0].rearrange("e p i d -> p e (i d)").bitcast(I32))
-        nc.sync.dma_start(g2[:, C:T], gate2[:, C:T])
-        w2 = [w2_first[:], w2_rest[:, 0, :], w2_rest[:, 1, :]]
+            scale_rows(nc.sync if q == 2 else nc.scalar, w2_plane, w2t_scales, q, 0, 1)
+        g2 = placed("g2", [P, C], F32, 23040)
+        nc.sync.dma_start(g2[:], gate2[:, 0:C])
+        list1 = sb.tile([P, T // 16], U16, name="list1")
+        nc.sync.dma_start(list1[:], offs)
 
-        gs = sb.tile([P, T], U8, name="gs", tag="gs", align_bytes=64)
-        nc.vector.tensor_copy(gs[:], dy_plane[:].indirect(list2[:]))
         groups = ((0, C), (C, T))
+        gs_head = sb.tile([P, 2 * C], U8, name="gs_head", tag="gs_head", align_bytes=64)
+        nc.vector.tensor_copy(gs_head[:], dy_plane[:].indirect(entries(list2, 0, 2 * C)))
         gw = []
         for lo, hi in groups:
             words = placed("gw_%d" % lo, [P, hi - lo], U32, 4 * lo)
             nc.vector.tensor_copy(words[:], dy_tile[:].bitcast(U32).indirect(entries(list2, lo, hi)))
             gw.append(words)
+        gs_tail = placed("gs_tail", [P, C], U8, 19392)
+        nc.vector.tensor_copy(gs_tail[:], dy_plane[:].indirect(entries(list2, 2 * C, T)))
+        gs = [gs_head[:, 0:C], gs_head[:, C : 2 * C], gs_tail[:]]
+        w2 = [w2_first[:]]
+        w2_scale = [w2_plane[:, 0, :]]
+        gate = [g2]
 
+        held = {(0, 1): 40960, (0, 2): 53248}
         dc = [sb.tile([P, WIDE], F32, name="dc_%d" % c) for c in range(PACK)]
         for n, (lo, hi) in enumerate(groups):
+            if n == 1:
+                w2_rest = placed("w2_rest", [P, E - 1, W], I32, 26112)
+                nc.sync.dma_start(w2_rest[:], w2t_words[1:E, 0].rearrange("e p i d -> p e (i d)").bitcast(I32))
+                rest_plane = placed("rest_plane", [P, E - 1, W], U8, 22528 - 512)
+                nc.gpsimd.memset(rest_plane[:].bitcast(I32), 0)
+                for q in range(4):
+                    scale_rows(nc.sync, rest_plane, w2t_scales, q, 1, E)
+                g2_rest = placed("g2_rest", [P, T - C], F32, 24064)
+                nc.sync.dma_start(g2_rest[:], gate2[:, C:T])
+                w2.extend([w2_rest[:, 0, :], w2_rest[:, 1, :]])
+                w2_scale.extend([rest_plane[:, 0, :], rest_plane[:, 1, :]])
+                gate.append(g2_rest)
             for c in range(PACK):
                 acc = bank(PACK * n + c)
                 for e in range(lo // C, hi // C):
                     nc.tensor.matmul_mx(
                         out=acc[:, e * C - lo : (e + 1) * C - lo],
                         lhsT=w2[e][:, c * P : (c + 1) * P].bitcast(FP8X4),
-                        lhsT_scale=w2_plane[:, e, c * P : (c + 1) * P],
+                        lhsT_scale=w2_scale[e][:, c * P : (c + 1) * P],
                         rhs=gw[n][:, e * C - lo : (e + 1) * C - lo].bitcast(FP8X4),
-                        rhs_scale=gs[:, e * C : (e + 1) * C],
+                        rhs_scale=gs[e],
                         start=True,
                         stop=True,
                     )
-                src = sb.tile([P, hi - lo], F32, name="src_%d_%d" % (n, c), tag="src_%d_%d" % (n, c), align_bytes=64)
+                if (n, c) in held:
+                    src = placed("src_%d_%d" % (n, c), [P, hi - lo], F32, held[(n, c)])
+                else:
+                    src = sb.tile([P, hi - lo], F32, name="src_%d_%d" % (n, c), tag="src_%d_%d" % (n, c), align_bytes=64)
                 nc.scalar.activation(src[:], acc[:, 0 : hi - lo], COPY)
-                nc.vector.tensor_tensor(dc[c][:].indirect(entries(list2, lo, hi)), src[:], g2[:, lo:hi], MULT)
+                nc.vector.tensor_tensor(dc[c][:].indirect(entries(list2, lo, hi)), src[:], gate[n][:], MULT)
 
-        a_sb = placed("a_sb", [P, PACK, T], F32, 7168)
+        a_sb = placed("a_sb", [P, PACK, T], F32, 40960)
         nc.sync.dma_start(a_sb[:], a.rearrange("(c p) j -> p c j", p=P))
-        w1 = placed("w1", [P, E, 2 * W], U8, 19456)
+        w1 = placed("w1", [P, E, 2 * W], U8, 53248)
         nc.sync.dma_start(w1[:].bitcast(I32), w1t_words[:, 0].rearrange("e p b -> p e b").bitcast(I32))
         g1 = sb.tile([P, T // P], F32, name="g1", tag="src_0_0", align_bytes=64)
         with nc.allow_non_contiguous_dma(reason="one gate value a partition"):
             nc.sync.dma_start(g1[:], gate1[0, :].rearrange("(b p) -> p b", p=P))
-        w1_plane = sb.tile([P, E, W], U8, name="w1_plane", tag="gs", align_bytes=64)
+        w1_plane = sb.tile([P, E, W], U8, name="w1_plane", tag="src_0_3", align_bytes=64)
         nc.gpsimd.memset(w1_plane[:].bitcast(I32), 0)
         for q in range(4):
-            scale_rows(nc.sync, w1_plane, w1t_scales, q)
+            scale_rows(nc.sync, w1_plane, w1t_scales, q, 0, E)
 
         slope = []
         for e in range(E):

@@ -31,118 +31,102 @@ def tile_moe_seb_relu2_kernel(
     nc = tc.nc
     with ExitStack() as ctx:
         sb = ctx.enter_context(tc.tile_pool(name="sb", bufs=1))
-        shared = ctx.enter_context(tc.tile_pool(name="shared", bufs=1))
         ps = ctx.enter_context(tc.psum_pool(name="ps", bufs=1))
 
         def bank(n):
             return ps.tile([P, W], F32, name="bank%d" % n, tag="bank%d" % n)
-
-        def placed(name, shape, dtype, offset):
-            return shared.tile(shape, dtype, name=name, offset=offset, align_bytes=64)
 
         def entries(lst, lo, hi):
             return lst[:, lo // 16 : hi // 16]
 
         def scale_rows(engine, plane, rows, q, e0, e1):
             engine.dma_start(
-                plane[:].bitcast(I32)[32 * q : 32 * q + 4, :, :],
+                plane[:].bitcast(I32)[32 * q : 32 * q + 4, e0:e1, :],
                 rows[e0:e1, 0, 4 * q : 4 * q + 4, :].rearrange("e r i -> r e i").bitcast(I32),
             )
 
-        dy_plane = placed("dy_plane", [P, T], U8, 3072)
-        w2_plane = placed("w2_plane", [P, 1, W], U8, 22528)
+        dy_plane = sb.tile([P, T], U8, name="dy_plane", align_bytes=64)
+        w2_plane = sb.tile([P, E, W], U8, name="w2_plane", align_bytes=64)
+        w1_plane = sb.tile([P, E, W], U8, name="w1_plane", align_bytes=64)
         ident = sb.tile([P, P], F32, name="ident")
-
         nc.gpsimd.memset(dy_plane[:].bitcast(I32), 0)
         nc.gpsimd.memset(w2_plane[:].bitcast(I32), 0)
+        nc.gpsimd.memset(w1_plane[:].bitcast(I32), 0)
         make_identity(nc, ident[:])
 
         list2 = sb.tile([P, T // 16], U16, name="list2")
         nc.sync.dma_start(list2[:], offs2)
         for q in range(4):
             (nc.scalar if q < 2 else nc.sync).dma_start(dy_plane[:].bitcast(I32)[32 * q : 32 * q + 4, :], dy_scales[0, 4 * q : 4 * q + 4, :].bitcast(I32))
-        dy_tile = placed("dy_tile", [P, T], I32, 19392)
+        dy_tile = sb.tile([P, T], I32, name="dy_tile", tag="dy_tile", align_bytes=64)
         nc.sync.dma_start(dy_tile[:], dy_words[0].rearrange("p t d -> p (t d)").bitcast(I32))
-        w2_first = placed("w2_first", [P, W], I32, 24064 + 64)
+        w2_first = sb.tile([P, W], I32, name="w2_first", align_bytes=64)
         nc.sync.dma_start(w2_first[:], w2t_words[0, 0].rearrange("p i d -> p (i d)").bitcast(I32))
         for q in range(4):
             scale_rows(nc.sync if q == 2 else nc.scalar, w2_plane, w2t_scales, q, 0, 1)
-        g2 = placed("g2", [P, C], F32, 23040)
-        nc.sync.dma_start(g2[:], gate2[:, 0:C])
+        g2_first = sb.tile([P, C], F32, name="g2_first")
+        nc.sync.dma_start(g2_first[:], gate2[:, 0:C])
+        for q in range(4):
+            scale_rows(nc.sync, w2_plane, w2t_scales, q, 1, E)
+        w2_rest = sb.tile([P, E - 1, W], I32, name="w2_rest", align_bytes=64)
+        nc.sync.dma_start(w2_rest[:], w2t_words[1:E, 0].rearrange("e p i d -> p e (i d)").bitcast(I32))
+        g2_rest = sb.tile([P, T - C], F32, name="g2_rest")
+        nc.sync.dma_start(g2_rest[:], gate2[:, C:T])
+        a_sb = sb.tile([P, PACK, T], F32, name="a_sb")
+        nc.sync.dma_start(a_sb[:], a.rearrange("(c p) j -> p c j", p=P))
         list1 = sb.tile([P, T // 16], U16, name="list1")
         nc.sync.dma_start(list1[:], offs)
+        g1 = sb.tile([P, T // P], F32, name="g1")
+        with nc.allow_non_contiguous_dma(reason="one gate value a partition"):
+            nc.sync.dma_start(g1[:], gate1[0, :].rearrange("(b p) -> p b", p=P))
+        for q in range(4):
+            scale_rows(nc.sync, w1_plane, w1t_scales, q, 0, E)
+        w1 = sb.tile([P, E, 2 * W], U8, name="w1", align_bytes=64)
+        nc.sync.dma_start(w1[:].bitcast(I32), w1t_words[:, 0].rearrange("e p b -> p e b").bitcast(I32))
+        w2 = [w2_first[:], w2_rest[:, 0, :], w2_rest[:, 1, :]]
+        gate = [g2_first, g2_rest]
 
         groups = ((0, C), (C, T))
-        gs_head = sb.tile([P, 2 * C], U8, name="gs_head", tag="gs_head", align_bytes=64)
+        gs_head = sb.tile([P, 2 * C], U8, name="gs_head", align_bytes=64)
         nc.vector.tensor_copy(gs_head[:], dy_plane[:].indirect(entries(list2, 0, 2 * C)))
         gw = []
         for lo, hi in groups:
-            words = placed("gw_%d" % lo, [P, hi - lo], U32, 4 * lo)
+            words = sb.tile([P, hi - lo], U32, name="gw_%d" % lo, align_bytes=64)
             nc.vector.tensor_copy(words[:], dy_tile[:].bitcast(U32).indirect(entries(list2, lo, hi)))
             gw.append(words)
-        gs_tail = placed("gs_tail", [P, C], U8, 19392)
+        gs_tail = sb.tile([P, C], U8, name="gs_tail", tag="dy_tile", align_bytes=64)
         nc.vector.tensor_copy(gs_tail[:], dy_plane[:].indirect(entries(list2, 2 * C, T)))
         gs = [gs_head[:, 0:C], gs_head[:, C : 2 * C], gs_tail[:]]
-        w2 = [w2_first[:]]
-        w2_scale = [w2_plane[:, 0, :]]
-        gate = [g2]
 
-        held = {(0, 1): 40960, (0, 2): 53248}
         dc = [sb.tile([P, WIDE], F32, name="dc_%d" % c) for c in range(PACK)]
         for n, (lo, hi) in enumerate(groups):
-            if n == 1:
-                w2_rest = placed("w2_rest", [P, E - 1, W], I32, 26112)
-                nc.sync.dma_start(w2_rest[:], w2t_words[1:E, 0].rearrange("e p i d -> p e (i d)").bitcast(I32))
-                rest_plane = placed("rest_plane", [P, E - 1, W], U8, 22528 - 512)
-                nc.gpsimd.memset(rest_plane[:].bitcast(I32), 0)
-                for q in range(4):
-                    scale_rows(nc.sync, rest_plane, w2t_scales, q, 1, E)
-                g2_rest = placed("g2_rest", [P, T - C], F32, 24064)
-                nc.sync.dma_start(g2_rest[:], gate2[:, C:T])
-                w2.extend([w2_rest[:, 0, :], w2_rest[:, 1, :]])
-                w2_scale.extend([rest_plane[:, 0, :], rest_plane[:, 1, :]])
-                gate.append(g2_rest)
             for c in range(PACK):
                 acc = bank(PACK * n + c)
                 for e in range(lo // C, hi // C):
                     nc.tensor.matmul_mx(
                         out=acc[:, e * C - lo : (e + 1) * C - lo],
                         lhsT=w2[e][:, c * P : (c + 1) * P].bitcast(FP8X4),
-                        lhsT_scale=w2_scale[e][:, c * P : (c + 1) * P],
+                        lhsT_scale=w2_plane[:, e, c * P : (c + 1) * P],
                         rhs=gw[n][:, e * C - lo : (e + 1) * C - lo].bitcast(FP8X4),
                         rhs_scale=gs[e],
                         start=True,
                         stop=True,
                     )
-                if (n, c) in held:
-                    src = placed("src_%d_%d" % (n, c), [P, hi - lo], F32, held[(n, c)])
-                else:
-                    src = sb.tile([P, hi - lo], F32, name="src_%d_%d" % (n, c), tag="src_%d_%d" % (n, c), align_bytes=64)
+                src = sb.tile([P, hi - lo], F32, name="src_%d_%d" % (n, c), tag="src_%d_%d" % (n, c), align_bytes=64)
                 nc.scalar.activation(src[:], acc[:, 0 : hi - lo], COPY)
                 nc.vector.tensor_tensor(dc[c][:].indirect(entries(list2, lo, hi)), src[:], gate[n][:], MULT)
 
-        a_sb = placed("a_sb", [P, PACK, T], F32, 40960)
-        nc.sync.dma_start(a_sb[:], a.rearrange("(c p) j -> p c j", p=P))
-        w1 = placed("w1", [P, E, 2 * W], U8, 53248)
-        nc.sync.dma_start(w1[:].bitcast(I32), w1t_words[:, 0].rearrange("e p b -> p e b").bitcast(I32))
-        g1 = sb.tile([P, T // P], F32, name="g1", tag="src_0_0", align_bytes=64)
-        with nc.allow_non_contiguous_dma(reason="one gate value a partition"):
-            nc.sync.dma_start(g1[:], gate1[0, :].rearrange("(b p) -> p b", p=P))
-        w1_plane = sb.tile([P, E, W], U8, name="w1_plane", tag="src_0_3", align_bytes=64)
-        nc.gpsimd.memset(w1_plane[:].bitcast(I32), 0)
-        for q in range(4):
-            scale_rows(nc.sync, w1_plane, w1t_scales, q, 0, E)
-
-        slope = []
+        slope = {}
         for e in range(E):
-            r = sb.tile([P, PACK, C], F32, name="slope_%d" % e, tag="slope_%d" % e, align_bytes=64)
-            nc.scalar.activation(r[:], a_sb[:, :, e * C : (e + 1) * C], RELU, scale=2.0)
-            slope.append(r)
+            for c in range(PACK):
+                r = sb.tile([P, C], F32, name="slope_%d_%d" % (e, c), tag="slope_%d" % (PACK * e + c), align_bytes=64)
+                nc.scalar.activation(r[:], a_sb[:, c, e * C : (e + 1) * C], RELU, scale=2.0)
+                slope[(e, c)] = r
 
-        def gather(e, dst, planes):
-            for x, c in enumerate(planes):
-                nc.vector.tensor_tensor(dst[:, x, :], dc[c][:].indirect(entries(list1, e * C, (e + 1) * C)), slope[e][:, c, :], MULT)
-            return [dst[:, x, :] for x in range(len(planes))]
+        def gather(e, c, tag):
+            da = sb.tile([P, C], F32, name="da_%d_%d" % (e, c), tag=tag, align_bytes=64)
+            nc.vector.tensor_tensor(da[:], dc[c][:].indirect(entries(list1, e * C, (e + 1) * C)), slope[(e, c)][:], MULT)
+            return da
 
         def regroup(e, da, h, slot_banks, word_banks):
             pairs = []
@@ -174,9 +158,9 @@ def tile_moe_seb_relu2_kernel(
             nc.vector.quantize_mx(out=codes[:].bitcast(FP8X4), scales=plane[:], in_=h)
             return codes, plane
 
-        def first_layer(kb, lo, hi, quantised):
+        def first_layer(kb, lo, hi, quantised, bank_no):
             codes, plane = quantised
-            acc = bank(PACK + kb)
+            acc = bank(bank_no)
             for e in range(lo // C, hi // C):
                 cols = slice(e * C - lo, (e + 1) * C - lo)
                 nc.tensor.matmul_mx(
@@ -192,31 +176,26 @@ def tile_moe_seb_relu2_kernel(
             nc.scalar.activation(res[:], acc[:, 0 : hi - lo], COPY)
             return res
 
-        da0 = sb.tile([P, PACK, C], F32, name="da_0", align_bytes=64)
-        planes0 = gather(0, da0, (0, 1, 2, 3))
-        h_first = sb.tile([P, PACK * C], BF16, name="h_first", tag="h_first", align_bytes=64)
+        planes0 = [gather(0, c, tag) for c, tag in enumerate(("src_1_2", "src_1_3", "slope_0", "slope_1"))]
+        h_first = sb.tile([P, PACK * C], BF16, name="h_first", align_bytes=64)
         regroup(0, planes0, h_first[:], (0, 1), (2, 3))
-        da1 = sb.tile([P, PACK, C], F32, name="da_1", tag="slope_0", align_bytes=64)
-        planes1 = gather(1, da1, (0, 1, 2, 3))
-        da2a = sb.tile([P, 1, C], F32, name="da_2a", tag="slope_1", align_bytes=64)
-        planes2 = gather(2, da2a, (0,))
+        planes1 = [gather(1, c, "slope_%d" % (PACK + c - 2)) for c in range(PACK)]
+        planes2 = [gather(2, 0, "slope_6")]
         first = quantise("first", h_first[:], C)
-        h_rest = placed("h_rest", [P, PACK * (T - C)], BF16, 34368)
+        h_rest = sb.tile([P, PACK * (T - C)], BF16, name="h_rest", align_bytes=64)
         regroup(1, planes1, h_rest[:, 0 : PACK * C], (2, 3), (0, 1))
-        res0 = [first_layer(kb, 0, C, first) for kb in range(W // P)]
-        da2b = sb.tile([P, PACK - 1, C], F32, name="da_2b", tag="h_first", align_bytes=64)
-        planes2 = planes2 + gather(2, da2b, (1, 2, 3))
+        res0 = [first_layer(kb, 0, C, first, PACK + kb) for kb in range(2)]
+        planes2 = planes2 + [gather(2, c, "slope_%d" % (c + 1)) for c in range(1, PACK)]
         regroup(2, planes2, h_rest[:, PACK * C : 2 * PACK * C], (0, 1), (2, 3))
 
-        dx = [sb.tile([P, T], F32, name="dx_%d" % kb) for kb in range(2)]
+        dx = [sb.tile([P, T], F32, name="dx_%d" % kb) for kb in range(W // P)]
         for kb in range(2):
             nc.vector.tensor_copy(dx[kb][:].indirect(entries(list1, 0, C)), res0[kb][:])
         rest = quantise("rest", h_rest[:], T - C)
-        dx.append(placed("dx_2", [P, T], F32, 33344))
-        dx.append(placed("dx_3", [P, T], F32, 36416))
-        for kb in range(2, W // P):
-            nc.vector.tensor_copy(dx[kb][:].indirect(entries(list1, 0, C)), res0[kb][:])
+        for kb, bank_no in ((2, 3), (3, 3)):
+            res = first_layer(kb, 0, C, first, bank_no)
+            nc.vector.tensor_copy(dx[kb][:].indirect(entries(list1, 0, C)), res[:])
         for kb in range(W // P):
-            res = first_layer(kb, C, T, rest)
+            res = first_layer(kb, C, T, rest, PACK + kb)
             nc.vector.tensor_copy(dx[kb][:].indirect(entries(list1, C, T)), res[:])
             nc.sync.dma_start(out[kb * P : (kb + 1) * P, :], dx[kb][:])

@@ -116,26 +116,30 @@ def tile_moe_seb_relu2_kernel(
                 nc.scalar.activation(src[:], acc[:, 0 : hi - lo], COPY)
                 nc.vector.tensor_tensor(dc[c][:].indirect(entries(list2, lo, hi)), src[:], gate[n][:], MULT)
 
+        runs = ((0, P), (P, 3 * P), (3 * P, T))
         slope = {}
-        for e in range(E):
+        for n, (lo, hi) in enumerate(runs):
             for c in range(PACK):
-                r = sb.tile([P, C], F32, name="slope_%d_%d" % (e, c), tag="slope_%d" % (PACK * e + c), align_bytes=64)
-                nc.scalar.activation(r[:], a_sb[:, c, e * C : (e + 1) * C], RELU, scale=2.0)
-                slope[(e, c)] = r
+                r = sb.tile([P, hi - lo], F32, name="slope_%d_%d" % (n, c), tag="slope_%d" % (PACK * n + c), align_bytes=64)
+                nc.scalar.activation(r[:], a_sb[:, c, lo:hi], RELU, scale=2.0)
+                slope[(n, c)] = r
 
-        def gather(e, c, tag):
-            da = sb.tile([P, C], F32, name="da_%d_%d" % (e, c), tag=tag, align_bytes=64)
-            nc.vector.tensor_tensor(da[:], dc[c][:].indirect(entries(list1, e * C, (e + 1) * C)), slope[(e, c)][:], MULT)
+        def gather(n, c, tag):
+            lo, hi = runs[n]
+            da = sb.tile([P, hi - lo], F32, name="da_%d_%d" % (n, c), tag=tag, align_bytes=64)
+            nc.vector.tensor_tensor(da[:], dc[c][:].indirect(entries(list1, lo, hi)), slope[(n, c)][:], MULT)
             return da
 
-        def regroup(e, da, h, slot_banks, word_banks):
+        def regroup(n, da, slot_banks, word_banks, tags):
+            lo, hi = runs[n]
+            h = sb.tile([P, PACK * (hi - lo)], BF16, name="h_%d" % n, tag="h_%d" % n, align_bytes=64)
             pairs = []
-            for b in range(C // P):
+            for b in range((hi - lo) // P):
                 by_slot = bank(slot_banks[b])
                 for c in range(PACK):
                     nc.tensor.transpose(by_slot[:, c * P : (c + 1) * P], da[c][:, b * P : (b + 1) * P], ident[:])
-                blk = e * C // P + b
-                rounded = sb.tile([P, W], BF16, name="rounded_%d" % blk, align_bytes=64)
+                blk = lo // P + b
+                rounded = sb.tile([P, W], BF16, name="rounded_%d" % blk, tag=tags[b], align_bytes=64)
                 nc.scalar.activation(
                     rounded[:].rearrange("j (u p x) -> j u p x", u=2, x=2),
                     by_slot[:].rearrange("j (p u x) -> j u p x", u=2, x=2),
@@ -143,59 +147,78 @@ def tile_moe_seb_relu2_kernel(
                     scale=g1[:, blk : blk + 1],
                 )
                 pairs.append(rounded[:].bitcast(F32))
-            for b in range(C // P):
+            for b in range((hi - lo) // P):
                 back = bank(word_banks[b])
                 for u in range(2):
                     nc.tensor.transpose(back[:, u * P : (u + 1) * P], pairs[b][:, u * P : (u + 1) * P], ident[:])
                 nc.scalar.copy(
-                    h.bitcast(F32)[:, 2 * b * P : 2 * (b + 1) * P].rearrange("p (j u) -> p j u", u=2),
+                    h[:].bitcast(F32)[:, 2 * b * P : 2 * (b + 1) * P].rearrange("p (j u) -> p j u", u=2),
                     back[:, 0 : 2 * P].rearrange("p (u j) -> p j u", u=2),
                 )
+            return h
 
-        def quantise(name, h, slots):
-            codes = sb.tile([P, slots], U32, name="codes_" + name, align_bytes=64)
-            plane = sb.tile([P, slots], U8, name="plane_" + name, align_bytes=64)
-            nc.vector.quantize_mx(out=codes[:].bitcast(FP8X4), scales=plane[:], in_=h)
-            return codes, plane
+        def by_expert(n):
+            lo, hi = runs[n]
+            cuts = sorted(set([lo, hi] + [e * C for e in range(E) if lo < e * C < hi]))
+            return list(zip(cuts[:-1], cuts[1:]))
 
-        def first_layer(kb, lo, hi, quantised, bank_no):
-            codes, plane = quantised
+        quantised = {}
+
+        def quantise(n, h, cuts):
+            lo = runs[n][0]
+            for x0, x1 in cuts:
+                codes = sb.tile([P, x1 - x0], U32, name="codes_%d" % x0, align_bytes=64)
+                plane = sb.tile([P, x1 - x0], U8, name="plane_%d" % x0, align_bytes=64)
+                nc.vector.quantize_mx(out=codes[:].bitcast(FP8X4), scales=plane[:], in_=h[:, PACK * (x0 - lo) : PACK * (x1 - lo)])
+                for y0, y1 in by_expert(n):
+                    if x0 <= y0 < x1:
+                        quantised[y0] = (codes[:, y0 - x0 : y1 - x0], plane[:, y0 - x0 : y1 - x0])
+
+        def first_layer(n, blocks, bank_no):
+            lo, hi = runs[n]
             acc = bank(bank_no)
-            for e in range(lo // C, hi // C):
-                cols = slice(e * C - lo, (e + 1) * C - lo)
-                nc.tensor.matmul_mx(
-                    out=acc[:, cols],
-                    lhsT=w1[:, e, 2 * kb * P : 2 * (kb + 1) * P].bitcast(FP4X4),
-                    lhsT_scale=w1_plane[:, e, kb * P : (kb + 1) * P],
-                    rhs=codes[:, cols].bitcast(FP8X4),
-                    rhs_scale=plane[:, cols],
-                    start=True,
-                    stop=True,
-                )
-            res = sb.tile([P, hi - lo], F32, name="res_%d_%d" % (lo, kb))
-            nc.scalar.activation(res[:], acc[:, 0 : hi - lo], COPY)
-            return res
-
-        planes0 = [gather(0, c, tag) for c, tag in enumerate(("src_1_2", "src_1_3", "slope_0", "slope_1"))]
-        h_first = sb.tile([P, PACK * C], BF16, name="h_first", align_bytes=64)
-        regroup(0, planes0, h_first[:], (0, 1), (2, 3))
-        planes1 = [gather(1, c, "slope_%d" % (PACK + c - 2)) for c in range(PACK)]
-        planes2 = [gather(2, 0, "slope_6")]
-        first = quantise("first", h_first[:], C)
-        h_rest = sb.tile([P, PACK * (T - C)], BF16, name="h_rest", align_bytes=64)
-        regroup(1, planes1, h_rest[:, 0 : PACK * C], (2, 3), (0, 1))
-        res0 = [first_layer(kb, 0, C, first, PACK + kb) for kb in range(2)]
-        planes2 = planes2 + [gather(2, c, "slope_%d" % (c + 1)) for c in range(1, PACK)]
-        regroup(2, planes2, h_rest[:, PACK * C : 2 * PACK * C], (0, 1), (2, 3))
+            for x, kb in enumerate(blocks):
+                for x0, x1 in by_expert(n):
+                    e = x0 // C
+                    nc.tensor.matmul_mx(
+                        out=acc[:, x * (hi - lo) + x0 - lo : x * (hi - lo) + x1 - lo],
+                        lhsT=w1[:, e, 2 * kb * P : 2 * (kb + 1) * P].bitcast(FP4X4),
+                        lhsT_scale=w1_plane[:, e, kb * P : (kb + 1) * P],
+                        rhs=quantised[x0][0].bitcast(FP8X4),
+                        rhs_scale=quantised[x0][1],
+                        start=True,
+                        stop=True,
+                    )
+            res = sb.tile([P, len(blocks) * (hi - lo)], F32, name="res_%d_%d" % (n, blocks[0]))
+            nc.scalar.activation(res[:], acc[:, 0 : len(blocks) * (hi - lo)], COPY)
+            return [res[:, x * (hi - lo) : (x + 1) * (hi - lo)] for x in range(len(blocks))]
 
         dx = [sb.tile([P, T], F32, name="dx_%d" % kb) for kb in range(W // P)]
+
+        def scatter(n, kb, res):
+            nc.vector.tensor_copy(dx[kb][:].indirect(entries(list1, *runs[n])), res)
+
+        da0 = [gather(0, c, tag) for c, tag in enumerate(("src_1_2", "src_1_3", "slope_0", "slope_1"))]
+        h0 = regroup(0, da0, (0,), (1,), ("rounded_0",))
+        da1 = [gather(1, c, "slope_%d" % (PACK + c - 2)) for c in range(PACK)]
+        da2 = [gather(2, 0, "slope_6")]
+        quantise(0, h0, [runs[0]])
+        h1 = regroup(1, da1, (0, 1), (3, 4), ("h_0", "rounded_2"))
+        res = first_layer(0, (0,), 5)
+        da2 = da2 + [gather(2, c, "slope_%d" % (c + 1)) for c in range(1, PACK)]
+        scatter(0, 0, res[0])
+        quantise(1, h1, [runs[1]])
+        res = first_layer(0, (1,), 3) + first_layer(0, (2, 3), 4)
+        for kb in range(1, PACK):
+            scatter(0, kb, res[kb - 1])
+        res = first_layer(1, (0,), 5) + first_layer(1, (1,), 2)
+        h2 = regroup(2, da2, (5, 3, 4), (7, 6, 0), ("rounded_3", "rounded_4", "rounded_5"))
         for kb in range(2):
-            nc.vector.tensor_copy(dx[kb][:].indirect(entries(list1, 0, C)), res0[kb][:])
-        rest = quantise("rest", h_rest[:], T - C)
-        for kb, bank_no in ((2, 3), (3, 3)):
-            res = first_layer(kb, 0, C, first, bank_no)
-            nc.vector.tensor_copy(dx[kb][:].indirect(entries(list1, 0, C)), res[:])
-        for kb in range(W // P):
-            res = first_layer(kb, C, T, rest, PACK + kb)
-            nc.vector.tensor_copy(dx[kb][:].indirect(entries(list1, C, T)), res[:])
+            scatter(1, kb, res[kb])
+        quantise(2, h2, by_expert(2)[::-1])
+        res = first_layer(1, (2, 3), 6)
+        for kb in range(2, PACK):
+            scatter(1, kb, res[kb - 2])
+        for kb, bank_no in enumerate((0, 7, 6, 0)):
+            scatter(2, kb, first_layer(2, (kb,), bank_no)[0])
             nc.sync.dma_start(out[kb * P : (kb + 1) * P, :], dx[kb][:])

@@ -58,12 +58,15 @@ def tile_moe_seb_relu2_kernel(
         nc.sync.dma_start(list2[:], offs2)
         for q in range(4):
             (nc.scalar if q < 2 else nc.sync).dma_start(dy_plane[:].bitcast(I32)[32 * q : 32 * q + 4, :], dy_scales[0, 4 * q : 4 * q + 4, :].bitcast(I32))
-        dy_tile = sb.tile([P, T], I32, name="dy_tile", tag="dy_tile", align_bytes=64)
+        dy_tile = sb.tile([P, T], I32, name="dy_tile", align_bytes=64)
         nc.sync.dma_start(dy_tile[:], dy_words[0].rearrange("p t d -> p (t d)").bitcast(I32))
-        w2_first = sb.tile([P, W], I32, name="w2_first", align_bytes=64)
-        nc.sync.dma_start(w2_first[:], w2t_words[0, 0].rearrange("p i d -> p (i d)").bitcast(I32))
+        first_words = w2t_words[0, 0].rearrange("p i d -> p (i d)").bitcast(I32)
+        w2_lead = sb.tile([P, P], I32, name="w2_lead", tag="w2_lead", align_bytes=64)
+        nc.sync.dma_start(w2_lead[:], first_words[:, 0:P])
         for q in range(4):
             scale_rows(nc.sync if q == 2 else nc.scalar, w2_plane, w2t_scales, q, 0, 1)
+        w2_first = sb.tile([P, W - P], I32, name="w2_first", align_bytes=64)
+        nc.sync.dma_start(w2_first[:], first_words[:, P:W])
         g2_first = sb.tile([P, C], F32, name="g2_first")
         nc.sync.dma_start(g2_first[:], gate2[:, 0:C])
         for q in range(4):
@@ -83,32 +86,34 @@ def tile_moe_seb_relu2_kernel(
             scale_rows(nc.sync, w1_plane, w1t_scales, q, 0, E)
         w1 = sb.tile([P, E, 2 * W], U8, name="w1", align_bytes=64)
         nc.sync.dma_start(w1[:].bitcast(I32), w1t_words[:, 0].rearrange("e p b -> p e b").bitcast(I32))
-        w2 = [w2_first[:], w2_rest[:, 0, :], w2_rest[:, 1, :]]
+        w2 = [[w2_lead[:]] + [w2_first[:, x : x + P] for x in range(0, W - P, P)]]
+        w2 = w2 + [[w2_rest[:, e, x : x + P] for x in range(0, W, P)] for e in range(E - 1)]
         gate = [g2_first, g2_rest]
 
         groups = ((0, C), (C, T))
-        gs_head = sb.tile([P, 2 * C], U8, name="gs_head", align_bytes=64)
-        nc.vector.tensor_copy(gs_head[:], dy_plane[:].indirect(entries(list2, 0, 2 * C)))
+        gs_head = sb.tile([P, T // 2], U8, name="gs_head", align_bytes=64)
+        nc.vector.tensor_copy(gs_head[:], dy_plane[:].indirect(entries(list2, 0, T // 2)))
         gw = []
         for lo, hi in groups:
             words = sb.tile([P, hi - lo], U32, name="gw_%d" % lo, align_bytes=64)
             nc.vector.tensor_copy(words[:], dy_tile[:].bitcast(U32).indirect(entries(list2, lo, hi)))
             gw.append(words)
-        gs_tail = sb.tile([P, C], U8, name="gs_tail", tag="dy_tile", align_bytes=64)
-        nc.vector.tensor_copy(gs_tail[:], dy_plane[:].indirect(entries(list2, 2 * C, T)))
-        gs = [gs_head[:, 0:C], gs_head[:, C : 2 * C], gs_tail[:]]
+        gs_tail = sb.tile([P, T // 2], U8, name="gs_tail", tag="w2_lead", align_bytes=64)
+        nc.vector.tensor_copy(gs_tail[:], dy_plane[:].indirect(entries(list2, T // 2, T)))
+        pieces = (((0, C),), ((C, T // 2), (T // 2, 2 * C), (2 * C, T)))
 
         dc = [sb.tile([P, WIDE], F32, name="dc_%d" % c) for c in range(PACK)]
         for n, (lo, hi) in enumerate(groups):
             for c in range(PACK):
                 acc = bank(PACK * n + c)
-                for e in range(lo // C, hi // C):
+                for x0, x1 in pieces[n]:
+                    e = x0 // C
                     nc.tensor.matmul_mx(
-                        out=acc[:, e * C - lo : (e + 1) * C - lo],
-                        lhsT=w2[e][:, c * P : (c + 1) * P].bitcast(FP8X4),
+                        out=acc[:, x0 - lo : x1 - lo],
+                        lhsT=w2[e][c].bitcast(FP8X4),
                         lhsT_scale=w2_plane[:, e, c * P : (c + 1) * P],
-                        rhs=gw[n][:, e * C - lo : (e + 1) * C - lo].bitcast(FP8X4),
-                        rhs_scale=gs[e],
+                        rhs=gw[n][:, x0 - lo : x1 - lo].bitcast(FP8X4),
+                        rhs_scale=gs_head[:, x0:x1] if x0 < T // 2 else gs_tail[:, x0 - T // 2 : x1 - T // 2],
                         start=True,
                         stop=True,
                     )
@@ -135,17 +140,18 @@ def tile_moe_seb_relu2_kernel(
             h = sb.tile([P, PACK * (hi - lo)], BF16, name="h_%d" % n, tag="h_%d" % n, align_bytes=64)
             pairs = []
             for b in range((hi - lo) // P):
-                by_slot = bank(slot_banks[b])
-                for c in range(PACK):
-                    nc.tensor.transpose(by_slot[:, c * P : (c + 1) * P], da[c][:, b * P : (b + 1) * P], ident[:])
                 blk = lo // P + b
                 rounded = sb.tile([P, W], BF16, name="rounded_%d" % blk, tag=tags[b], align_bytes=64)
-                nc.scalar.activation(
-                    rounded[:].rearrange("j (u p x) -> j u p x", u=2, x=2),
-                    by_slot[:].rearrange("j (p u x) -> j u p x", u=2, x=2),
-                    COPY,
-                    scale=g1[:, blk : blk + 1],
-                )
+                for c0, c1, bank_no in slot_banks[b]:
+                    by_slot = bank(bank_no)
+                    for c in range(c0, c1):
+                        nc.tensor.transpose(by_slot[:, c * P : (c + 1) * P], da[c][:, b * P : (b + 1) * P], ident[:])
+                    nc.scalar.activation(
+                        rounded[:].rearrange("j (u p x) -> j u p x", u=2, x=2)[:, :, 32 * c0 : 32 * c1, :],
+                        by_slot[:, c0 * P : c1 * P].rearrange("j (p u x) -> j u p x", u=2, x=2),
+                        COPY,
+                        scale=g1[:, blk : blk + 1],
+                    )
                 pairs.append(rounded[:].bitcast(F32))
             for b in range((hi - lo) // P):
                 back = bank(word_banks[b])
@@ -199,11 +205,11 @@ def tile_moe_seb_relu2_kernel(
             nc.vector.tensor_copy(dx[kb][:].indirect(entries(list1, *runs[n])), res)
 
         da0 = [gather(0, c, tag) for c, tag in enumerate(("src_1_2", "src_1_3", "slope_0", "slope_1"))]
-        h0 = regroup(0, da0, (0,), (1,), ("rounded_0",))
+        h0 = regroup(0, da0, [[(0, 3, 0), (3, 4, 2)]], (1,), ("rounded_0",))
         da1 = [gather(1, c, "slope_%d" % (PACK + c - 2)) for c in range(PACK)]
         da2 = [gather(2, 0, "slope_6")]
         quantise(0, h0, [runs[0]])
-        h1 = regroup(1, da1, (0, 1), (3, 4), ("h_0", "rounded_2"))
+        h1 = regroup(1, da1, [[(0, PACK, n)] for n in (2, 1)], (3, 4), ("rounded_0", "rounded_2"))
         res = first_layer(0, (0,), 5)
         da2 = da2 + [gather(2, c, "slope_%d" % (c + 1)) for c in range(1, PACK)]
         scatter(0, 0, res[0])
@@ -212,7 +218,7 @@ def tile_moe_seb_relu2_kernel(
         for kb in range(1, PACK):
             scatter(0, kb, res[kb - 1])
         res = first_layer(1, (0,), 5) + first_layer(1, (1,), 2)
-        h2 = regroup(2, da2, (5, 3, 4), (7, 6, 0), ("rounded_3", "rounded_4", "rounded_5"))
+        h2 = regroup(2, da2, [[(0, PACK, n)] for n in (5, 3, 4)], (7, 6, 0), ("rounded_3", "rounded_4", "rounded_5"))
         for kb in range(2):
             scatter(1, kb, res[kb])
         quantise(2, h2, by_expert(2)[::-1])

@@ -21,8 +21,23 @@ T = 768
 E = 3
 C = 256
 W = 512
-WIDE = 1024
+ROW_TILES = W // P
+QUADRANTS = 4
+HALF = T // 2
+DC_COLUMNS = 1024
 FLOPS = 2 * 2 * W * W * T
+
+GROUPS = ((0, C), (C, T))
+RUNS = ((0, P), (P, 3 * P), (3 * P, T))
+
+
+def cut(lo, hi, marks):
+    edges = [lo] + [m for m in marks if lo < m < hi] + [hi]
+    return list(zip(edges[:-1], edges[1:]))
+
+
+def by_expert(run):
+    return cut(*RUNS[run], (C, 2 * C))
 
 
 def tile_moe_seb_relu2_kernel(
@@ -33,13 +48,13 @@ def tile_moe_seb_relu2_kernel(
         sb = ctx.enter_context(tc.tile_pool(name="sb", bufs=1))
         ps = ctx.enter_context(tc.psum_pool(name="ps", bufs=1))
 
-        def bank(n):
-            return ps.tile([P, W], F32, name="bank%d" % n, tag="bank%d" % n)
+        def bank(number):
+            return ps.tile([P, W], F32, name="bank%d" % number, tag="bank%d" % number)
 
         def entries(lst, lo, hi):
             return lst[:, lo // 16 : hi // 16]
 
-        def scale_rows(engine, plane, rows, q, e0, e1):
+        def load_scale_rows(engine, plane, rows, q, e0, e1):
             engine.dma_start(
                 plane[:].bitcast(I32)[32 * q : 32 * q + 4, e0:e1, :],
                 rows[e0:e1, 0, 4 * q : 4 * q + 4, :].rearrange("e r i -> r e i").bitcast(I32),
@@ -50,107 +65,107 @@ def tile_moe_seb_relu2_kernel(
         w1_plane = sb.tile([P, E, W], U8, name="w1_plane", align_bytes=64)
         ident = sb.tile([P, P], F32, name="ident")
         nc.gpsimd.memset(dy_plane[:].bitcast(I32), 0)
-        nc.gpsimd.memset(w2_plane[:].bitcast(I32), 0)
+        nc.gpsimd.memset(w2_plane[:].bitcast(I32)[:, 0:1, :], 0)
+        nc.gpsimd.memset(w2_plane[:].bitcast(I32)[:, 1:E, :], 0)
         nc.gpsimd.memset(w1_plane[:].bitcast(I32), 0)
         make_identity(nc, ident[:])
 
         list2 = sb.tile([P, T // 16], U16, name="list2")
         nc.sync.dma_start(list2[:], offs2)
-        for q in range(4):
-            (nc.scalar if q < 2 else nc.sync).dma_start(dy_plane[:].bitcast(I32)[32 * q : 32 * q + 4, :], dy_scales[0, 4 * q : 4 * q + 4, :].bitcast(I32))
+        for q in range(QUADRANTS):
+            queue = nc.scalar if q < QUADRANTS // 2 else nc.sync
+            queue.dma_start(dy_plane[:].bitcast(I32)[32 * q : 32 * q + 4, :], dy_scales[0, 4 * q : 4 * q + 4, :].bitcast(I32))
         dy_tile = sb.tile([P, T], I32, name="dy_tile", align_bytes=64)
         nc.sync.dma_start(dy_tile[:], dy_words[0].rearrange("p t d -> p (t d)").bitcast(I32))
         first_words = w2t_words[0, 0].rearrange("p i d -> p (i d)").bitcast(I32)
         w2_lead = sb.tile([P, P], I32, name="w2_lead", tag="w2_lead", align_bytes=64)
+        for q, queue in enumerate((nc.scalar, nc.scalar, nc.sync, nc.scalar)):
+            load_scale_rows(queue, w2_plane, w2t_scales, q, 0, 1)
         nc.sync.dma_start(w2_lead[:], first_words[:, 0:P])
-        for q in range(4):
-            scale_rows(nc.sync if q == 2 else nc.scalar, w2_plane, w2t_scales, q, 0, 1)
-        w2_first = sb.tile([P, W - P], I32, name="w2_first", align_bytes=64)
-        nc.sync.dma_start(w2_first[:], first_words[:, P:W])
         g2_first = sb.tile([P, C], F32, name="g2_first")
         nc.sync.dma_start(g2_first[:], gate2[:, 0:C])
-        for q in range(4):
-            scale_rows(nc.sync, w2_plane, w2t_scales, q, 1, E)
+        w2_first = sb.tile([P, W - P], I32, name="w2_first", align_bytes=64)
+        nc.sync.dma_start(w2_first[:], first_words[:, P:W])
+        for q in range(QUADRANTS):
+            load_scale_rows(nc.sync, w2_plane, w2t_scales, q, 1, E)
         w2_rest = sb.tile([P, E - 1, W], I32, name="w2_rest", align_bytes=64)
         nc.sync.dma_start(w2_rest[:], w2t_words[1:E, 0].rearrange("e p i d -> p e (i d)").bitcast(I32))
         g2_rest = sb.tile([P, T - C], F32, name="g2_rest")
         nc.sync.dma_start(g2_rest[:], gate2[:, C:T])
-        a_sb = sb.tile([P, PACK, T], F32, name="a_sb")
-        nc.sync.dma_start(a_sb[:], a.rearrange("(c p) j -> p c j", p=P))
+        a_rows = sb.tile([P, ROW_TILES, T], F32, name="a_rows")
+        nc.sync.dma_start(a_rows[:], a.rearrange("(c p) j -> p c j", p=P))
         list1 = sb.tile([P, T // 16], U16, name="list1")
         nc.sync.dma_start(list1[:], offs)
         g1 = sb.tile([P, T // P], F32, name="g1")
         with nc.allow_non_contiguous_dma(reason="one gate value a partition"):
             nc.sync.dma_start(g1[:], gate1[0, :].rearrange("(b p) -> p b", p=P))
-        for q in range(4):
-            scale_rows(nc.sync, w1_plane, w1t_scales, q, 0, E)
+        for q in range(QUADRANTS):
+            load_scale_rows(nc.sync, w1_plane, w1t_scales, q, 0, E)
         w1 = sb.tile([P, E, 2 * W], U8, name="w1", align_bytes=64)
         nc.sync.dma_start(w1[:].bitcast(I32), w1t_words[:, 0].rearrange("e p b -> p e b").bitcast(I32))
         w2 = [[w2_lead[:]] + [w2_first[:, x : x + P] for x in range(0, W - P, P)]]
         w2 = w2 + [[w2_rest[:, e, x : x + P] for x in range(0, W, P)] for e in range(E - 1)]
-        gate = [g2_first, g2_rest]
+        g2 = [g2_first, g2_rest]
 
-        groups = ((0, C), (C, T))
-        gs_head = sb.tile([P, T // 2], U8, name="gs_head", align_bytes=64)
-        nc.vector.tensor_copy(gs_head[:], dy_plane[:].indirect(entries(list2, 0, T // 2)))
-        gw = []
-        for lo, hi in groups:
-            words = sb.tile([P, hi - lo], U32, name="gw_%d" % lo, align_bytes=64)
-            nc.vector.tensor_copy(words[:], dy_tile[:].bitcast(U32).indirect(entries(list2, lo, hi)))
-            gw.append(words)
-        gs_tail = sb.tile([P, T // 2], U8, name="gs_tail", tag="w2_lead", align_bytes=64)
-        nc.vector.tensor_copy(gs_tail[:], dy_plane[:].indirect(entries(list2, T // 2, T)))
-        pieces = (((0, C),), ((C, T // 2), (T // 2, 2 * C), (2 * C, T)))
+        scales_head = sb.tile([P, HALF], U8, name="scales_head", align_bytes=64)
+        nc.vector.tensor_copy(scales_head[:], dy_plane[:].indirect(entries(list2, 0, HALF)))
+        words = []
+        for lo, hi in GROUPS:
+            picked = sb.tile([P, hi - lo], U32, name="words_%d" % lo, align_bytes=64)
+            nc.vector.tensor_copy(picked[:], dy_tile[:].bitcast(U32).indirect(entries(list2, lo, hi)))
+            words.append(picked)
+        scales_tail = sb.tile([P, HALF], U8, name="scales_tail", tag="w2_lead", align_bytes=64)
+        nc.vector.tensor_copy(scales_tail[:], dy_plane[:].indirect(entries(list2, HALF, T)))
 
-        dc = [sb.tile([P, WIDE], F32, name="dc_%d" % c) for c in range(PACK)]
-        for n, (lo, hi) in enumerate(groups):
-            for c in range(PACK):
-                acc = bank(PACK * n + c)
-                for x0, x1 in pieces[n]:
+        dc = [sb.tile([P, DC_COLUMNS], F32, name="dc_%d" % c) for c in range(ROW_TILES)]
+        for group, (lo, hi) in enumerate(GROUPS):
+            for c in range(ROW_TILES):
+                acc = bank(ROW_TILES * group + c)
+                for x0, x1 in cut(lo, hi, (HALF, 2 * C)):
                     e = x0 // C
                     nc.tensor.matmul_mx(
                         out=acc[:, x0 - lo : x1 - lo],
                         lhsT=w2[e][c].bitcast(FP8X4),
                         lhsT_scale=w2_plane[:, e, c * P : (c + 1) * P],
-                        rhs=gw[n][:, x0 - lo : x1 - lo].bitcast(FP8X4),
-                        rhs_scale=gs_head[:, x0:x1] if x0 < T // 2 else gs_tail[:, x0 - T // 2 : x1 - T // 2],
+                        rhs=words[group][:, x0 - lo : x1 - lo].bitcast(FP8X4),
+                        rhs_scale=scales_head[:, x0:x1] if x0 < HALF else scales_tail[:, x0 - HALF : x1 - HALF],
                         start=True,
                         stop=True,
                     )
-                src = sb.tile([P, hi - lo], F32, name="src_%d_%d" % (n, c), tag="src_%d_%d" % (n, c), align_bytes=64)
-                nc.scalar.activation(src[:], acc[:, 0 : hi - lo], COPY)
-                nc.vector.tensor_tensor(dc[c][:].indirect(entries(list2, lo, hi)), src[:], gate[n][:], MULT)
+                tag = "sums2_%d_%d" % (group, c)
+                sums2 = sb.tile([P, hi - lo], F32, name=tag, tag=tag, align_bytes=64)
+                nc.scalar.activation(sums2[:], acc[:, 0 : hi - lo], COPY)
+                nc.vector.tensor_tensor(dc[c][:].indirect(entries(list2, lo, hi)), sums2[:], g2[group][:], MULT)
 
-        runs = ((0, P), (P, 3 * P), (3 * P, T))
         slope = {}
-        for n, (lo, hi) in enumerate(runs):
-            for c in range(PACK):
-                r = sb.tile([P, hi - lo], F32, name="slope_%d_%d" % (n, c), tag="slope_%d" % (PACK * n + c), align_bytes=64)
-                nc.scalar.activation(r[:], a_sb[:, c, lo:hi], RELU, scale=2.0)
-                slope[(n, c)] = r
+        for run, (lo, hi) in enumerate(RUNS):
+            for c in range(ROW_TILES):
+                tag = "slope_%d_%d" % (run, c)
+                slope[(run, c)] = sb.tile([P, hi - lo], F32, name=tag, tag=tag, align_bytes=64)
+                nc.scalar.activation(slope[(run, c)][:], a_rows[:, c, lo:hi], RELU, scale=2.0)
 
-        def gather(n, c, tag):
-            lo, hi = runs[n]
-            da = sb.tile([P, hi - lo], F32, name="da_%d_%d" % (n, c), tag=tag, align_bytes=64)
-            nc.vector.tensor_tensor(da[:], dc[c][:].indirect(entries(list1, lo, hi)), slope[(n, c)][:], MULT)
+        def gather(run, c, tag):
+            lo, hi = RUNS[run]
+            da = sb.tile([P, hi - lo], F32, name="da_%d_%d" % (run, c), tag=tag, align_bytes=64)
+            nc.vector.tensor_tensor(da[:], dc[c][:].indirect(entries(list1, lo, hi)), slope[(run, c)][:], MULT)
             return da
 
-        def regroup(n, da, slot_banks, word_banks, tags):
-            lo, hi = runs[n]
-            h = sb.tile([P, PACK * (hi - lo)], BF16, name="h_%d" % n, tag="h_%d" % n, align_bytes=64)
+        def regroup(run, da, slot_banks, word_banks, tags):
+            lo, hi = RUNS[run]
+            h = sb.tile([P, PACK * (hi - lo)], BF16, name="h_%d" % run, tag="h_%d" % run, align_bytes=64)
             pairs = []
             for b in range((hi - lo) // P):
-                blk = lo // P + b
-                rounded = sb.tile([P, W], BF16, name="rounded_%d" % blk, tag=tags[b], align_bytes=64)
-                for c0, c1, bank_no in slot_banks[b]:
-                    by_slot = bank(bank_no)
+                block = lo // P + b
+                rounded = sb.tile([P, W], BF16, name="rounded_%d" % block, tag=tags[b], align_bytes=64)
+                for c0, c1, number in slot_banks[b]:
+                    by_slot = bank(number)
                     for c in range(c0, c1):
                         nc.tensor.transpose(by_slot[:, c * P : (c + 1) * P], da[c][:, b * P : (b + 1) * P], ident[:])
                     nc.scalar.activation(
-                        rounded[:].rearrange("j (u p x) -> j u p x", u=2, x=2)[:, :, 32 * c0 : 32 * c1, :],
+                        rounded[:].rearrange("j (u p x) -> j u p x", u=2, x=2)[:, :, c0 * P // PACK : c1 * P // PACK, :],
                         by_slot[:, c0 * P : c1 * P].rearrange("j (p u x) -> j u p x", u=2, x=2),
                         COPY,
-                        scale=g1[:, blk : blk + 1],
+                        scale=g1[:, block : block + 1],
                     )
                 pairs.append(rounded[:].bitcast(F32))
             for b in range((hi - lo) // P):
@@ -163,31 +178,27 @@ def tile_moe_seb_relu2_kernel(
                 )
             return h
 
-        def by_expert(n):
-            lo, hi = runs[n]
-            cuts = sorted(set([lo, hi] + [e * C for e in range(E) if lo < e * C < hi]))
-            return list(zip(cuts[:-1], cuts[1:]))
-
         quantised = {}
 
-        def quantise(n, h, cuts):
-            lo = runs[n][0]
-            for x0, x1 in cuts:
+        def quantise(run, h, calls):
+            lo = RUNS[run][0]
+            for x0, x1 in calls:
                 codes = sb.tile([P, x1 - x0], U32, name="codes_%d" % x0, align_bytes=64)
                 plane = sb.tile([P, x1 - x0], U8, name="plane_%d" % x0, align_bytes=64)
                 nc.vector.quantize_mx(out=codes[:].bitcast(FP8X4), scales=plane[:], in_=h[:, PACK * (x0 - lo) : PACK * (x1 - lo)])
-                for y0, y1 in by_expert(n):
+                for y0, y1 in by_expert(run):
                     if x0 <= y0 < x1:
                         quantised[y0] = (codes[:, y0 - x0 : y1 - x0], plane[:, y0 - x0 : y1 - x0])
 
-        def first_layer(n, blocks, bank_no):
-            lo, hi = runs[n]
-            acc = bank(bank_no)
-            for x, kb in enumerate(blocks):
-                for x0, x1 in by_expert(n):
+        def first_layer(run, row_tiles, number):
+            lo, hi = RUNS[run]
+            width = hi - lo
+            acc = bank(number)
+            for x, kb in enumerate(row_tiles):
+                for x0, x1 in by_expert(run):
                     e = x0 // C
                     nc.tensor.matmul_mx(
-                        out=acc[:, x * (hi - lo) + x0 - lo : x * (hi - lo) + x1 - lo],
+                        out=acc[:, x * width + x0 - lo : x * width + x1 - lo],
                         lhsT=w1[:, e, 2 * kb * P : 2 * (kb + 1) * P].bitcast(FP4X4),
                         lhsT_scale=w1_plane[:, e, kb * P : (kb + 1) * P],
                         rhs=quantised[x0][0].bitcast(FP8X4),
@@ -195,36 +206,40 @@ def tile_moe_seb_relu2_kernel(
                         start=True,
                         stop=True,
                     )
-            res = sb.tile([P, len(blocks) * (hi - lo)], F32, name="res_%d_%d" % (n, blocks[0]))
-            nc.scalar.activation(res[:], acc[:, 0 : len(blocks) * (hi - lo)], COPY)
-            return [res[:, x * (hi - lo) : (x + 1) * (hi - lo)] for x in range(len(blocks))]
+            sums1 = sb.tile([P, len(row_tiles) * width], F32, name="sums1_%d_%d" % (run, row_tiles[0]))
+            nc.scalar.activation(sums1[:], acc[:, 0 : len(row_tiles) * width], COPY)
+            return [sums1[:, x * width : (x + 1) * width] for x in range(len(row_tiles))]
 
-        dx = [sb.tile([P, T], F32, name="dx_%d" % kb) for kb in range(W // P)]
+        dx = [sb.tile([P, T], F32, name="dx_%d" % kb) for kb in range(ROW_TILES)]
 
-        def scatter(n, kb, res):
-            nc.vector.tensor_copy(dx[kb][:].indirect(entries(list1, *runs[n])), res)
+        def scatter(run, kb, values):
+            nc.vector.tensor_copy(dx[kb][:].indirect(entries(list1, *RUNS[run])), values)
 
-        da0 = [gather(0, c, tag) for c, tag in enumerate(("src_1_2", "src_1_3", "slope_0", "slope_1"))]
-        h0 = regroup(0, da0, [[(0, 3, 0), (3, 4, 2)]], (1,), ("rounded_0",))
-        da1 = [gather(1, c, "slope_%d" % (PACK + c - 2)) for c in range(PACK)]
-        da2 = [gather(2, 0, "slope_6")]
-        quantise(0, h0, [runs[0]])
-        h1 = regroup(1, da1, [[(0, PACK, n)] for n in (2, 1)], (3, 4), ("rounded_0", "rounded_2"))
-        res = first_layer(0, (0,), 5)
-        da2 = da2 + [gather(2, c, "slope_%d" % (c + 1)) for c in range(1, PACK)]
-        scatter(0, 0, res[0])
-        quantise(1, h1, [runs[1]])
-        res = first_layer(0, (1,), 3) + first_layer(0, (2, 3), 4)
-        for kb in range(1, PACK):
-            scatter(0, kb, res[kb - 1])
-        res = first_layer(1, (0,), 5) + first_layer(1, (1,), 2)
-        h2 = regroup(2, da2, [[(0, PACK, n)] for n in (5, 3, 4)], (7, 6, 0), ("rounded_3", "rounded_4", "rounded_5"))
+        def whole(numbers):
+            return [[(0, ROW_TILES, number)] for number in numbers]
+
+        da0 = [gather(0, c, tag) for c, tag in enumerate(("sums2_1_2", "sums2_1_3", "slope_0_0", "slope_0_1"))]
+        h0 = regroup(0, da0, [[(0, ROW_TILES - 1, 0), (ROW_TILES - 1, ROW_TILES, 2)]], (1,), ("rounded_0",))
+        da1_tags = ("slope_0_2", "slope_0_3", "slope_1_0", "slope_1_1")
+        da1 = [gather(1, c, tag) for c, tag in enumerate(da1_tags)]
+        da2 = [gather(2, 0, "slope_1_2")]
+        quantise(0, h0, [RUNS[0]])
+        h1 = regroup(1, da1, whole((2, 1)), (3, 4), ("rounded_0", "rounded_2"))
+        sums = first_layer(0, (0,), 5)
+        da2 = da2 + [gather(2, c, da1_tags[c - 1]) for c in range(1, ROW_TILES)]
+        scatter(0, 0, sums[0])
+        quantise(1, h1, [RUNS[1]])
+        sums = first_layer(0, (1,), 3) + first_layer(0, (2, 3), 4)
+        for kb in range(1, ROW_TILES):
+            scatter(0, kb, sums[kb - 1])
+        sums = first_layer(1, (0,), 5) + first_layer(1, (1,), 2)
+        h2 = regroup(2, da2, whole((5, 3, 4)), (7, 6, 0), ("rounded_3", "rounded_4", "rounded_5"))
         for kb in range(2):
-            scatter(1, kb, res[kb])
+            scatter(1, kb, sums[kb])
         quantise(2, h2, by_expert(2)[::-1])
-        res = first_layer(1, (2, 3), 6)
-        for kb in range(2, PACK):
-            scatter(1, kb, res[kb - 2])
-        for kb, bank_no in enumerate((0, 7, 6, 0)):
-            scatter(2, kb, first_layer(2, (kb,), bank_no)[0])
+        sums = first_layer(1, (2, 3), 6)
+        for kb in range(2, ROW_TILES):
+            scatter(1, kb, sums[kb - 2])
+        for kb, number in enumerate((0, 7, 6, 0)):
+            scatter(2, kb, first_layer(2, (kb,), number)[0])
             nc.sync.dma_start(out[kb * P : (kb + 1) * P, :], dx[kb][:])

@@ -24,20 +24,16 @@ W = 512
 ROW_TILES = W // P
 QUADRANTS = 4
 HALF = T // 2
-DC_COLUMNS = 1024
+WINDOW = 1024
 FLOPS = 2 * 2 * W * W * T
 
 GROUPS = ((0, C), (C, T))
-RUNS = ((0, P), (P, 3 * P), (3 * P, T))
+RUNS = ((0, P), (P, HALF), (HALF, T))
 
 
 def cut(lo, hi, marks):
     edges = [lo] + [m for m in marks if lo < m < hi] + [hi]
     return list(zip(edges[:-1], edges[1:]))
-
-
-def by_expert(run):
-    return cut(*RUNS[run], (C, 2 * C))
 
 
 def tile_moe_seb_relu2_kernel(
@@ -82,18 +78,21 @@ def tile_moe_seb_relu2_kernel(
         for q, queue in enumerate((nc.scalar, nc.scalar, nc.sync, nc.scalar)):
             load_scale_rows(queue, w2_plane, w2t_scales, q, 0, 1)
         nc.sync.dma_start(w2_lead[:], first_words[:, 0:P])
-        g2_first = sb.tile([P, C], F32, name="g2_first")
-        nc.sync.dma_start(g2_first[:], gate2[:, 0:C])
+        g2 = sb.tile([P, T], F32, name="g2")
+        nc.sync.dma_start(g2[:, 0:C], gate2[:, 0:C])
         w2_first = sb.tile([P, W - P], I32, name="w2_first", align_bytes=64)
         nc.sync.dma_start(w2_first[:], first_words[:, P:W])
         for q in range(QUADRANTS):
             load_scale_rows(nc.sync, w2_plane, w2t_scales, q, 1, E)
         w2_rest = sb.tile([P, E - 1, W], I32, name="w2_rest", align_bytes=64)
         nc.sync.dma_start(w2_rest[:], w2t_words[1:E, 0].rearrange("e p i d -> p e (i d)").bitcast(I32))
-        g2_rest = sb.tile([P, T - C], F32, name="g2_rest")
-        nc.sync.dma_start(g2_rest[:], gate2[:, C:T])
-        a_rows = sb.tile([P, ROW_TILES, T], F32, name="a_rows")
-        nc.sync.dma_start(a_rows[:], a.rearrange("(c p) j -> p c j", p=P))
+        nc.sync.dma_start(g2[:, C:T], gate2[:, C:T])
+        a_rest = sb.tile([P, ROW_TILES - 1, T], F32, name="a_rest")
+        nc.sync.dma_start(a_rest[:], a[P:W, :].rearrange("(c p) j -> p c j", p=P))
+        a_head = sb.tile([P, HALF], F32, name="a_head", tag="a_head", align_bytes=64)
+        nc.sync.dma_start(a_head[:], a[0:P, 0:HALF])
+        a_tail = sb.tile([P, HALF], F32, name="a_tail", tag="a_tail", align_bytes=64)
+        nc.sync.dma_start(a_tail[:], a[0:P, HALF:T])
         list1 = sb.tile([P, T // 16], U16, name="list1")
         nc.sync.dma_start(list1[:], offs)
         g1 = sb.tile([P, T // P], F32, name="g1")
@@ -105,7 +104,6 @@ def tile_moe_seb_relu2_kernel(
         nc.sync.dma_start(w1[:].bitcast(I32), w1t_words[:, 0].rearrange("e p b -> p e b").bitcast(I32))
         w2 = [[w2_lead[:]] + [w2_first[:, x : x + P] for x in range(0, W - P, P)]]
         w2 = w2 + [[w2_rest[:, e, x : x + P] for x in range(0, W, P)] for e in range(E - 1)]
-        g2 = [g2_first, g2_rest]
 
         scales_head = sb.tile([P, HALF], U8, name="scales_head", align_bytes=64)
         nc.vector.tensor_copy(scales_head[:], dy_plane[:].indirect(entries(list2, 0, HALF)))
@@ -117,85 +115,103 @@ def tile_moe_seb_relu2_kernel(
         scales_tail = sb.tile([P, HALF], U8, name="scales_tail", tag="w2_lead", align_bytes=64)
         nc.vector.tensor_copy(scales_tail[:], dy_plane[:].indirect(entries(list2, HALF, T)))
 
-        dc = [sb.tile([P, DC_COLUMNS], F32, name="dc_%d" % c) for c in range(ROW_TILES)]
-        for group, (lo, hi) in enumerate(GROUPS):
-            for c in range(ROW_TILES):
-                acc = bank(ROW_TILES * group + c)
-                for x0, x1 in cut(lo, hi, (HALF, 2 * C)):
+        def second_layer(c, lo, hi, numbers):
+            sums2 = sb.tile([P, hi - lo], F32, name="sums2_%d_%d" % (c, lo))
+            for (y0, y1), number in zip(cut(lo, hi, (lo + W,)), numbers):
+                acc = bank(number)
+                for x0, x1 in cut(y0, y1, (C, HALF, 2 * C)):
                     e = x0 // C
+                    group = min(e, 1)
+                    first = GROUPS[group][0]
                     nc.tensor.matmul_mx(
-                        out=acc[:, x0 - lo : x1 - lo],
+                        out=acc[:, x0 - y0 : x1 - y0],
                         lhsT=w2[e][c].bitcast(FP8X4),
                         lhsT_scale=w2_plane[:, e, c * P : (c + 1) * P],
-                        rhs=words[group][:, x0 - lo : x1 - lo].bitcast(FP8X4),
+                        rhs=words[group][:, x0 - first : x1 - first].bitcast(FP8X4),
                         rhs_scale=scales_head[:, x0:x1] if x0 < HALF else scales_tail[:, x0 - HALF : x1 - HALF],
                         start=True,
                         stop=True,
                     )
-                tag = "sums2_%d_%d" % (group, c)
-                sums2 = sb.tile([P, hi - lo], F32, name=tag, tag=tag, align_bytes=64)
-                nc.scalar.activation(sums2[:], acc[:, 0 : hi - lo], COPY)
-                nc.vector.tensor_tensor(dc[c][:].indirect(entries(list2, lo, hi)), sums2[:], g2[group][:], MULT)
+                nc.scalar.activation(sums2[:, y0 - lo : y1 - lo], acc[:, 0 : y1 - y0], COPY)
+            return sums2
 
-        slope = {}
-        for run, (lo, hi) in enumerate(RUNS):
-            for c in range(ROW_TILES):
-                tag = "slope_%d_%d" % (run, c)
-                slope[(run, c)] = sb.tile([P, hi - lo], F32, name=tag, tag=tag, align_bytes=64)
-                nc.scalar.activation(slope[(run, c)][:], a_rows[:, c, lo:hi], RELU, scale=2.0)
+        def scatter_dc(window, sums2, lo, hi):
+            nc.vector.tensor_tensor(window[:].indirect(entries(list2, lo, hi)), sums2[:], g2[:, lo:hi], MULT)
 
-        def gather(run, c, tag):
-            lo, hi = RUNS[run]
-            da = sb.tile([P, hi - lo], F32, name="da_%d_%d" % (run, c), tag=tag, align_bytes=64)
-            nc.vector.tensor_tensor(da[:], dc[c][:].indirect(entries(list1, lo, hi)), slope[(run, c)][:], MULT)
-            return da
+        dc = {c: sb.tile([P, WINDOW], F32, name="dc_%d" % c) for c in (0, 1, 3)}
+        for group, (lo, hi) in enumerate(GROUPS):
+            for c in range(2):
+                scatter_dc(dc[c], second_layer(c, lo, hi, (2 * group + c,)), lo, hi)
+        scatter_dc(dc[3], second_layer(3, 0, T, (4, 5)), 0, T)
+        last_sums2 = second_layer(2, 0, T, (6, 7))
 
-        def regroup(run, da, slot_banks, word_banks, tags):
-            lo, hi = RUNS[run]
-            h = sb.tile([P, PACK * (hi - lo)], BF16, name="h_%d" % run, tag="h_%d" % run, align_bytes=64)
-            pairs = []
-            for b in range((hi - lo) // P):
-                block = lo // P + b
-                rounded = sb.tile([P, W], BF16, name="rounded_%d" % block, tag=tags[b], align_bytes=64)
-                for c0, c1, number in slot_banks[b]:
-                    by_slot = bank(number)
-                    for c in range(c0, c1):
-                        nc.tensor.transpose(by_slot[:, c * P : (c + 1) * P], da[c][:, b * P : (b + 1) * P], ident[:])
-                    nc.scalar.activation(
-                        rounded[:].rearrange("j (u p x) -> j u p x", u=2, x=2)[:, :, c0 * P // PACK : c1 * P // PACK, :],
-                        by_slot[:, c0 * P : c1 * P].rearrange("j (p u x) -> j u p x", u=2, x=2),
-                        COPY,
-                        scale=g1[:, block : block + 1],
-                    )
-                pairs.append(rounded[:].bitcast(F32))
-            for b in range((hi - lo) // P):
-                back = bank(word_banks[b])
-                for u in range(2):
-                    nc.tensor.transpose(back[:, u * P : (u + 1) * P], pairs[b][:, u * P : (u + 1) * P], ident[:])
-                nc.scalar.copy(
-                    h[:].bitcast(F32)[:, 2 * b * P : 2 * (b + 1) * P].rearrange("p (j u) -> p j u", u=2),
-                    back[:, 0 : 2 * P].rearrange("p (u j) -> p j u", u=2),
-                )
-            return h
+        def make_slope(c, lo, hi, source, tag):
+            slope = sb.tile([P, hi - lo], F32, name="slope_%d_%d" % (c, lo), tag=tag, align_bytes=64)
+            nc.scalar.activation(slope[:], source, RELU, scale=2.0)
+            return slope
+
+        slopes = {}
+        for c, lo, hi in ((1, 0, P), (3, 0, P), (2, 0, P), (2, P, T), (1, P, HALF), (3, P, HALF), (3, HALF, T), (1, HALF, T)):
+            slopes[(c, lo)] = make_slope(c, lo, hi, a_rest[:, c - 1, lo:hi], "slope_%d_%d" % (c, lo))
+        slopes[(0, 0)] = make_slope(0, 0, HALF, a_head[:], "slope_0_0")
+
+        da = {}
+
+        def gather(c, lo, hi, tag):
+            piece = sb.tile([P, hi - lo], F32, name="da_%d_%d" % (c, lo), tag=tag, align_bytes=64)
+            nc.vector.tensor_tensor(piece[:], dc[c][:].indirect(entries(list1, lo, hi)), slopes[(c, lo)][:], MULT)
+            for x in range(lo, hi, P):
+                da[(c, x // P)] = piece[:, x - lo : x - lo + P]
+
+        rounded = {}
+
+        def turn(parts, number):
+            by_slot = bank(number)
+            for c, block in parts:
+                x = sorted(parts, key=lambda part: part[::-1]).index((c, block))
+                nc.tensor.transpose(by_slot[:, x * P : (x + 1) * P], da[(c, block)], ident[:])
+            return by_slot
+
+        def round_off(block, c0, c1, by_slot):
+            if block not in rounded:
+                tag = "rounded_%d" % block
+                rounded[block] = sb.tile([P, W], BF16, name=tag, tag=tag, align_bytes=64)
+            nc.scalar.activation(
+                rounded[block][:].rearrange("j (u p x) -> j u p x", u=2, x=2)[:, :, c0 * P // PACK : c1 * P // PACK, :],
+                by_slot.rearrange("j (p u x) -> j u p x", u=2, x=2),
+                COPY,
+                scale=g1[:, block : block + 1],
+            )
+
+        def turn_back(block, number, h, first_block):
+            back = bank(number)
+            pairs = rounded[block][:].bitcast(F32)
+            for u in range(2):
+                nc.tensor.transpose(back[:, u * P : (u + 1) * P], pairs[:, u * P : (u + 1) * P], ident[:])
+            b = block - first_block
+            nc.scalar.copy(
+                h[:].bitcast(F32)[:, 2 * b * P : 2 * (b + 1) * P].rearrange("p (j u) -> p j u", u=2),
+                back[:, 0 : 2 * P].rearrange("p (u j) -> p j u", u=2),
+            )
+
+        def new_h(lo, hi):
+            return sb.tile([P, PACK * (hi - lo)], BF16, name="h_%d" % lo, tag="h_%d" % lo, align_bytes=64)
 
         quantised = {}
 
-        def quantise(run, h, calls):
-            lo = RUNS[run][0]
-            for x0, x1 in calls:
-                codes = sb.tile([P, x1 - x0], U32, name="codes_%d" % x0, align_bytes=64)
-                plane = sb.tile([P, x1 - x0], U8, name="plane_%d" % x0, align_bytes=64)
-                nc.vector.quantize_mx(out=codes[:].bitcast(FP8X4), scales=plane[:], in_=h[:, PACK * (x0 - lo) : PACK * (x1 - lo)])
-                for y0, y1 in by_expert(run):
-                    if x0 <= y0 < x1:
-                        quantised[y0] = (codes[:, y0 - x0 : y1 - x0], plane[:, y0 - x0 : y1 - x0])
+        def quantise(h, lo, hi):
+            codes = sb.tile([P, hi - lo], U32, name="codes_%d" % lo, align_bytes=64)
+            plane = sb.tile([P, hi - lo], U8, name="plane_%d" % lo, align_bytes=64)
+            nc.vector.quantize_mx(out=codes[:].bitcast(FP8X4), scales=plane[:], in_=h[:])
+            for y0, y1 in cut(lo, hi, (C, 2 * C)):
+                quantised[y0] = (codes[:, y0 - lo : y1 - lo], plane[:, y0 - lo : y1 - lo])
 
         def first_layer(run, row_tiles, number):
             lo, hi = RUNS[run]
             width = hi - lo
             acc = bank(number)
             for x, kb in enumerate(row_tiles):
-                for x0, x1 in by_expert(run):
+                for x0, x1 in cut(lo, hi, (C, 2 * C)):
                     e = x0 // C
                     nc.tensor.matmul_mx(
                         out=acc[:, x * width + x0 - lo : x * width + x1 - lo],
@@ -206,40 +222,76 @@ def tile_moe_seb_relu2_kernel(
                         start=True,
                         stop=True,
                     )
-            sums1 = sb.tile([P, len(row_tiles) * width], F32, name="sums1_%d_%d" % (run, row_tiles[0]))
-            nc.scalar.activation(sums1[:], acc[:, 0 : len(row_tiles) * width], COPY)
-            return [sums1[:, x * width : (x + 1) * width] for x in range(len(row_tiles))]
+            return acc[:, 0 : len(row_tiles) * width]
 
-        dx = [sb.tile([P, T], F32, name="dx_%d" % kb) for kb in range(ROW_TILES)]
+        def copy_out(acc, width, tag):
+            sums1 = sb.tile([P, width], F32, name="sums1_" + tag, tag=tag, align_bytes=64)
+            nc.scalar.activation(sums1[:], acc, COPY)
+            return sums1
 
-        def scatter(run, kb, values):
-            nc.vector.tensor_copy(dx[kb][:].indirect(entries(list1, *RUNS[run])), values)
+        dx = [sb.tile([P, WINDOW], F32, name="dx_%d" % kb) for kb in range(ROW_TILES)]
 
-        def whole(numbers):
-            return [[(0, ROW_TILES, number)] for number in numbers]
+        def scatter(kb, lo, hi, values):
+            nc.vector.tensor_copy(dx[kb][:].indirect(entries(list1, lo, hi)), values)
 
-        da0 = [gather(0, c, tag) for c, tag in enumerate(("sums2_1_2", "sums2_1_3", "slope_0_0", "slope_0_1"))]
-        h0 = regroup(0, da0, [[(0, ROW_TILES - 1, 0), (ROW_TILES - 1, ROW_TILES, 2)]], (1,), ("rounded_0",))
-        da1_tags = ("slope_0_2", "slope_0_3", "slope_1_0", "slope_1_1")
-        da1 = [gather(1, c, tag) for c, tag in enumerate(da1_tags)]
-        da2 = [gather(2, 0, "slope_1_2")]
-        quantise(0, h0, [RUNS[0]])
-        h1 = regroup(1, da1, whole((2, 1)), (3, 4), ("rounded_0", "rounded_2"))
-        sums = first_layer(0, (0,), 5)
-        da2 = da2 + [gather(2, c, da1_tags[c - 1]) for c in range(1, ROW_TILES)]
-        scatter(0, 0, sums[0])
-        quantise(1, h1, [RUNS[1]])
-        sums = first_layer(0, (1,), 3) + first_layer(0, (2, 3), 4)
-        for kb in range(1, ROW_TILES):
-            scatter(0, kb, sums[kb - 1])
-        sums = first_layer(1, (0,), 5) + first_layer(1, (1,), 2)
-        h2 = regroup(2, da2, whole((5, 3, 4)), (7, 6, 0), ("rounded_3", "rounded_4", "rounded_5"))
+        def store(kb):
+            nc.sync.dma_start(out[kb * P : (kb + 1) * P, :], dx[kb][:, 0:T])
+
+        gather(0, 0, HALF, "da_0_0")
+        gather(1, 0, P, "a_head")
+        round_off(0, 0, 2, turn(((0, 0), (1, 0)), 0)[:, 0 : 2 * P])
+        by_slot = turn(((0, 1), (0, 2)), 3)
+        for block in (1, 2):
+            round_off(block, 0, 1, by_slot[:, (block - 1) * P : block * P])
+        dc[2] = sb.tile([P, WINDOW], F32, name="dc_2", tag="slope_0_0", align_bytes=64)
+        scatter_dc(dc[2], last_sums2, 0, T)
+        gather(3, 0, P, "slope_1_0")
+        gather(2, 0, P, "da_2_0")
+        gather(2, P, T, "da_2_1")
+        gather(1, P, HALF, "slope_2_0")
+        gather(3, P, HALF, "slope_2_128")
+        gather(3, HALF, T, "slope_1_128")
+        round_off(0, 2, 4, turn(((3, 0), (2, 0)), 0)[:, 0 : 2 * P])
+        h0 = new_h(0, P)
+        turn_back(0, 1, h0, 0)
+        slopes[(0, HALF)] = make_slope(0, HALF, T, a_tail[:], "rounded_0")
+        quantise(h0, 0, P)
+        gather(0, HALF, T, "da_0_1")
+        gather(1, HALF, T, "a_tail")
+        for block in (1, 2):
+            round_off(block, 1, 4, turn([(c, block) for c in (2, 1, 3)], block - 1)[:, 0 : 3 * P])
+        acc = [first_layer(0, (0, 1), 2), first_layer(0, (2, 3), 5)]
+        sums = copy_out(acc[0], 2 * P, "s0_01")
         for kb in range(2):
-            scatter(1, kb, sums[kb])
-        quantise(2, h2, by_expert(2)[::-1])
-        sums = first_layer(1, (2, 3), 6)
+            scatter(kb, 0, P, sums[:, kb * P : (kb + 1) * P])
+        h1 = new_h(P, HALF)
+        turn_back(1, 3, h1, 1)
+        turn_back(2, 4, h1, 1)
+        quantise(h1, P, HALF)
+        by_slot = [turn([(c, block) for c in (2, 3, 0, 1)], number)[:] for block, number in ((3, 1), (4, 3), (5, 4))]
+        sums = copy_out(acc[1], 2 * P, "rounded_2")
+        round_off(3, 0, 4, by_slot[0])
         for kb in range(2, ROW_TILES):
-            scatter(1, kb, sums[kb - 2])
-        for kb, number in enumerate((0, 7, 6, 0)):
-            scatter(2, kb, first_layer(2, (kb,), number)[0])
-            nc.sync.dma_start(out[kb * P : (kb + 1) * P, :], dx[kb][:])
+            scatter(kb, 0, P, sums[:, (kb - 2) * P : (kb - 1) * P])
+        round_off(4, 0, 4, by_slot[1])
+        acc = [first_layer(1, (0,), 0), first_layer(1, (1,), 2), first_layer(1, (2, 3), 6)]
+        sums = copy_out(acc[0], C, "s1_0")
+        scatter(0, P, HALF, sums[:])
+        round_off(5, 0, 4, by_slot[2])
+        h2 = new_h(HALF, 2 * C)
+        h3 = new_h(2 * C, T)
+        turn_back(3, 7, h2, 3)
+        turn_back(4, 5, h3, 4)
+        turn_back(5, 1, h3, 4)
+        quantise(h2, HALF, 2 * C)
+        quantise(h3, 2 * C, T)
+        scatter(1, P, HALF, copy_out(acc[1], C, "rounded_5")[:])
+        both = sb.tile([P, 2, T - P], F32, name="both")
+        nc.scalar.activation(both[:, :, 0:C], acc[2].rearrange("p (x j) -> p x j", x=2), COPY)
+        for kb, number in ((2, 3), (3, 4)):
+            nc.scalar.activation(both[:, kb - 2, C : T - P], first_layer(2, (kb,), number), COPY)
+            scatter(kb, P, T, both[:, kb - 2, :])
+            store(kb)
+        for kb, number in ((0, 7), (1, 5)):
+            scatter(kb, HALF, T, copy_out(first_layer(2, (kb,), number), HALF, "s2_%d" % kb)[:])
+            store(kb)

@@ -105,21 +105,21 @@ def tile_moe_seb_relu2_kernel(
         w2 = [[w2_lead[:]] + [w2_first[:, x : x + P] for x in range(0, W - P, P)]]
         w2 = w2 + [[w2_rest[:, e, x : x + P] for x in range(0, W, P)] for e in range(E - 1)]
 
-        scales_head = sb.tile([P, HALF], U8, name="scales_head", align_bytes=64)
-        nc.vector.tensor_copy(scales_head[:], dy_plane[:].indirect(entries(list2, 0, HALF)))
+        scales_head = sb.tile([P, 2 * C], U8, name="scales_head", align_bytes=64)
+        nc.vector.tensor_copy(scales_head[:], dy_plane[:].indirect(entries(list2, 0, 2 * C)))
         words = []
         for lo, hi in GROUPS:
             picked = sb.tile([P, hi - lo], U32, name="words_%d" % lo, align_bytes=64)
             nc.vector.tensor_copy(picked[:], dy_tile[:].bitcast(U32).indirect(entries(list2, lo, hi)))
             words.append(picked)
-        scales_tail = sb.tile([P, HALF], U8, name="scales_tail", tag="w2_lead", align_bytes=64)
-        nc.vector.tensor_copy(scales_tail[:], dy_plane[:].indirect(entries(list2, HALF, T)))
+        scales_tail = sb.tile([P, C], U8, name="scales_tail", tag="w2_lead", align_bytes=64)
+        nc.vector.tensor_copy(scales_tail[:], dy_plane[:].indirect(entries(list2, 2 * C, T)))
 
         def second_layer(c, lo, hi, numbers):
             sums2 = sb.tile([P, hi - lo], F32, name="sums2_%d_%d" % (c, lo))
             for (y0, y1), number in zip(cut(lo, hi, (lo + W,)), numbers):
                 acc = bank(number)
-                for x0, x1 in cut(y0, y1, (C, HALF, 2 * C)):
+                for x0, x1 in cut(y0, y1, (C, 2 * C)):
                     e = x0 // C
                     group = min(e, 1)
                     first = GROUPS[group][0]
@@ -128,7 +128,7 @@ def tile_moe_seb_relu2_kernel(
                         lhsT=w2[e][c].bitcast(FP8X4),
                         lhsT_scale=w2_plane[:, e, c * P : (c + 1) * P],
                         rhs=words[group][:, x0 - first : x1 - first].bitcast(FP8X4),
-                        rhs_scale=scales_head[:, x0:x1] if x0 < HALF else scales_tail[:, x0 - HALF : x1 - HALF],
+                        rhs_scale=scales_head[:, x0:x1] if x0 < 2 * C else scales_tail[:],
                         start=True,
                         stop=True,
                     )
@@ -286,12 +286,12 @@ def tile_moe_seb_relu2_kernel(
         quantise(h2, HALF, 2 * C)
         quantise(h3, 2 * C, T)
         scatter(1, P, HALF, copy_out(acc[1], C, "rounded_5")[:])
+        for kb, number in ((0, 7), (1, 5)):
+            scatter(kb, HALF, T, copy_out(first_layer(2, (kb,), number), HALF, "s2_%d" % kb)[:])
+            store(kb)
         both = sb.tile([P, 2, T - P], F32, name="both")
         nc.scalar.activation(both[:, :, 0:C], acc[2].rearrange("p (x j) -> p x j", x=2), COPY)
         for kb, number in ((2, 3), (3, 4)):
             nc.scalar.activation(both[:, kb - 2, C : T - P], first_layer(2, (kb,), number), COPY)
             scatter(kb, P, T, both[:, kb - 2, :])
-            store(kb)
-        for kb, number in ((0, 7), (1, 5)):
-            scatter(kb, HALF, T, copy_out(first_layer(2, (kb,), number), HALF, "s2_%d" % kb)[:])
             store(kb)

@@ -78,15 +78,17 @@ def tile_moe_seb_relu2_kernel(
         for q, queue in enumerate((nc.scalar, nc.scalar, nc.sync, nc.scalar)):
             load_scale_rows(queue, w2_plane, w2t_scales, q, 0, 1)
         nc.sync.dma_start(w2_lead[:], first_words[:, 0:P])
-        g2 = sb.tile([P, T], F32, name="g2")
-        nc.sync.dma_start(g2[:, 0:C], gate2[:, 0:C])
+        g2 = sb.tile([P, C], F32, name="g2")
+        nc.sync.dma_start(g2[:], gate2[:, 0:C])
         w2_first = sb.tile([P, W - P], I32, name="w2_first", align_bytes=64)
         nc.sync.dma_start(w2_first[:], first_words[:, P:W])
+        g2_columns = sb.tile([P, T // P], F32, name="g2_columns")
+        with nc.allow_non_contiguous_dma(reason="one gate value a partition"):
+            nc.sync.dma_start(g2_columns[:], gate2[0, :].rearrange("(b p) -> p b", p=P))
         for q in range(QUADRANTS):
             load_scale_rows(nc.sync, w2_plane, w2t_scales, q, 1, E)
         w2_rest = sb.tile([P, E - 1, W], I32, name="w2_rest", align_bytes=64)
         nc.sync.dma_start(w2_rest[:], w2t_words[1:E, 0].rearrange("e p i d -> p e (i d)").bitcast(I32))
-        nc.sync.dma_start(g2[:, C:T], gate2[:, C:T])
         a_rest = sb.tile([P, ROW_TILES - 1, T], F32, name="a_rest")
         nc.sync.dma_start(a_rest[:], a[P:W, :].rearrange("(c p) j -> p c j", p=P))
         a_head = sb.tile([P, HALF], F32, name="a_head", tag="a_head", align_bytes=64)
@@ -102,8 +104,6 @@ def tile_moe_seb_relu2_kernel(
             load_scale_rows(nc.sync, w1_plane, w1t_scales, q, 0, E)
         w1 = sb.tile([P, E, 2 * W], U8, name="w1", align_bytes=64)
         nc.sync.dma_start(w1[:].bitcast(I32), w1t_words[:, 0].rearrange("e p b -> p e b").bitcast(I32))
-        w2 = [[w2_lead[:]] + [w2_first[:, x : x + P] for x in range(0, W - P, P)]]
-        w2 = w2 + [[w2_rest[:, e, x : x + P] for x in range(0, W, P)] for e in range(E - 1)]
 
         scales_head = sb.tile([P, 2 * C], U8, name="scales_head", align_bytes=64)
         nc.vector.tensor_copy(scales_head[:], dy_plane[:].indirect(entries(list2, 0, 2 * C)))
@@ -115,35 +115,65 @@ def tile_moe_seb_relu2_kernel(
         scales_tail = sb.tile([P, C], U8, name="scales_tail", tag="w2_lead", align_bytes=64)
         nc.vector.tensor_copy(scales_tail[:], dy_plane[:].indirect(entries(list2, 2 * C, T)))
 
-        def second_layer(c, lo, hi, numbers):
-            sums2 = sb.tile([P, hi - lo], F32, name="sums2_%d_%d" % (c, lo))
-            for (y0, y1), number in zip(cut(lo, hi, (lo + W,)), numbers):
-                acc = bank(number)
-                for x0, x1 in cut(y0, y1, (C, 2 * C)):
-                    e = x0 // C
-                    group = min(e, 1)
-                    first = GROUPS[group][0]
-                    nc.tensor.matmul_mx(
-                        out=acc[:, x0 - y0 : x1 - y0],
-                        lhsT=w2[e][c].bitcast(FP8X4),
-                        lhsT_scale=w2_plane[:, e, c * P : (c + 1) * P],
-                        rhs=words[group][:, x0 - first : x1 - first].bitcast(FP8X4),
-                        rhs_scale=scales_head[:, x0:x1] if x0 < 2 * C else scales_tail[:],
-                        start=True,
-                        stop=True,
-                    )
-                nc.scalar.activation(sums2[:, y0 - lo : y1 - lo], acc[:, 0 : y1 - y0], COPY)
-            return sums2
+        def copy_out(acc, width, tag):
+            sums = sb.tile([P, width], F32, name="sums_" + tag, tag=tag, align_bytes=64)
+            nc.scalar.activation(sums[:], acc, COPY)
+            return sums
 
-        def scatter_dc(window, sums2, lo, hi):
-            nc.vector.tensor_tensor(window[:].indirect(entries(list2, lo, hi)), sums2[:], g2[:, lo:hi], MULT)
+        dc = [sb.tile([P, WINDOW], F32, name="dc_%d" % c) for c in range(ROW_TILES)]
+        for c, columns in enumerate((w2_lead[:], w2_first[:, 0:P])):
+            acc = bank(c)
+            nc.tensor.matmul_mx(
+                out=acc[:, 0:C],
+                lhsT=columns.bitcast(FP8X4),
+                lhsT_scale=w2_plane[:, 0, c * P : (c + 1) * P],
+                rhs=words[0][:].bitcast(FP8X4),
+                rhs_scale=scales_head[:, 0:C],
+                start=True,
+                stop=True,
+            )
+            sums = copy_out(acc[:, 0:C], C, "lead_%d" % c)
+            nc.vector.tensor_tensor(dc[c][:].indirect(entries(list2, 0, C)), sums[:], g2[:], MULT)
 
-        dc = {c: sb.tile([P, WINDOW], F32, name="dc_%d" % c) for c in (0, 1, 3)}
-        for group, (lo, hi) in enumerate(GROUPS):
+        gated = {}
+
+        def product(block, c0, number):
+            x = block * P
+            e = x // C
+            acc = bank(number)
+            width = W - c0 * P
+            nc.tensor.matmul_mx(
+                out=acc[:, 0:width],
+                lhsT=(words[0][:, x : x + P] if e == 0 else words[1][:, x - C : x - C + P]).bitcast(FP8X4),
+                lhsT_scale=scales_head[:, x : x + P] if x < 2 * C else scales_tail[:, x - 2 * C : x - 2 * C + P],
+                rhs=(w2_first[:, P:] if e == 0 else w2_rest[:, e - 1, :]).bitcast(FP8X4),
+                rhs_scale=w2_plane[:, e, c0 * P : W],
+                start=True,
+                stop=True,
+            )
+            sums = sb.tile([P, width], F32, name="gated_%d" % block)
+            nc.scalar.activation(sums[:], acc[:, 0:width], COPY, scale=g2_columns[:, block : block + 1])
+            for c in range(c0, ROW_TILES):
+                gated[(c, block)] = sums[:, (c - c0) * P : (c - c0 + 1) * P]
+
+        def scatter_dc(c, lo, hi, number):
+            back = bank(number)
+            for x in range(lo, hi, P):
+                nc.tensor.transpose(back[:, x - lo : x - lo + P], gated[(c, x // P)], ident[:])
+            sums = copy_out(back[:, 0 : hi - lo], hi - lo, "dc_%d_%d" % (c, lo))
+            nc.vector.tensor_copy(dc[c][:].indirect(entries(list2, lo, hi)), sums[:])
+
+        for block in range(2):
+            product(block, 2, 2 + block)
+        for c in (3, 2):
+            scatter_dc(c, 0, C, 2 + c)
+        for e in (1, 2):
+            for block in (2 * e, 2 * e + 1):
+                product(block, 0, (block + 4) % 8)
             for c in range(2):
-                scatter_dc(dc[c], second_layer(c, lo, hi, (2 * group + c,)), lo, hi)
-        scatter_dc(dc[3], second_layer(3, 0, T, (4, 5)), 0, T)
-        last_sums2 = second_layer(2, 0, T, (6, 7))
+                scatter_dc(c, e * C, (e + 1) * C, 2 * e + c)
+        for c in (3, 2):
+            scatter_dc(c, C, T, 4 + c)
 
         def make_slope(c, lo, hi, source, tag):
             slope = sb.tile([P, hi - lo], F32, name="slope_%d_%d" % (c, lo), tag=tag, align_bytes=64)
@@ -224,11 +254,6 @@ def tile_moe_seb_relu2_kernel(
                     )
             return acc[:, 0 : len(row_tiles) * width]
 
-        def copy_out(acc, width, tag):
-            sums1 = sb.tile([P, width], F32, name="sums1_" + tag, tag=tag, align_bytes=64)
-            nc.scalar.activation(sums1[:], acc, COPY)
-            return sums1
-
         dx = [sb.tile([P, WINDOW], F32, name="dx_%d" % kb) for kb in range(ROW_TILES)]
 
         def scatter(kb, lo, hi, values):
@@ -239,15 +264,10 @@ def tile_moe_seb_relu2_kernel(
 
         gather(0, 0, HALF, "da_0_0")
         gather(1, 0, P, "a_head")
-        round_off(0, 0, 2, turn(((0, 0), (1, 0)), 0)[:, 0 : 2 * P])
-        by_slot = turn(((0, 1), (0, 2)), 3)
-        for block in (1, 2):
-            round_off(block, 0, 1, by_slot[:, (block - 1) * P : block * P])
-        dc[2] = sb.tile([P, WINDOW], F32, name="dc_2", tag="slope_0_0", align_bytes=64)
-        scatter_dc(dc[2], last_sums2, 0, T)
-        gather(3, 0, P, "slope_1_0")
-        gather(2, 0, P, "da_2_0")
-        gather(2, P, T, "da_2_1")
+        round_off(0, 0, 2, turn(((0, 0), (1, 0)), 2)[:, 0 : 2 * P])
+        gather(3, 0, P, "slope_0_0")
+        gather(2, 0, P, "slope_1_0")
+        gather(2, P, T, "slope_3_0")
         gather(1, P, HALF, "slope_2_0")
         gather(3, P, HALF, "slope_2_128")
         gather(3, HALF, T, "slope_1_128")
@@ -259,7 +279,7 @@ def tile_moe_seb_relu2_kernel(
         gather(0, HALF, T, "da_0_1")
         gather(1, HALF, T, "a_tail")
         for block in (1, 2):
-            round_off(block, 1, 4, turn([(c, block) for c in (2, 1, 3)], block - 1)[:, 0 : 3 * P])
+            round_off(block, 0, 4, turn([(c, block) for c in (0, 2, 1, 3)], block - 1)[:])
         acc = [first_layer(0, (0, 1), 2), first_layer(0, (2, 3), 5)]
         sums = copy_out(acc[0], 2 * P, "s0_01")
         for kb in range(2):

@@ -62,8 +62,8 @@ def tile_moe_seb_relu2_kernel(
         ident = sb.tile([P, P], F32, name="ident")
         nc.gpsimd.memset(dy_plane[:].bitcast(I32), 0)
         nc.gpsimd.memset(w2_plane[:].bitcast(I32)[:, 0:1, :], 0)
-        nc.gpsimd.memset(w2_plane[:].bitcast(I32)[:, 1:E, :], 0)
-        nc.gpsimd.memset(w1_plane[:].bitcast(I32), 0)
+        nc.vector.memset(w2_plane[:].bitcast(I32)[:, 1:E, :], 0)
+        nc.vector.memset(w1_plane[:].bitcast(I32), 0)
         make_identity(nc, ident[:])
 
         list2 = sb.tile([P, T // 16], U16, name="list2")

@@ -1,7 +1,6 @@
 from contextlib import ExitStack
 
 import concourse.mybir as mybir
-from concourse.masks import make_identity
 
 F32 = mybir.dt.float32
 BF16 = mybir.dt.bfloat16
@@ -12,8 +11,8 @@ U8 = mybir.dt.uint8
 FP8X4 = mybir.dt.float8_e4m3fn_x4
 FP4X4 = mybir.dt.float4_e2m1fn_x4
 COPY = mybir.ActivationFunctionType.Copy
-RELU = mybir.ActivationFunctionType.Relu
 MULT = mybir.AluOpType.mult
+MAX = mybir.AluOpType.max
 
 P = 128
 PACK = 4
@@ -21,13 +20,11 @@ T = 768
 E = 3
 C = 256
 W = 512
-ROW_TILES = W // P
 QUADRANTS = 4
 HALF = T // 2
 WINDOW = 1024
 FLOPS = 2 * 2 * W * W * T
 
-GROUPS = ((0, C), (C, T))
 RUNS = ((0, P), (P, HALF), (HALF, T))
 
 
@@ -50,21 +47,18 @@ def tile_moe_seb_relu2_kernel(
         def entries(lst, lo, hi):
             return lst[:, lo // 16 : hi // 16]
 
-        def load_scale_rows(engine, plane, rows, q, e0, e1):
+        def load_scale_rows(engine, plane, rows, q):
             engine.dma_start(
-                plane[:].bitcast(I32)[32 * q : 32 * q + 4, e0:e1, :],
-                rows[e0:e1, 0, 4 * q : 4 * q + 4, :].rearrange("e r i -> r e i").bitcast(I32),
+                plane[:].bitcast(I32)[32 * q : 32 * q + 4, :, :],
+                rows[:, 0, 4 * q : 4 * q + 4, :].rearrange("e r i -> r e i").bitcast(I32),
             )
 
         dy_plane = sb.tile([P, T], U8, name="dy_plane", align_bytes=64)
         w2_plane = sb.tile([P, E, W], U8, name="w2_plane", align_bytes=64)
         w1_plane = sb.tile([P, E, W], U8, name="w1_plane", align_bytes=64)
-        ident = sb.tile([P, P], F32, name="ident")
         nc.gpsimd.memset(dy_plane[:].bitcast(I32), 0)
-        nc.gpsimd.memset(w2_plane[:].bitcast(I32)[:, 0:1, :], 0)
-        nc.vector.memset(w2_plane[:].bitcast(I32)[:, 1:E, :], 0)
+        nc.vector.memset(w2_plane[:].bitcast(I32), 0)
         nc.vector.memset(w1_plane[:].bitcast(I32), 0)
-        make_identity(nc, ident[:])
 
         list2 = sb.tile([P, T // 16], U16, name="list2")
         nc.sync.dma_start(list2[:], offs2)
@@ -73,166 +67,133 @@ def tile_moe_seb_relu2_kernel(
             queue.dma_start(dy_plane[:].bitcast(I32)[32 * q : 32 * q + 4, :], dy_scales[0, 4 * q : 4 * q + 4, :].bitcast(I32))
         dy_tile = sb.tile([P, T], I32, name="dy_tile", align_bytes=64)
         nc.sync.dma_start(dy_tile[:], dy_words[0].rearrange("p t d -> p (t d)").bitcast(I32))
-        first_words = w2t_words[0, 0].rearrange("p i d -> p (i d)").bitcast(I32)
-        w2_lead = sb.tile([P, P], I32, name="w2_lead", tag="w2_lead", align_bytes=64)
         for q, queue in enumerate((nc.scalar, nc.scalar, nc.sync, nc.scalar)):
-            load_scale_rows(queue, w2_plane, w2t_scales, q, 0, 1)
-        nc.sync.dma_start(w2_lead[:], first_words[:, 0:P])
-        g2 = sb.tile([P, C], F32, name="g2")
-        nc.sync.dma_start(g2[:], gate2[:, 0:C])
-        w2_first = sb.tile([P, W - P], I32, name="w2_first", align_bytes=64)
-        nc.sync.dma_start(w2_first[:], first_words[:, P:W])
-        g2_columns = sb.tile([P, T // P], F32, name="g2_columns")
-        with nc.allow_non_contiguous_dma(reason="one gate value a partition"):
-            nc.sync.dma_start(g2_columns[:], gate2[0, :].rearrange("(b p) -> p b", p=P))
-        for q in range(QUADRANTS):
-            load_scale_rows(nc.sync, w2_plane, w2t_scales, q, 1, E)
+            load_scale_rows(queue, w2_plane, w2t_scales, q)
+        w2_first = sb.tile([P, W], I32, name="w2_first", align_bytes=64)
+        nc.sync.dma_start(w2_first[:], w2t_words[0, 0].rearrange("p i d -> p (i d)").bitcast(I32))
+        g2 = sb.tile([P, T], F32, name="g2")
+        nc.sync.dma_start(g2[:], gate2)
         w2_rest = sb.tile([P, E - 1, W], I32, name="w2_rest", align_bytes=64)
         nc.sync.dma_start(w2_rest[:], w2t_words[1:E, 0].rearrange("e p i d -> p e (i d)").bitcast(I32))
-        a_rest = sb.tile([P, ROW_TILES - 1, T], F32, name="a_rest")
-        nc.sync.dma_start(a_rest[:], a[P:W, :].rearrange("(c p) j -> p c j", p=P))
-        a_head = sb.tile([P, HALF], F32, name="a_head", tag="a_head", align_bytes=64)
-        nc.sync.dma_start(a_head[:], a[0:P, 0:HALF])
-        a_tail = sb.tile([P, HALF], F32, name="a_tail", tag="a_tail", align_bytes=64)
-        nc.sync.dma_start(a_tail[:], a[0:P, HALF:T])
+        g1 = sb.tile([P, T], F32, name="g1")
+        nc.sync.dma_start(g1[:], gate1)
+        a_tile = sb.tile([P, PACK, T], F32, name="a_tile")
+        nc.sync.dma_start(a_tile[:], a.rearrange("(p t) j -> p t j", t=PACK))
         list1 = sb.tile([P, T // 16], U16, name="list1")
         nc.sync.dma_start(list1[:], offs)
-        g1 = sb.tile([P, T // P], F32, name="g1")
-        with nc.allow_non_contiguous_dma(reason="one gate value a partition"):
-            nc.sync.dma_start(g1[:], gate1[0, :].rearrange("(b p) -> p b", p=P))
         for q in range(QUADRANTS):
-            load_scale_rows(nc.sync, w1_plane, w1t_scales, q, 0, E)
+            load_scale_rows(nc.sync, w1_plane, w1t_scales, q)
         w1 = sb.tile([P, E, 2 * W], U8, name="w1", align_bytes=64)
         nc.sync.dma_start(w1[:].bitcast(I32), w1t_words[:, 0].rearrange("e p b -> p e b").bitcast(I32))
 
+        w2 = []
+        w2_scale = []
+
+        def sort_words(e, source):
+            ordered = sb.tile([P, W], U32, name="w2_%d" % e, align_bytes=64)
+            nc.scalar.copy(
+                ordered[:].rearrange("p (t m) -> p m t", t=PACK),
+                source.bitcast(U32).rearrange("p (m t) -> p m t", t=PACK),
+            )
+            w2.append(ordered)
+
+        def sort_scales(e0, e1):
+            ordered = sb.tile([P, e1 - e0, W], U8, name="w2_scale_%d" % e0, align_bytes=64)
+            nc.vector.tensor_copy(
+                ordered[:].rearrange("p e (t m) -> p e t m", t=PACK),
+                w2_plane[:, e0:e1, :].rearrange("p e (m t) -> p e t m", t=PACK),
+            )
+            for e in range(e0, e1):
+                w2_scale.append(ordered[:, e - e0, :])
+
+        sort_words(0, w2_first[:])
+        for e in range(1, E):
+            sort_words(e, w2_rest[:, e - 1, :])
+
         scales_head = sb.tile([P, 2 * C], U8, name="scales_head", align_bytes=64)
         nc.vector.tensor_copy(scales_head[:], dy_plane[:].indirect(entries(list2, 0, 2 * C)))
-        words = []
-        for lo, hi in GROUPS:
-            picked = sb.tile([P, hi - lo], U32, name="words_%d" % lo, align_bytes=64)
-            nc.vector.tensor_copy(picked[:], dy_tile[:].bitcast(U32).indirect(entries(list2, lo, hi)))
-            words.append(picked)
-        scales_tail = sb.tile([P, C], U8, name="scales_tail", tag="w2_lead", align_bytes=64)
+        words_first = sb.tile([P, C], U32, name="words_first", align_bytes=64)
+        nc.vector.tensor_copy(words_first[:], dy_tile[:].bitcast(U32).indirect(entries(list2, 0, C)))
+        sort_scales(0, 1)
+        words_rest = sb.tile([P, T - C], U32, name="words_rest", align_bytes=64)
+        nc.vector.tensor_copy(words_rest[:], dy_tile[:].bitcast(U32).indirect(entries(list2, C, T)))
+        scales_tail = sb.tile([P, C], U8, name="scales_tail", align_bytes=64)
         nc.vector.tensor_copy(scales_tail[:], dy_plane[:].indirect(entries(list2, 2 * C, T)))
+        sort_scales(1, E)
+        words = (words_first[:], words_rest[:, 0:C], words_rest[:, C : 2 * C])
+        scales = (scales_head[:, 0:C], scales_head[:, C : 2 * C], scales_tail[:])
 
-        def copy_out(acc, width, tag):
-            sums = sb.tile([P, width], F32, name="sums_" + tag, tag=tag, align_bytes=64)
-            nc.scalar.activation(sums[:], acc, COPY)
-            return sums
+        dc = [sb.tile([P, WINDOW], F32, name="dc_%d" % t) for t in range(PACK)]
 
-        dc = [sb.tile([P, WINDOW], F32, name="dc_%d" % c) for c in range(ROW_TILES)]
-        for c, columns in enumerate((w2_lead[:], w2_first[:, 0:P])):
-            acc = bank(c)
-            nc.tensor.matmul_mx(
-                out=acc[:, 0:C],
-                lhsT=columns.bitcast(FP8X4),
-                lhsT_scale=w2_plane[:, 0, c * P : (c + 1) * P],
-                rhs=words[0][:].bitcast(FP8X4),
-                rhs_scale=scales_head[:, 0:C],
-                start=True,
-                stop=True,
-            )
-            sums = copy_out(acc[:, 0:C], C, "lead_%d" % c)
-            nc.vector.tensor_tensor(dc[c][:].indirect(entries(list2, 0, C)), sums[:], g2[:], MULT)
-
-        gated = {}
-
-        def product(block, c0, number):
-            x = block * P
-            e = x // C
+        def second_layer(t, e0, e1, number):
             acc = bank(number)
-            width = W - c0 * P
-            nc.tensor.matmul_mx(
-                out=acc[:, 0:width],
-                lhsT=(words[0][:, x : x + P] if e == 0 else words[1][:, x - C : x - C + P]).bitcast(FP8X4),
-                lhsT_scale=scales_head[:, x : x + P] if x < 2 * C else scales_tail[:, x - 2 * C : x - 2 * C + P],
-                rhs=(w2_first[:, P:] if e == 0 else w2_rest[:, e - 1, :]).bitcast(FP8X4),
-                rhs_scale=w2_plane[:, e, c0 * P : W],
-                start=True,
-                stop=True,
-            )
-            sums = sb.tile([P, width], F32, name="gated_%d" % block)
-            nc.scalar.activation(sums[:], acc[:, 0:width], COPY, scale=g2_columns[:, block : block + 1])
-            for c in range(c0, ROW_TILES):
-                gated[(c, block)] = sums[:, (c - c0) * P : (c - c0 + 1) * P]
+            for e in range(e0, e1):
+                nc.tensor.matmul_mx(
+                    out=acc[:, (e - e0) * C : (e - e0 + 1) * C],
+                    lhsT=w2[e][:, t * P : (t + 1) * P].bitcast(FP8X4),
+                    lhsT_scale=w2_scale[e][:, t * P : (t + 1) * P],
+                    rhs=words[e].bitcast(FP8X4),
+                    rhs_scale=scales[e],
+                    start=True,
+                    stop=True,
+                )
+            return acc[:, 0 : (e1 - e0) * C]
 
-        def scatter_dc(c, lo, hi, number):
-            back = bank(number)
-            for x in range(lo, hi, P):
-                nc.tensor.transpose(back[:, x - lo : x - lo + P], gated[(c, x // P)], ident[:])
-            sums = copy_out(back[:, 0 : hi - lo], hi - lo, "dc_%d_%d" % (c, lo))
-            nc.vector.tensor_copy(dc[c][:].indirect(entries(list2, lo, hi)), sums[:])
+        def gated(t, e0, e1, number, into):
+            nc.vector.tensor_tensor(into, second_layer(t, e0, e1, number), g2[:, e0 * C : e1 * C], MULT)
 
-        for block in range(2):
-            product(block, 2, 2 + block)
-        for c in (3, 2):
-            scatter_dc(c, 0, C, 2 + c)
-        for e in (1, 2):
-            for block in (2 * e, 2 * e + 1):
-                product(block, 0, (block + 4) % 8)
-            for c in range(2):
-                scatter_dc(c, e * C, (e + 1) * C, 2 * e + c)
-        for c in (3, 2):
-            scatter_dc(c, C, T, 4 + c)
+        def scalar_scatter(window, lst, lo, hi, values):
+            nc.scalar.activation(window[:].indirect(entries(lst, lo, hi)), values, COPY)
 
-        def make_slope(c, lo, hi, source, tag):
-            slope = sb.tile([P, hi - lo], F32, name="slope_%d_%d" % (c, lo), tag=tag, align_bytes=64)
-            nc.scalar.activation(slope[:], source, RELU, scale=2.0)
-            return slope
+        lead = {t: sb.tile([P, C], F32, name="lead_%d" % t) for t in (1, 2)}
+        rest = {t: sb.tile([P, 2 * C], F32, name="rest_%d" % t) for t in (1, 2)}
+        last = sb.tile([P, T], F32, name="last")
+        plain = sb.tile([P, T], F32, name="plain")
+        for t in (1, 2):
+            gated(t, 0, 1, t - 1, lead[t][:])
+        scalar_scatter(dc[1], list2, 0, C, lead[1][:])
+        nc.scalar.activation(plain[:, 0 : 2 * C], second_layer(0, 0, 2, 6), COPY)
+        scalar_scatter(dc[2], list2, 0, C, lead[2][:])
+        nc.scalar.activation(plain[:, 2 * C : T], second_layer(0, 2, 3, 7), COPY)
+        for t in (1, 2):
+            gated(t, 1, 3, t + 1, rest[t][:])
+            for e in (1, 2):
+                scalar_scatter(dc[t], list2, e * C, (e + 1) * C, rest[t][:, (e - 1) * C : e * C])
+        gated(3, 0, 2, 4, last[:, 0 : 2 * C])
+        gated(3, 2, 3, 5, last[:, 2 * C : T])
+        nc.vector.tensor_tensor(dc[0][:].indirect(list2[:]), plain[:], g2[:], MULT)
+        for lo in (0, HALF):
+            scalar_scatter(dc[3], list2, lo, lo + HALF, last[:, lo : lo + HALF])
 
-        slopes = {}
-        for c, lo, hi in ((1, 0, P), (3, 0, P), (2, 0, P), (2, P, T), (1, P, HALF), (3, P, HALF), (3, HALF, T), (1, HALF, T)):
-            slopes[(c, lo)] = make_slope(c, lo, hi, a_rest[:, c - 1, lo:hi], "slope_%d_%d" % (c, lo))
-        slopes[(0, 0)] = make_slope(0, 0, HALF, a_head[:], "slope_0_0")
+        factor = [sb.tile([P, T], F32, name="factor_%d" % t) for t in range(PACK)]
+        da = [sb.tile([P, PACK, hi - lo], F32, name="da_%d" % lo) for lo, hi in RUNS]
 
-        da = {}
+        def make_factor(t):
+            nc.vector.scalar_tensor_tensor(factor[t][:], a_tile[:, t, :], 0.0, g1[:], MAX, MULT)
 
-        def gather(c, lo, hi, tag):
-            piece = sb.tile([P, hi - lo], F32, name="da_%d_%d" % (c, lo), tag=tag, align_bytes=64)
-            nc.vector.tensor_tensor(piece[:], dc[c][:].indirect(entries(list1, lo, hi)), slopes[(c, lo)][:], MULT)
-            for x in range(lo, hi, P):
-                da[(c, x // P)] = piece[:, x - lo : x - lo + P]
+        def gather(t, run):
+            lo, hi = RUNS[run]
+            nc.vector.tensor_tensor(da[run][:, t, :], dc[t][:].indirect(entries(list1, lo, hi)), factor[t][:, lo:hi], MULT)
 
-        rounded = {}
+        woven = {}
 
-        def turn(parts, number):
-            by_slot = bank(number)
-            for c, block in parts:
-                x = sorted(parts, key=lambda part: part[::-1]).index((c, block))
-                nc.tensor.transpose(by_slot[:, x * P : (x + 1) * P], da[(c, block)], ident[:])
-            return by_slot
-
-        def round_off(block, c0, c1, by_slot):
-            if block not in rounded:
-                tag = "rounded_%d" % block
-                rounded[block] = sb.tile([P, W], BF16, name=tag, tag=tag, align_bytes=64)
-            nc.scalar.activation(
-                rounded[block][:].rearrange("j (u p x) -> j u p x", u=2, x=2)[:, :, c0 * P // PACK : c1 * P // PACK, :],
-                by_slot.rearrange("j (p u x) -> j u p x", u=2, x=2),
-                COPY,
-                scale=g1[:, block : block + 1],
-            )
-
-        def turn_back(block, number, h, first_block):
-            back = bank(number)
-            pairs = rounded[block][:].bitcast(F32)
-            for u in range(2):
-                nc.tensor.transpose(back[:, u * P : (u + 1) * P], pairs[:, u * P : (u + 1) * P], ident[:])
-            b = block - first_block
-            nc.scalar.copy(
-                h[:].bitcast(F32)[:, 2 * b * P : 2 * (b + 1) * P].rearrange("p (j u) -> p j u", u=2),
-                back[:, 0 : 2 * P].rearrange("p (u j) -> p j u", u=2),
-            )
-
-        def new_h(lo, hi):
-            return sb.tile([P, PACK * (hi - lo)], BF16, name="h_%d" % lo, tag="h_%d" % lo, align_bytes=64)
+        def weave(run, on_scalar):
+            lo, hi = RUNS[run]
+            h = sb.tile([P, hi - lo, PACK], BF16, name="h_%d" % run, align_bytes=64)
+            source = da[run][:].rearrange("p t j -> p j t")
+            if on_scalar:
+                nc.scalar.activation(h[:], source, COPY, scale=2.0)
+            else:
+                nc.vector.tensor_scalar(h[:], source, 2.0, None, MULT)
+            woven[run] = h
 
         quantised = {}
 
-        def quantise(h, lo, hi):
+        def quantise(run):
+            lo, hi = RUNS[run]
             codes = sb.tile([P, hi - lo], U32, name="codes_%d" % lo, align_bytes=64)
             plane = sb.tile([P, hi - lo], U8, name="plane_%d" % lo, align_bytes=64)
-            nc.vector.quantize_mx(out=codes[:].bitcast(FP8X4), scales=plane[:], in_=h[:])
+            nc.vector.quantize_mx(out=codes[:].bitcast(FP8X4), scales=plane[:], in_=woven[run][:].rearrange("p j t -> p (j t)"))
             for y0, y1 in cut(lo, hi, (C, 2 * C)):
                 quantised[y0] = (codes[:, y0 - lo : y1 - lo], plane[:, y0 - lo : y1 - lo])
 
@@ -254,64 +215,51 @@ def tile_moe_seb_relu2_kernel(
                     )
             return acc[:, 0 : len(row_tiles) * width]
 
-        dx = [sb.tile([P, WINDOW], F32, name="dx_%d" % kb) for kb in range(ROW_TILES)]
-
-        def scatter(kb, lo, hi, values):
-            nc.vector.tensor_copy(dx[kb][:].indirect(entries(list1, lo, hi)), values)
+        dx = [sb.tile([P, WINDOW], F32, name="dx_%d" % kb) for kb in range(PACK)]
+        own = sb.tile([P, T], F32, name="own")
 
         def store(kb):
             nc.sync.dma_start(out[kb * P : (kb + 1) * P, :], dx[kb][:, 0:T])
 
-        gather(0, 0, HALF, "da_0_0")
-        gather(1, 0, P, "a_head")
-        round_off(0, 0, 2, turn(((0, 0), (1, 0)), 2)[:, 0 : 2 * P])
-        gather(3, 0, P, "slope_0_0")
-        gather(2, 0, P, "slope_1_0")
-        gather(2, P, T, "slope_3_0")
-        gather(1, P, HALF, "slope_2_0")
-        gather(3, P, HALF, "slope_2_128")
-        gather(3, HALF, T, "slope_1_128")
-        round_off(0, 2, 4, turn(((3, 0), (2, 0)), 0)[:, 0 : 2 * P])
-        h0 = new_h(0, P)
-        turn_back(0, 1, h0, 0)
-        slopes[(0, HALF)] = make_slope(0, HALF, T, a_tail[:], "rounded_0")
-        quantise(h0, 0, P)
-        gather(0, HALF, T, "da_0_1")
-        gather(1, HALF, T, "a_tail")
-        for block in (1, 2):
-            round_off(block, 0, 4, turn([(c, block) for c in (0, 2, 1, 3)], block - 1)[:])
-        acc = [first_layer(0, (0, 1), 2), first_layer(0, (2, 3), 5)]
-        sums = copy_out(acc[0], 2 * P, "s0_01")
-        for kb in range(2):
-            scatter(kb, 0, P, sums[:, kb * P : (kb + 1) * P])
-        h1 = new_h(P, HALF)
-        turn_back(1, 3, h1, 1)
-        turn_back(2, 4, h1, 1)
-        quantise(h1, P, HALF)
-        by_slot = [turn([(c, block) for c in (2, 3, 0, 1)], number)[:] for block, number in ((3, 1), (4, 3), (5, 4))]
-        sums = copy_out(acc[1], 2 * P, "rounded_2")
-        round_off(3, 0, 4, by_slot[0])
-        for kb in range(2, ROW_TILES):
-            scatter(kb, 0, P, sums[:, (kb - 2) * P : (kb - 1) * P])
-        round_off(4, 0, 4, by_slot[1])
-        acc = [first_layer(1, (0,), 0), first_layer(1, (1,), 2), first_layer(1, (2, 3), 6)]
-        sums = copy_out(acc[0], C, "s1_0")
-        scatter(0, P, HALF, sums[:])
-        round_off(5, 0, 4, by_slot[2])
-        h2 = new_h(HALF, 2 * C)
-        h3 = new_h(2 * C, T)
-        turn_back(3, 7, h2, 3)
-        turn_back(4, 5, h3, 4)
-        turn_back(5, 1, h3, 4)
-        quantise(h2, HALF, 2 * C)
-        quantise(h3, 2 * C, T)
-        scatter(1, P, HALF, copy_out(acc[1], C, "rounded_5")[:])
-        for kb, number in ((0, 7), (1, 5)):
-            scatter(kb, HALF, T, copy_out(first_layer(2, (kb,), number), HALF, "s2_%d" % kb)[:])
-            store(kb)
-        both = sb.tile([P, 2, T - P], F32, name="both")
-        nc.scalar.activation(both[:, :, 0:C], acc[2].rearrange("p (x j) -> p x j", x=2), COPY)
-        for kb, number in ((2, 3), (3, 4)):
-            nc.scalar.activation(both[:, kb - 2, C : T - P], first_layer(2, (kb,), number), COPY)
-            scatter(kb, P, T, both[:, kb - 2, :])
-            store(kb)
+        def copy_out(acc, name):
+            sums = sb.tile([P, acc.shape[1]], F32, name=name)
+            nc.vector.tensor_copy(sums[:], acc)
+            return sums
+
+        for t in range(2):
+            make_factor(t)
+            for run in range(3):
+                gather(t, run)
+        make_factor(2)
+        make_factor(3)
+        for run in range(3):
+            gather(2, run)
+        gather(3, 0)
+        gather(3, 1)
+        weave(0, False)
+        weave(1, True)
+        gather(3, 2)
+        quantise(0)
+        weave(2, False)
+        sums = copy_out(first_layer(0, (1, 2, 3), 0), "s0")
+        for kb in (1, 2, 3):
+            scalar_scatter(dx[kb], list1, 0, P, sums[:, (kb - 1) * P : kb * P])
+        quantise(1)
+        nc.vector.tensor_copy(own[:, 0:P], first_layer(0, (0,), 1))
+        quantise(2)
+        sums = copy_out(first_layer(1, (1, 2), 2), "s1_12")
+        for kb in (1, 2):
+            scalar_scatter(dx[kb], list1, P, HALF, sums[:, (kb - 1) * C : kb * C])
+        sums = copy_out(first_layer(1, (3,), 3), "s1_3")
+        scalar_scatter(dx[3], list1, P, HALF, sums[:])
+        nc.vector.tensor_copy(own[:, P:HALF], first_layer(1, (0,), 4))
+        nc.vector.tensor_copy(own[:, HALF:T], first_layer(2, (0,), 5))
+        tails = {kb: copy_out(first_layer(2, (kb,), number), "s2_%d" % kb) for kb, number in ((2, 6), (3, 7), (1, 0))}
+        nc.vector.tensor_copy(dx[0][:].indirect(list1[:]), own[:])
+        store(0)
+        scalar_scatter(dx[2], list1, HALF, T, tails[2][:])
+        store(2)
+        nc.vector.tensor_copy(dx[1][:].indirect(entries(list1, HALF, T)), tails[1][:])
+        store(1)
+        scalar_scatter(dx[3], list1, HALF, T, tails[3][:])
+        store(3)

@@ -39,6 +39,7 @@ def tile_moe_seb_relu2_kernel(
     nc = tc.nc
     with ExitStack() as ctx:
         sb = ctx.enter_context(tc.tile_pool(name="sb", bufs=1))
+        held = ctx.enter_context(tc.tile_pool(name="held", bufs=1))
         ps = ctx.enter_context(tc.psum_pool(name="ps", bufs=1))
 
         def bank(number):
@@ -54,10 +55,12 @@ def tile_moe_seb_relu2_kernel(
             )
 
         dy_plane = sb.tile([P, T], U8, name="dy_plane", align_bytes=64)
-        w2_plane = sb.tile([P, E, W], U8, name="w2_plane", align_bytes=64)
+        w2_plane = sb.tile([P, W], U8, name="w2_plane", align_bytes=64)
+        w2_plane_last = sb.tile([P, W], U8, name="w2_plane_last", align_bytes=64)
         w1_plane = sb.tile([P, E, W], U8, name="w1_plane", align_bytes=64)
         nc.gpsimd.memset(dy_plane[:].bitcast(I32), 0)
         nc.vector.memset(w2_plane[:].bitcast(I32), 0)
+        nc.vector.memset(w2_plane_last[:].bitcast(I32), 0)
         nc.vector.memset(w1_plane[:].bitcast(I32), 0)
 
         list2 = sb.tile([P, T // 16], U16, name="list2")
@@ -67,18 +70,26 @@ def tile_moe_seb_relu2_kernel(
             queue.dma_start(dy_plane[:].bitcast(I32)[32 * q : 32 * q + 4, :], dy_scales[0, 4 * q : 4 * q + 4, :].bitcast(I32))
         dy_tile = sb.tile([P, T], I32, name="dy_tile", align_bytes=64)
         nc.sync.dma_start(dy_tile[:], dy_words[0].rearrange("p t d -> p (t d)").bitcast(I32))
-        for q, queue in enumerate((nc.scalar, nc.scalar, nc.sync, nc.scalar)):
-            load_scale_rows(queue, w2_plane, w2t_scales, q)
         w2_first = sb.tile([P, W], I32, name="w2_first", align_bytes=64)
         nc.sync.dma_start(w2_first[:], w2t_words[0, 0].rearrange("p i d -> p (i d)").bitcast(I32))
-        g2 = sb.tile([P, T], F32, name="g2")
-        nc.sync.dma_start(g2[:], gate2)
+        for q in range(QUADRANTS):
+            queue = nc.scalar if q == 0 else nc.sync
+            queue.dma_start(w2_plane[:].bitcast(I32)[32 * q : 32 * q + 8, :], w2t_scales[0:2, 0, 4 * q : 4 * q + 4, :].bitcast(I32))
         w2_rest = sb.tile([P, E - 1, W], I32, name="w2_rest", align_bytes=64)
         nc.sync.dma_start(w2_rest[:], w2t_words[1:E, 0].rearrange("e p i d -> p e (i d)").bitcast(I32))
+        g2_first = held.tile([P, C], F32, name="g2_first", offset=0, align_bytes=64)
+        nc.sync.dma_start(g2_first[:], gate2[:, 0:C])
+        for q in range(QUADRANTS):
+            nc.sync.dma_start(w2_plane_last[:].bitcast(I32)[32 * q : 32 * q + 4, :], w2t_scales[2, 0, 4 * q : 4 * q + 4, :].bitcast(I32))
+        g2_rest = sb.tile([P, T - C], F32, name="g2_rest")
+        nc.sync.dma_start(g2_rest[:], gate2[:, C:T])
+        a_rows = a.rearrange("(p t) j -> p t j", t=PACK)
+        a_first = sb.tile([P, T], F32, name="a_first", tag="dc_0")
+        nc.sync.dma_start(a_first[:], a_rows[:, 0, :])
+        a_rest = sb.tile([P, PACK - 1, T], F32, name="a_rest")
+        nc.sync.dma_start(a_rest[:], a_rows[:, 1:PACK, :])
         g1 = sb.tile([P, T], F32, name="g1")
         nc.sync.dma_start(g1[:], gate1)
-        a_tile = sb.tile([P, PACK, T], F32, name="a_tile")
-        nc.sync.dma_start(a_tile[:], a.rearrange("(p t) j -> p t j", t=PACK))
         list1 = sb.tile([P, T // 16], U16, name="list1")
         nc.sync.dma_start(list1[:], offs)
         for q in range(QUADRANTS):
@@ -97,14 +108,12 @@ def tile_moe_seb_relu2_kernel(
             )
             w2.append(ordered)
 
-        def sort_scales(e0, e1):
-            ordered = sb.tile([P, e1 - e0, W], U8, name="w2_scale_%d" % e0, align_bytes=64)
+        def sort_scales(plane, ordered):
             nc.vector.tensor_copy(
-                ordered[:].rearrange("p e (t m) -> p e t m", t=PACK),
-                w2_plane[:, e0:e1, :].rearrange("p e (m t) -> p e t m", t=PACK),
+                ordered[:].rearrange("p (t m) -> p t m", t=PACK),
+                plane[:].rearrange("p (m t) -> p t m", t=PACK),
             )
-            for e in range(e0, e1):
-                w2_scale.append(ordered[:, e - e0, :])
+            return ordered
 
         sort_words(0, w2_first[:])
         for e in range(1, E):
@@ -112,18 +121,14 @@ def tile_moe_seb_relu2_kernel(
 
         scales_head = sb.tile([P, 2 * C], U8, name="scales_head", align_bytes=64)
         nc.vector.tensor_copy(scales_head[:], dy_plane[:].indirect(entries(list2, 0, 2 * C)))
-        words_first = sb.tile([P, C], U32, name="words_first", align_bytes=64)
-        nc.vector.tensor_copy(words_first[:], dy_tile[:].bitcast(U32).indirect(entries(list2, 0, C)))
-        sort_scales(0, 1)
-        words_rest = sb.tile([P, T - C], U32, name="words_rest", align_bytes=64)
-        nc.vector.tensor_copy(words_rest[:], dy_tile[:].bitcast(U32).indirect(entries(list2, C, T)))
-        scales_tail = sb.tile([P, C], U8, name="scales_tail", align_bytes=64)
-        nc.vector.tensor_copy(scales_tail[:], dy_plane[:].indirect(entries(list2, 2 * C, T)))
-        sort_scales(1, E)
-        words = (words_first[:], words_rest[:, 0:C], words_rest[:, C : 2 * C])
-        scales = (scales_head[:, 0:C], scales_head[:, C : 2 * C], scales_tail[:])
+        words = {}
 
-        dc = [sb.tile([P, WINDOW], F32, name="dc_%d" % t) for t in range(PACK)]
+        def gather_words(e, picked):
+            words[e] = picked
+            nc.vector.tensor_copy(picked[:], dy_tile[:].bitcast(U32).indirect(entries(list2, e * C, (e + 1) * C)))
+
+        scales = {0: scales_head[:, 0:C], 1: scales_head[:, C : 2 * C]}
+        dc = {t: sb.tile([P, WINDOW], F32, name="dc_%d" % t) for t in range(1, PACK)}
 
         def second_layer(t, e0, e1, number):
             acc = bank(number)
@@ -132,54 +137,58 @@ def tile_moe_seb_relu2_kernel(
                     out=acc[:, (e - e0) * C : (e - e0 + 1) * C],
                     lhsT=w2[e][:, t * P : (t + 1) * P].bitcast(FP8X4),
                     lhsT_scale=w2_scale[e][:, t * P : (t + 1) * P],
-                    rhs=words[e].bitcast(FP8X4),
+                    rhs=words[e][:].bitcast(FP8X4),
                     rhs_scale=scales[e],
                     start=True,
                     stop=True,
                 )
             return acc[:, 0 : (e1 - e0) * C]
 
-        def gated(t, e0, e1, number, into):
-            nc.vector.tensor_tensor(into, second_layer(t, e0, e1, number), g2[:, e0 * C : e1 * C], MULT)
+        def gated(acc, e0, into):
+            nc.vector.tensor_tensor(into, acc, g2_first[:] if e0 == 0 else g2_rest[:], MULT)
 
         def scalar_scatter(window, lst, lo, hi, values):
             nc.scalar.activation(window[:].indirect(entries(lst, lo, hi)), values, COPY)
 
-        lead = {t: sb.tile([P, C], F32, name="lead_%d" % t) for t in (1, 2)}
-        rest = {t: sb.tile([P, 2 * C], F32, name="rest_%d" % t) for t in (1, 2)}
-        last = sb.tile([P, T], F32, name="last")
-        plain = sb.tile([P, T], F32, name="plain")
-        for t in (1, 2):
-            gated(t, 0, 1, t - 1, lead[t][:])
-        scalar_scatter(dc[1], list2, 0, C, lead[1][:])
-        nc.scalar.activation(plain[:, 0 : 2 * C], second_layer(0, 0, 2, 6), COPY)
-        scalar_scatter(dc[2], list2, 0, C, lead[2][:])
-        nc.scalar.activation(plain[:, 2 * C : T], second_layer(0, 2, 3, 7), COPY)
-        for t in (1, 2):
-            gated(t, 1, 3, t + 1, rest[t][:])
+        lead = {t: sb.tile([P, C], F32, name="lead_%d" % t) for t in range(PACK)}
+        rest = {t: sb.tile([P, 2 * C], F32, name="rest_%d" % t) for t in range(PACK)}
+
+        for e in range(2):
+            gather_words(e, sb.tile([P, C], U32, name="words_%d" % e, align_bytes=64))
+        both = sort_scales(w2_plane, sb.tile([P, W], U8, name="w2_scale", align_bytes=64))
+        w2_scale.extend((both[:], both[4:P, :]))
+        for t in (1, 2, 3, 0):
+            gated(second_layer(t, 0, 1, t), 0, lead[t][:])
+            if t > 0:
+                scalar_scatter(dc[t], list2, 0, C, lead[t][:])
+        gather_words(2, held.tile([P, C], U32, name="words_2", offset=3 * C, align_bytes=64))
+        scales_tail = held.tile([P, C], U8, name="scales_tail", offset=0, align_bytes=64)
+        nc.vector.tensor_copy(scales_tail[:], dy_plane[:].indirect(entries(list2, 2 * C, T)))
+        scales[2] = scales_tail[:]
+        w2_scale.append(sort_scales(w2_plane_last, sb.tile([P, W], U8, name="w2_scale_last", align_bytes=64))[:])
+        nc.scalar.activation(rest[0][:], second_layer(0, 1, 3, 4), COPY)
+        for t in (1, 2, 3):
+            gated(second_layer(t, 1, 3, t + 4), 1, rest[t][:])
             for e in (1, 2):
                 scalar_scatter(dc[t], list2, e * C, (e + 1) * C, rest[t][:, (e - 1) * C : e * C])
-        gated(3, 0, 2, 4, last[:, 0 : 2 * C])
-        gated(3, 2, 3, 5, last[:, 2 * C : T])
-        nc.vector.tensor_tensor(dc[0][:].indirect(list2[:]), plain[:], g2[:], MULT)
-        for lo in (0, HALF):
-            scalar_scatter(dc[3], list2, lo, lo + HALF, last[:, lo : lo + HALF])
 
         factor = [sb.tile([P, T], F32, name="factor_%d" % t) for t in range(PACK)]
         da = [sb.tile([P, PACK, hi - lo], F32, name="da_%d" % lo) for lo, hi in RUNS]
 
         def make_factor(t):
-            nc.vector.scalar_tensor_tensor(factor[t][:], a_tile[:, t, :], 0.0, g1[:], MAX, MULT)
+            nc.vector.scalar_tensor_tensor(factor[t][:], a_first[:] if t == 0 else a_rest[:, t - 1, :], 0.0, g1[:], MAX, MULT)
 
-        def gather(t, run):
-            lo, hi = RUNS[run]
-            nc.vector.tensor_tensor(da[run][:, t, :], dc[t][:].indirect(entries(list1, lo, hi)), factor[t][:, lo:hi], MULT)
+        def gather(t, run, lo, hi):
+            first = RUNS[run][0]
+            nc.vector.tensor_tensor(
+                da[run][:, t, lo - first : hi - first], dc[t][:].indirect(entries(list1, lo, hi)), factor[t][:, lo:hi], MULT
+            )
 
         woven = {}
 
-        def weave(run, on_scalar):
+        def weave(run, on_scalar, tag):
             lo, hi = RUNS[run]
-            h = sb.tile([P, hi - lo, PACK], BF16, name="h_%d" % run, align_bytes=64)
+            h = sb.tile([P, hi - lo, PACK], BF16, name="h_%d" % run, tag=tag, align_bytes=64)
             source = da[run][:].rearrange("p t j -> p j t")
             if on_scalar:
                 nc.scalar.activation(h[:], source, COPY, scale=2.0)
@@ -191,7 +200,7 @@ def tile_moe_seb_relu2_kernel(
 
         def quantise(run):
             lo, hi = RUNS[run]
-            codes = sb.tile([P, hi - lo], U32, name="codes_%d" % lo, align_bytes=64)
+            codes = sb.tile([P, hi - lo], U32, name="codes_%d" % lo, tag="codes_%d" % lo, align_bytes=64)
             plane = sb.tile([P, hi - lo], U8, name="plane_%d" % lo, align_bytes=64)
             nc.vector.quantize_mx(out=codes[:].bitcast(FP8X4), scales=plane[:], in_=woven[run][:].rearrange("p j t -> p (j t)"))
             for y0, y1 in cut(lo, hi, (C, 2 * C)):
@@ -226,34 +235,42 @@ def tile_moe_seb_relu2_kernel(
             nc.vector.tensor_copy(sums[:], acc)
             return sums
 
-        for t in range(2):
-            make_factor(t)
-            for run in range(3):
-                gather(t, run)
+        make_factor(0)
+        make_factor(1)
+        dc[0] = sb.tile([P, WINDOW], F32, name="dc_0", tag="dc_0")
+        nc.vector.tensor_tensor(dc[0][:].indirect(entries(list2, C, T)), rest[0][:], g2_rest[:], MULT)
+        scalar_scatter(dc[0], list2, 0, C, lead[0][:])
         make_factor(2)
         make_factor(3)
-        for run in range(3):
-            gather(2, run)
-        gather(3, 0)
-        gather(3, 1)
-        weave(0, False)
-        weave(1, True)
-        gather(3, 2)
+        for t in (1, 2, 3):
+            for run, (lo, hi) in enumerate(RUNS):
+                gather(t, run, lo, hi)
+        picked = sb.tile([P, HALF], F32, name="picked")
+        nc.scalar.activation(picked[:], dc[0][:].indirect(entries(list1, HALF, T)), COPY)
+        gather(0, 0, 0, P)
+        gather(0, 1, P, C)
+        weave(0, False, "h_0")
+        gather(0, 1, C, HALF)
+        weave(1, True, "h_1")
         quantise(0)
-        weave(2, False)
-        sums = copy_out(first_layer(0, (1, 2, 3), 0), "s0")
-        for kb in (1, 2, 3):
-            scalar_scatter(dx[kb], list1, 0, P, sums[:, (kb - 1) * P : kb * P])
+        nc.vector.tensor_tensor(da[2][:, 0, :], picked[:], factor[0][:, HALF:T], MULT)
+        sums = copy_out(first_layer(0, (1,), 0), "s0_1")
+        scalar_scatter(dx[1], list1, 0, P, sums[:])
+        sums = copy_out(first_layer(0, (2, 3), 1), "s0_23")
+        for kb in (2, 3):
+            scalar_scatter(dx[kb], list1, 0, P, sums[:, (kb - 2) * P : (kb - 1) * P])
         quantise(1)
-        nc.vector.tensor_copy(own[:, 0:P], first_layer(0, (0,), 1))
-        quantise(2)
-        sums = copy_out(first_layer(1, (1, 2), 2), "s1_12")
+        first_own = first_layer(0, (0,), 2)
+        sums = copy_out(first_layer(1, (1, 2), 3), "s1_12")
         for kb in (1, 2):
             scalar_scatter(dx[kb], list1, P, HALF, sums[:, (kb - 1) * C : kb * C])
-        sums = copy_out(first_layer(1, (3,), 3), "s1_3")
+        weave(2, False, "codes_0")
+        sums = copy_out(first_layer(1, (3,), 4), "s1_3")
         scalar_scatter(dx[3], list1, P, HALF, sums[:])
-        nc.vector.tensor_copy(own[:, P:HALF], first_layer(1, (0,), 4))
-        nc.vector.tensor_copy(own[:, HALF:T], first_layer(2, (0,), 5))
+        quantise(2)
+        nc.vector.tensor_copy(own[:, 0:P], first_own)
+        nc.vector.tensor_copy(own[:, P:HALF], first_layer(1, (0,), 5))
+        nc.vector.tensor_copy(own[:, HALF:T], first_layer(2, (0,), 1))
         tails = {kb: copy_out(first_layer(2, (kb,), number), "s2_%d" % kb) for kb, number in ((2, 6), (3, 7), (1, 0))}
         nc.vector.tensor_copy(dx[0][:].indirect(list1[:]), own[:])
         store(0)

@@ -239,7 +239,8 @@ def tile_moe_seb_relu2_kernel(
         make_factor(1)
         dc[0] = sb.tile([P, WINDOW], F32, name="dc_0", tag="dc_0")
         nc.vector.tensor_tensor(dc[0][:].indirect(entries(list2, C, T)), rest[0][:], g2_rest[:], MULT)
-        scalar_scatter(dc[0], list2, 0, C, lead[0][:])
+        nc.vector.tensor_copy(dc[0][:].indirect(entries(list2, P, C)), lead[0][:, P:C])
+        scalar_scatter(dc[0], list2, 0, P, lead[0][:, 0:P])
         make_factor(2)
         make_factor(3)
         for t in (1, 2, 3):

@@ -150,7 +150,7 @@ def tile_moe_seb_relu2_kernel(
         def scalar_scatter(window, lst, lo, hi, values):
             nc.scalar.activation(window[:].indirect(entries(lst, lo, hi)), values, COPY)
 
-        lead = {t: sb.tile([P, C], F32, name="lead_%d" % t) for t in range(PACK)}
+        lead = {t: sb.tile([P, C], F32, name="lead_%d" % t, tag="lead_%d" % t) for t in range(PACK)}
         rest = {t: sb.tile([P, 2 * C], F32, name="rest_%d" % t) for t in range(PACK)}
 
         for e in range(2):
@@ -243,18 +243,22 @@ def tile_moe_seb_relu2_kernel(
         scalar_scatter(dc[0], list2, 0, P, lead[0][:, 0:P])
         make_factor(2)
         make_factor(3)
-        for t in (1, 2, 3):
+        for t in (1, 2):
             for run, (lo, hi) in enumerate(RUNS):
                 gather(t, run, lo, hi)
-        picked = sb.tile([P, HALF], F32, name="picked")
-        nc.scalar.activation(picked[:], dc[0][:].indirect(entries(list1, HALF, T)), COPY)
+        picked = {}
+        for t in (0, 3):
+            picked[t] = sb.tile([P, HALF], F32, name="picked_%d" % t, tag="lead_0" if t == 3 else "picked_0")
+            nc.scalar.activation(picked[t][:], dc[t][:].indirect(entries(list1, HALF, T)), COPY)
+        gather(3, 0, 0, P)
+        gather(3, 1, P, HALF)
         gather(0, 0, 0, P)
-        gather(0, 1, P, C)
+        gather(0, 1, P, HALF)
         weave(0, False, "h_0")
-        gather(0, 1, C, HALF)
         weave(1, True, "h_1")
+        nc.vector.tensor_tensor(da[2][:, 0, :], picked[0][:], factor[0][:, HALF:T], MULT)
         quantise(0)
-        nc.vector.tensor_tensor(da[2][:, 0, :], picked[:], factor[0][:, HALF:T], MULT)
+        nc.vector.tensor_tensor(da[2][:, 3, :], picked[3][:], factor[3][:, HALF:T], MULT)
         sums = copy_out(first_layer(0, (1,), 0), "s0_1")
         scalar_scatter(dx[1], list1, 0, P, sums[:])
         sums = copy_out(first_layer(0, (2, 3), 1), "s0_23")

@@ -81,8 +81,8 @@ def tile_moe_seb_relu2_kernel(
         nc.sync.dma_start(g2_first[:], gate2[:, 0:C])
         for q in range(QUADRANTS):
             nc.sync.dma_start(w2_plane_last[:].bitcast(I32)[32 * q : 32 * q + 4, :], w2t_scales[2, 0, 4 * q : 4 * q + 4, :].bitcast(I32))
-        g2_rest = sb.tile([P, T - C], F32, name="g2_rest")
-        nc.sync.dma_start(g2_rest[:], gate2[:, C:T])
+        g2 = sb.tile([P, T], F32, name="g2")
+        nc.sync.dma_start(g2[:], gate2)
         a_rows = a.rearrange("(p t) j -> p t j", t=PACK)
         a_first = sb.tile([P, T], F32, name="a_first", tag="dc_0")
         nc.sync.dma_start(a_first[:], a_rows[:, 0, :])
@@ -144,33 +144,38 @@ def tile_moe_seb_relu2_kernel(
                 )
             return acc[:, 0 : (e1 - e0) * C]
 
-        def gated(acc, e0, into):
-            nc.vector.tensor_tensor(into, acc, g2_first[:] if e0 == 0 else g2_rest[:], MULT)
+        def gated(acc, gate, into):
+            nc.vector.tensor_tensor(into, acc, gate, MULT)
 
         def scalar_scatter(window, lst, lo, hi, values):
             nc.scalar.activation(window[:].indirect(entries(lst, lo, hi)), values, COPY)
 
-        lead = {t: sb.tile([P, C], F32, name="lead_%d" % t, tag="lead_%d" % t) for t in range(PACK)}
-        rest = {t: sb.tile([P, 2 * C], F32, name="rest_%d" % t) for t in range(PACK)}
+        lead = {t: sb.tile([P, C], F32, name="lead_%d" % t) for t in range(1, PACK)}
+        rest = {t: sb.tile([P, 2 * C], F32, name="rest_%d" % t) for t in range(1, PACK)}
+        whole = sb.tile([P, T], F32, name="whole", tag="whole")
 
         for e in range(2):
             gather_words(e, sb.tile([P, C], U32, name="words_%d" % e, align_bytes=64))
         both = sort_scales(w2_plane, sb.tile([P, W], U8, name="w2_scale", align_bytes=64))
         w2_scale.extend((both[:], both[4:P, :]))
-        for t in (1, 2, 3, 0):
-            gated(second_layer(t, 0, 1, t), 0, lead[t][:])
-            if t > 0:
-                scalar_scatter(dc[t], list2, 0, C, lead[t][:])
+        first = {t: second_layer(t, 0, 1, t) for t in (1, 2, 3, 0)}
+        for t in (1, 2):
+            gated(first[t], g2_first[:], lead[t][:])
+            scalar_scatter(dc[t], list2, 0, C, lead[t][:])
         gather_words(2, held.tile([P, C], U32, name="words_2", offset=3 * C, align_bytes=64))
         scales_tail = held.tile([P, C], U8, name="scales_tail", offset=0, align_bytes=64)
         nc.vector.tensor_copy(scales_tail[:], dy_plane[:].indirect(entries(list2, 2 * C, T)))
         scales[2] = scales_tail[:]
         w2_scale.append(sort_scales(w2_plane_last, sb.tile([P, W], U8, name="w2_scale_last", align_bytes=64))[:])
-        nc.scalar.activation(rest[0][:], second_layer(0, 1, 3, 4), COPY)
+        gated(first[3], g2[:, 0:C], lead[3][:])
+        gated(first[0], g2[:, 0:C], whole[:, 0:C])
+        scalar_scatter(dc[3], list2, 0, C, lead[3][:])
+        later = {t: second_layer(t, 1, 3, number) for t, number in ((1, 4), (2, 5), (3, 6), (0, 7))}
         for t in (1, 2, 3):
-            gated(second_layer(t, 1, 3, t + 4), 1, rest[t][:])
+            gated(later[t], g2[:, C:T], rest[t][:])
             for e in (1, 2):
                 scalar_scatter(dc[t], list2, e * C, (e + 1) * C, rest[t][:, (e - 1) * C : e * C])
+        gated(later[0], g2[:, C:T], whole[:, C:T])
 
         factor = [sb.tile([P, T], F32, name="factor_%d" % t) for t in range(PACK)]
         da = [sb.tile([P, PACK, hi - lo], F32, name="da_%d" % lo) for lo, hi in RUNS]
@@ -225,7 +230,7 @@ def tile_moe_seb_relu2_kernel(
             return acc[:, 0 : len(row_tiles) * width]
 
         dx = [sb.tile([P, WINDOW], F32, name="dx_%d" % kb) for kb in range(PACK)]
-        own = sb.tile([P, T], F32, name="own")
+        own = sb.tile([P, T - P], F32, name="own")
 
         def store(kb):
             nc.sync.dma_start(out[kb * P : (kb + 1) * P, :], dx[kb][:, 0:T])
@@ -238,9 +243,8 @@ def tile_moe_seb_relu2_kernel(
         make_factor(0)
         make_factor(1)
         dc[0] = sb.tile([P, WINDOW], F32, name="dc_0", tag="dc_0")
-        nc.vector.tensor_tensor(dc[0][:].indirect(entries(list2, C, T)), rest[0][:], g2_rest[:], MULT)
-        nc.vector.tensor_copy(dc[0][:].indirect(entries(list2, P, C)), lead[0][:, P:C])
-        scalar_scatter(dc[0], list2, 0, P, lead[0][:, 0:P])
+        nc.vector.tensor_copy(dc[0][:].indirect(entries(list2, P, T)), whole[:, P:T])
+        scalar_scatter(dc[0], list2, 0, P, whole[:, 0:P])
         make_factor(2)
         make_factor(3)
         for t in (1, 2):
@@ -248,7 +252,7 @@ def tile_moe_seb_relu2_kernel(
                 gather(t, run, lo, hi)
         picked = {}
         for t in (0, 3):
-            picked[t] = sb.tile([P, HALF], F32, name="picked_%d" % t, tag="lead_0" if t == 3 else "picked_0")
+            picked[t] = sb.tile([P, HALF], F32, name="picked_%d" % t, tag="whole" if t == 3 else "picked_0")
             nc.scalar.activation(picked[t][:], dc[t][:].indirect(entries(list1, HALF, T)), COPY)
         gather(3, 0, 0, P)
         gather(3, 1, P, HALF)
@@ -261,11 +265,10 @@ def tile_moe_seb_relu2_kernel(
         nc.vector.tensor_tensor(da[2][:, 3, :], picked[3][:], factor[3][:, HALF:T], MULT)
         sums = copy_out(first_layer(0, (1,), 0), "s0_1")
         scalar_scatter(dx[1], list1, 0, P, sums[:])
-        sums = copy_out(first_layer(0, (2, 3), 1), "s0_23")
-        for kb in (2, 3):
-            scalar_scatter(dx[kb], list1, 0, P, sums[:, (kb - 2) * P : (kb - 1) * P])
+        sums = copy_out(first_layer(0, (0, 2, 3), 1), "s0_023")
+        for x, kb in enumerate((0, 2, 3)):
+            scalar_scatter(dx[kb], list1, 0, P, sums[:, x * P : (x + 1) * P])
         quantise(1)
-        first_own = first_layer(0, (0,), 2)
         sums = copy_out(first_layer(1, (1, 2), 3), "s1_12")
         for kb in (1, 2):
             scalar_scatter(dx[kb], list1, P, HALF, sums[:, (kb - 1) * C : kb * C])
@@ -273,11 +276,10 @@ def tile_moe_seb_relu2_kernel(
         sums = copy_out(first_layer(1, (3,), 4), "s1_3")
         scalar_scatter(dx[3], list1, P, HALF, sums[:])
         quantise(2)
-        nc.vector.tensor_copy(own[:, 0:P], first_own)
-        nc.vector.tensor_copy(own[:, P:HALF], first_layer(1, (0,), 5))
-        nc.vector.tensor_copy(own[:, HALF:T], first_layer(2, (0,), 1))
+        nc.vector.tensor_copy(own[:, 0:C], first_layer(1, (0,), 5))
+        nc.vector.tensor_copy(own[:, C : T - P], first_layer(2, (0,), 1))
         tails = {kb: copy_out(first_layer(2, (kb,), number), "s2_%d" % kb) for kb, number in ((2, 6), (3, 7), (1, 0))}
-        nc.vector.tensor_copy(dx[0][:].indirect(list1[:]), own[:])
+        nc.vector.tensor_copy(dx[0][:].indirect(entries(list1, P, T)), own[:])
         store(0)
         scalar_scatter(dx[2], list1, HALF, T, tails[2][:])
         store(2)

@@ -177,11 +177,13 @@ def tile_moe_seb_relu2_kernel(
                 scalar_scatter(dc[t], list2, e * C, (e + 1) * C, rest[t][:, (e - 1) * C : e * C])
         gated(later[0], g2[:, C:T], whole[:, C:T])
 
-        factor = [sb.tile([P, T], F32, name="factor_%d" % t) for t in range(PACK)]
+        factor_first = sb.tile([P, T], F32, name="factor_first")
+        factor_rest = sb.tile([P, PACK - 1, T], F32, name="factor_rest")
+        factor = [factor_first[:]] + [factor_rest[:, t, :] for t in range(PACK - 1)]
         da = [sb.tile([P, PACK, hi - lo], F32, name="da_%d" % lo) for lo, hi in RUNS]
 
         def make_factor(t):
-            nc.vector.scalar_tensor_tensor(factor[t][:], a_first[:] if t == 0 else a_rest[:, t - 1, :], 0.0, g1[:], MAX, MULT)
+            nc.vector.scalar_tensor_tensor(factor[t], a_first[:] if t == 0 else a_rest[:, t - 1, :], 0.0, g1[:], MAX, MULT)
 
         def gather(t, run, lo, hi):
             first = RUNS[run][0]
@@ -194,11 +196,12 @@ def tile_moe_seb_relu2_kernel(
         def weave(run, on_scalar, tag):
             lo, hi = RUNS[run]
             h = sb.tile([P, hi - lo, PACK], BF16, name="h_%d" % run, tag=tag, align_bytes=64)
-            source = da[run][:].rearrange("p t j -> p j t")
+            source = da[run][:].rearrange("p t (c i) -> p c t i", i=PACK)
+            target = h[:].rearrange("p (c i) t -> p c t i", i=PACK)
             if on_scalar:
-                nc.scalar.activation(h[:], source, COPY, scale=2.0)
+                nc.scalar.activation(target, source, COPY, scale=2.0)
             else:
-                nc.vector.tensor_scalar(h[:], source, 2.0, None, MULT)
+                nc.vector.tensor_scalar(target, source, 2.0, None, MULT)
             woven[run] = h
 
         quantised = {}
@@ -245,8 +248,9 @@ def tile_moe_seb_relu2_kernel(
         dc[0] = sb.tile([P, WINDOW], F32, name="dc_0", tag="dc_0")
         nc.vector.tensor_copy(dc[0][:].indirect(entries(list2, P, T)), whole[:, P:T])
         scalar_scatter(dc[0], list2, 0, P, whole[:, 0:P])
-        make_factor(2)
-        make_factor(3)
+        nc.vector.scalar_tensor_tensor(
+            factor_rest[:, 1:, :], a_rest[:, 1:, :], 0.0, g1[:].unsqueeze(1).to_broadcast([P, 2, T]), MAX, MULT
+        )
         for t in (1, 2):
             for run, (lo, hi) in enumerate(RUNS):
                 gather(t, run, lo, hi)

@@ -145,14 +145,14 @@ def tile_moe_seb_relu2_kernel(
             return acc[:, 0 : (e1 - e0) * C]
 
         def gated(acc, gate, into):
-            nc.vector.tensor_tensor(into, acc, gate, MULT)
+            nc.vector.scalar_tensor_tensor(into, acc, 2.0, gate, MULT, MULT)
 
         def scalar_scatter(window, lst, lo, hi, values):
             nc.scalar.activation(window[:].indirect(entries(lst, lo, hi)), values, COPY)
 
         lead = {t: sb.tile([P, C], F32, name="lead_%d" % t) for t in range(1, PACK)}
-        rest = {t: sb.tile([P, 2 * C], F32, name="rest_%d" % t) for t in range(1, PACK)}
-        whole = sb.tile([P, T], F32, name="whole", tag="whole")
+        rest = {t: sb.tile([P, 2 * C], F32, name="rest_%d" % t, tag="rest_%d" % t) for t in range(1, PACK)}
+        whole = sb.tile([P, T], F32, name="whole")
 
         for e in range(2):
             gather_words(e, sb.tile([P, C], U32, name="words_%d" % e, align_bytes=64))
@@ -177,18 +177,16 @@ def tile_moe_seb_relu2_kernel(
                 scalar_scatter(dc[t], list2, e * C, (e + 1) * C, rest[t][:, (e - 1) * C : e * C])
         gated(later[0], g2[:, C:T], whole[:, C:T])
 
-        factor_first = sb.tile([P, T], F32, name="factor_first")
-        factor_rest = sb.tile([P, PACK - 1, T], F32, name="factor_rest")
-        factor = [factor_first[:]] + [factor_rest[:, t, :] for t in range(PACK - 1)]
-        da = [sb.tile([P, PACK, hi - lo], F32, name="da_%d" % lo) for lo, hi in RUNS]
+        factor = sb.tile([P, PACK, T], F32, name="factor")
+        da = [sb.tile([P, PACK, hi - lo], F32, name="da_%d" % lo) for lo, hi in RUNS[:2]]
 
         def make_factor(t):
-            nc.vector.scalar_tensor_tensor(factor[t], a_first[:] if t == 0 else a_rest[:, t - 1, :], 0.0, g1[:], MAX, MULT)
+            nc.vector.scalar_tensor_tensor(factor[:, t, :], a_first[:] if t == 0 else a_rest[:, t - 1, :], 0.0, g1[:], MAX, MULT)
 
         def gather(t, run, lo, hi):
             first = RUNS[run][0]
             nc.vector.tensor_tensor(
-                da[run][:, t, lo - first : hi - first], dc[t][:].indirect(entries(list1, lo, hi)), factor[t][:, lo:hi], MULT
+                da[run][:, t, lo - first : hi - first], dc[t][:].indirect(entries(list1, lo, hi)), factor[:, t, lo:hi], MULT
             )
 
         woven = {}
@@ -199,9 +197,9 @@ def tile_moe_seb_relu2_kernel(
             source = da[run][:].rearrange("p t (c i) -> p c t i", i=PACK)
             target = h[:].rearrange("p (c i) t -> p c t i", i=PACK)
             if on_scalar:
-                nc.scalar.activation(target, source, COPY, scale=2.0)
+                nc.scalar.activation(target, source, COPY)
             else:
-                nc.vector.tensor_scalar(target, source, 2.0, None, MULT)
+                nc.vector.tensor_copy(target, source)
             woven[run] = h
 
         quantised = {}
@@ -246,27 +244,24 @@ def tile_moe_seb_relu2_kernel(
         make_factor(0)
         make_factor(1)
         dc[0] = sb.tile([P, WINDOW], F32, name="dc_0", tag="dc_0")
-        nc.vector.tensor_copy(dc[0][:].indirect(entries(list2, P, T)), whole[:, P:T])
-        scalar_scatter(dc[0], list2, 0, P, whole[:, 0:P])
+        nc.vector.tensor_copy(dc[0][:].indirect(list2[:]), whole[:])
         nc.vector.scalar_tensor_tensor(
-            factor_rest[:, 1:, :], a_rest[:, 1:, :], 0.0, g1[:].unsqueeze(1).to_broadcast([P, 2, T]), MAX, MULT
+            factor[:, 2:, :], a_rest[:, 1:, :], 0.0, g1[:].unsqueeze(1).to_broadcast([P, 2, T]), MAX, MULT
         )
-        for t in (1, 2):
-            for run, (lo, hi) in enumerate(RUNS):
-                gather(t, run, lo, hi)
-        picked = {}
-        for t in (0, 3):
-            picked[t] = sb.tile([P, HALF], F32, name="picked_%d" % t, tag="whole" if t == 3 else "picked_0")
-            nc.scalar.activation(picked[t][:], dc[t][:].indirect(entries(list1, HALF, T)), COPY)
-        gather(3, 0, 0, P)
-        gather(3, 1, P, HALF)
-        gather(0, 0, 0, P)
-        gather(0, 1, P, HALF)
+        for t in (1, 2, 0):
+            for run in range(2):
+                gather(t, run, *RUNS[run])
+        picked = sb.tile([P, PACK, HALF], F32, name="picked", tag="rest_3")
+        for t in (0, 2, 3):
+            nc.scalar.activation(picked[:, t, :], dc[t][:].indirect(entries(list1, HALF, T)), COPY)
+        for run in range(2):
+            gather(3, run, *RUNS[run])
         weave(0, False, "h_0")
         weave(1, True, "h_1")
-        nc.vector.tensor_tensor(da[2][:, 0, :], picked[0][:], factor[0][:, HALF:T], MULT)
+        middle = HALF + HALF // 2
+        nc.vector.tensor_copy(picked[:, 1, 0 : HALF // 2], dc[1][:].indirect(entries(list1, HALF, middle)))
         quantise(0)
-        nc.vector.tensor_tensor(da[2][:, 3, :], picked[3][:], factor[3][:, HALF:T], MULT)
+        nc.vector.tensor_copy(picked[:, 1, HALF // 2 : HALF], dc[1][:].indirect(entries(list1, middle, T)))
         sums = copy_out(first_layer(0, (1,), 0), "s0_1")
         scalar_scatter(dx[1], list1, 0, P, sums[:])
         sums = copy_out(first_layer(0, (0, 2, 3), 1), "s0_023")
@@ -276,13 +271,21 @@ def tile_moe_seb_relu2_kernel(
         sums = copy_out(first_layer(1, (1, 2), 3), "s1_12")
         for kb in (1, 2):
             scalar_scatter(dx[kb], list1, P, HALF, sums[:, (kb - 1) * C : kb * C])
-        weave(2, False, "codes_0")
+        woven[2] = sb.tile([P, HALF, PACK], BF16, name="h_2", tag="codes_0", align_bytes=64)
+        nc.vector.tensor_tensor(
+            woven[2][:].rearrange("p (c i) t -> p c t i", i=PACK),
+            picked[:].rearrange("p t (c i) -> p c t i", i=PACK),
+            factor[:, :, HALF:T].rearrange("p t (c i) -> p c t i", i=PACK),
+            MULT,
+        )
         sums = copy_out(first_layer(1, (3,), 4), "s1_3")
         scalar_scatter(dx[3], list1, P, HALF, sums[:])
         quantise(2)
         nc.vector.tensor_copy(own[:, 0:C], first_layer(1, (0,), 5))
         nc.vector.tensor_copy(own[:, C : T - P], first_layer(2, (0,), 1))
-        tails = {kb: copy_out(first_layer(2, (kb,), number), "s2_%d" % kb) for kb, number in ((2, 6), (3, 7), (1, 0))}
+        tails = {kb: copy_out(first_layer(2, (kb,), number), "s2_%d" % kb) for kb, number in ((2, 6), (1, 0))}
+        tails[3] = sb.tile([P, HALF], F32, name="s2_3")
+        nc.scalar.activation(tails[3][:], first_layer(2, (3,), 7), COPY)
         nc.vector.tensor_copy(dx[0][:].indirect(entries(list1, P, T)), own[:])
         store(0)
         scalar_scatter(dx[2], list1, HALF, T, tails[2][:])

@@ -191,15 +191,12 @@ def tile_moe_seb_relu2_kernel(
 
         woven = {}
 
-        def weave(run, on_scalar, tag):
+        def weave(run):
             lo, hi = RUNS[run]
-            h = sb.tile([P, hi - lo, PACK], BF16, name="h_%d" % run, tag=tag, align_bytes=64)
-            source = da[run][:].rearrange("p t (c i) -> p c t i", i=PACK)
-            target = h[:].rearrange("p (c i) t -> p c t i", i=PACK)
-            if on_scalar:
-                nc.scalar.activation(target, source, COPY)
-            else:
-                nc.vector.tensor_copy(target, source)
+            h = sb.tile([P, hi - lo, PACK], BF16, name="h_%d" % run, align_bytes=64)
+            nc.vector.tensor_copy(
+                h[:].rearrange("p (c i) t -> p c t i", i=PACK), da[run][:].rearrange("p t (c i) -> p c t i", i=PACK)
+            )
             woven[run] = h
 
         quantised = {}
@@ -252,22 +249,19 @@ def tile_moe_seb_relu2_kernel(
             for run in range(2):
                 gather(t, run, *RUNS[run])
         picked = sb.tile([P, PACK, HALF], F32, name="picked", tag="rest_3")
-        for t in (0, 2, 3):
+        for t in (1, 2, 0, 3):
             nc.scalar.activation(picked[:, t, :], dc[t][:].indirect(entries(list1, HALF, T)), COPY)
         for run in range(2):
             gather(3, run, *RUNS[run])
-        weave(0, False, "h_0")
-        weave(1, True, "h_1")
-        middle = HALF + HALF // 2
-        nc.vector.tensor_copy(picked[:, 1, 0 : HALF // 2], dc[1][:].indirect(entries(list1, HALF, middle)))
-        quantise(0)
-        nc.vector.tensor_copy(picked[:, 1, HALF // 2 : HALF], dc[1][:].indirect(entries(list1, middle, T)))
+        for run in range(2):
+            weave(run)
+        for run in range(2):
+            quantise(run)
         sums = copy_out(first_layer(0, (1,), 0), "s0_1")
         scalar_scatter(dx[1], list1, 0, P, sums[:])
         sums = copy_out(first_layer(0, (0, 2, 3), 1), "s0_023")
         for x, kb in enumerate((0, 2, 3)):
             scalar_scatter(dx[kb], list1, 0, P, sums[:, x * P : (x + 1) * P])
-        quantise(1)
         sums = copy_out(first_layer(1, (1, 2), 3), "s1_12")
         for kb in (1, 2):
             scalar_scatter(dx[kb], list1, P, HALF, sums[:, (kb - 1) * C : kb * C])
@@ -283,9 +277,7 @@ def tile_moe_seb_relu2_kernel(
         quantise(2)
         nc.vector.tensor_copy(own[:, 0:C], first_layer(1, (0,), 5))
         nc.vector.tensor_copy(own[:, C : T - P], first_layer(2, (0,), 1))
-        tails = {kb: copy_out(first_layer(2, (kb,), number), "s2_%d" % kb) for kb, number in ((2, 6), (1, 0))}
-        tails[3] = sb.tile([P, HALF], F32, name="s2_3")
-        nc.scalar.activation(tails[3][:], first_layer(2, (3,), 7), COPY)
+        tails = {kb: copy_out(first_layer(2, (kb,), number), "s2_%d" % kb) for kb, number in ((2, 6), (3, 7), (1, 0))}
         nc.vector.tensor_copy(dx[0][:].indirect(entries(list1, P, T)), own[:])
         store(0)
         scalar_scatter(dx[2], list1, HALF, T, tails[2][:])

@@ -25,6 +25,7 @@ HALF = T // 2
 WINDOW = 1024
 FLOPS = 2 * 2 * W * W * T
 
+SPLIT = 352
 RUNS = ((0, P), (P, HALF), (HALF, T))
 
 
@@ -86,7 +87,7 @@ def tile_moe_seb_relu2_kernel(
         a_rows = a.rearrange("(p t) j -> p t j", t=PACK)
         a_first = sb.tile([P, T], F32, name="a_first", tag="dc_0")
         nc.sync.dma_start(a_first[:], a_rows[:, 0, :])
-        a_rest = sb.tile([P, PACK - 1, T], F32, name="a_rest")
+        a_rest = sb.tile([P, PACK - 1, T], F32, name="a_rest", tag="a_rest")
         nc.sync.dma_start(a_rest[:], a_rows[:, 1:PACK, :])
         g1 = sb.tile([P, T], F32, name="g1")
         nc.sync.dma_start(g1[:], gate1)
@@ -177,11 +178,8 @@ def tile_moe_seb_relu2_kernel(
                 scalar_scatter(dc[t], list2, e * C, (e + 1) * C, rest[t][:, (e - 1) * C : e * C])
         gated(later[0], g2[:, C:T], whole[:, C:T])
 
-        factor = sb.tile([P, PACK, T], F32, name="factor")
+        factor = sb.tile([P, PACK, HALF], F32, name="factor")
         da = [sb.tile([P, PACK, hi - lo], F32, name="da_%d" % lo) for lo, hi in RUNS[:2]]
-
-        def make_factor(t):
-            nc.vector.scalar_tensor_tensor(factor[:, t, :], a_first[:] if t == 0 else a_rest[:, t - 1, :], 0.0, g1[:], MAX, MULT)
 
         def gather(t, run, lo, hi):
             first = RUNS[run][0]
@@ -228,7 +226,6 @@ def tile_moe_seb_relu2_kernel(
             return acc[:, 0 : len(row_tiles) * width]
 
         dx = [sb.tile([P, WINDOW], F32, name="dx_%d" % kb) for kb in range(PACK)]
-        own = sb.tile([P, T - P], F32, name="own")
 
         def store(kb):
             nc.sync.dma_start(out[kb * P : (kb + 1) * P, :], dx[kb][:, 0:T])
@@ -238,51 +235,60 @@ def tile_moe_seb_relu2_kernel(
             nc.vector.tensor_copy(sums[:], acc)
             return sums
 
-        make_factor(0)
-        make_factor(1)
+        slope = sb.tile([P, PACK, HALF], F32, name="slope")
+        nc.vector.tensor_scalar(slope[:, 0, :], a_first[:, HALF:T], 0.0, None, MAX)
+        nc.vector.tensor_scalar(slope[:, 1, :], a_rest[:, 0, HALF:T], 0.0, None, MAX)
+        nc.vector.tensor_scalar(slope[:, 2:, :], a_rest[:, 1:, HALF:T], 0.0, None, MAX)
+        nc.vector.scalar_tensor_tensor(factor[:, 0, :], a_first[:, 0:HALF], 0.0, g1[:, 0:HALF], MAX, MULT)
+        nc.vector.scalar_tensor_tensor(
+            factor[:, 1:, :], a_rest[:, :, 0:HALF], 0.0, g1[:, 0:HALF].unsqueeze(1).to_broadcast([P, PACK - 1, HALF]), MAX, MULT
+        )
+        factor_late = sb.tile([P, PACK, HALF], F32, name="factor_late", tag="a_rest")
+        for t in range(PACK):
+            nc.gpsimd.tensor_tensor(factor_late[:, t, :], slope[:, t, :], g1[:, HALF:T], MULT)
         dc[0] = sb.tile([P, WINDOW], F32, name="dc_0", tag="dc_0")
         nc.vector.tensor_copy(dc[0][:].indirect(list2[:]), whole[:])
-        nc.vector.scalar_tensor_tensor(
-            factor[:, 2:, :], a_rest[:, 1:, :], 0.0, g1[:].unsqueeze(1).to_broadcast([P, 2, T]), MAX, MULT
-        )
         for t in (1, 2, 0):
             for run in range(2):
                 gather(t, run, *RUNS[run])
         picked = sb.tile([P, PACK, HALF], F32, name="picked", tag="rest_3")
-        for t in (1, 2, 0, 3):
-            nc.scalar.activation(picked[:, t, :], dc[t][:].indirect(entries(list1, HALF, T)), COPY)
+        for t, lo in ((1, HALF + P), (2, HALF), (0, HALF), (3, HALF)):
+            nc.scalar.activation(picked[:, t, lo - HALF :], dc[t][:].indirect(entries(list1, lo, T)), COPY)
         for run in range(2):
             gather(3, run, *RUNS[run])
         for run in range(2):
             weave(run)
         for run in range(2):
             quantise(run)
+        nc.vector.tensor_copy(picked[:, 1, 0:P], dc[1][:].indirect(entries(list1, HALF, HALF + P)))
         sums = copy_out(first_layer(0, (1,), 0), "s0_1")
         scalar_scatter(dx[1], list1, 0, P, sums[:])
         sums = copy_out(first_layer(0, (0, 2, 3), 1), "s0_023")
         for x, kb in enumerate((0, 2, 3)):
             scalar_scatter(dx[kb], list1, 0, P, sums[:, x * P : (x + 1) * P])
-        sums = copy_out(first_layer(1, (1, 2), 3), "s1_12")
-        for kb in (1, 2):
-            scalar_scatter(dx[kb], list1, P, HALF, sums[:, (kb - 1) * C : kb * C])
+        sums = copy_out(first_layer(1, (2, 3), 3), "s1_23")
+        for kb in (2, 3):
+            scalar_scatter(dx[kb], list1, P, HALF, sums[:, (kb - 2) * C : (kb - 1) * C])
         woven[2] = sb.tile([P, HALF, PACK], BF16, name="h_2", tag="codes_0", align_bytes=64)
         nc.vector.tensor_tensor(
             woven[2][:].rearrange("p (c i) t -> p c t i", i=PACK),
             picked[:].rearrange("p t (c i) -> p c t i", i=PACK),
-            factor[:, :, HALF:T].rearrange("p t (c i) -> p c t i", i=PACK),
+            factor_late[:].rearrange("p t (c i) -> p c t i", i=PACK),
             MULT,
         )
-        sums = copy_out(first_layer(1, (3,), 4), "s1_3")
-        scalar_scatter(dx[3], list1, P, HALF, sums[:])
+        shared = sb.tile([P, T - P], F32, name="shared")
+        nc.vector.tensor_copy(shared[:, 0:C], first_layer(1, (1,), 4))
+        scalar_scatter(dx[1], list1, P, SPLIT, shared[:, 0 : SPLIT - P])
+        middle = copy_out(first_layer(1, (0,), 5), "s1_0")
         quantise(2)
-        nc.vector.tensor_copy(own[:, 0:C], first_layer(1, (0,), 5))
-        nc.vector.tensor_copy(own[:, C : T - P], first_layer(2, (0,), 1))
-        tails = {kb: copy_out(first_layer(2, (kb,), number), "s2_%d" % kb) for kb, number in ((2, 6), (3, 7), (1, 0))}
-        nc.vector.tensor_copy(dx[0][:].indirect(entries(list1, P, T)), own[:])
+        nc.vector.tensor_copy(dx[0][:].indirect(entries(list1, P, HALF)), middle[:])
+        tails = {kb: copy_out(first_layer(2, (kb,), number), "s2_%d" % kb) for kb, number in ((0, 1), (2, 6), (3, 7))}
+        nc.vector.tensor_copy(shared[:, C : T - P], first_layer(2, (1,), 0))
+        nc.vector.tensor_copy(dx[0][:].indirect(entries(list1, HALF, T)), tails[0][:])
         store(0)
         scalar_scatter(dx[2], list1, HALF, T, tails[2][:])
         store(2)
-        nc.vector.tensor_copy(dx[1][:].indirect(entries(list1, HALF, T)), tails[1][:])
+        nc.vector.tensor_copy(dx[1][:].indirect(entries(list1, SPLIT, T)), shared[:, SPLIT - P : T - P])
         store(1)
         scalar_scatter(dx[3], list1, HALF, T, tails[3][:])
         store(3)

@@ -21,12 +21,10 @@ E = 3
 C = 256
 W = 512
 QUADRANTS = 4
-HALF = T // 2
 WINDOW = 1024
+HALF = T // 2
 FLOPS = 2 * 2 * W * W * T
-
-SPLIT = 352
-RUNS = ((0, P), (P, HALF), (HALF, T))
+DY_ROW = 4
 
 
 def cut(lo, hi, marks):
@@ -49,246 +47,274 @@ def tile_moe_seb_relu2_kernel(
         def entries(lst, lo, hi):
             return lst[:, lo // 16 : hi // 16]
 
-        def load_scale_rows(engine, plane, rows, q):
-            engine.dma_start(
-                plane[:].bitcast(I32)[32 * q : 32 * q + 4, :, :],
-                rows[:, 0, 4 * q : 4 * q + 4, :].rearrange("e r i -> r e i").bitcast(I32),
-            )
-
         dy_plane = sb.tile([P, T], U8, name="dy_plane", align_bytes=64)
-        w2_plane = sb.tile([P, W], U8, name="w2_plane", align_bytes=64)
-        w2_plane_last = sb.tile([P, W], U8, name="w2_plane_last", align_bytes=64)
+        w2_plane = held.tile([P, QUADRANTS, W], U8, name="w2_plane", offset=4 * W, align_bytes=64)
+        w2_plane_rest = sb.tile([P, W], U8, name="w2_plane_rest", align_bytes=64)
         w1_plane = sb.tile([P, E, W], U8, name="w1_plane", align_bytes=64)
-        nc.gpsimd.memset(dy_plane[:].bitcast(I32), 0)
-        nc.vector.memset(w2_plane[:].bitcast(I32), 0)
-        nc.vector.memset(w2_plane_last[:].bitcast(I32), 0)
+        nc.gpsimd.memset(w2_plane[:].bitcast(I32)[:, 0, :], 0)
+        nc.vector.memset(dy_plane[:].bitcast(I32), 0)
+        nc.vector.memset(w2_plane_rest[:].bitcast(I32), 0)
         nc.vector.memset(w1_plane[:].bitcast(I32), 0)
 
         list2 = sb.tile([P, T // 16], U16, name="list2")
         nc.sync.dma_start(list2[:], offs2)
-        for q in range(QUADRANTS):
-            queue = nc.scalar if q < QUADRANTS // 2 else nc.sync
-            queue.dma_start(dy_plane[:].bitcast(I32)[32 * q : 32 * q + 4, :], dy_scales[0, 4 * q : 4 * q + 4, :].bitcast(I32))
-        dy_tile = sb.tile([P, T], I32, name="dy_tile", align_bytes=64)
-        nc.sync.dma_start(dy_tile[:], dy_words[0].rearrange("p t d -> p (t d)").bitcast(I32))
         w2_first = sb.tile([P, W], I32, name="w2_first", align_bytes=64)
-        nc.sync.dma_start(w2_first[:], w2t_words[0, 0].rearrange("p i d -> p (i d)").bitcast(I32))
+        dy_tile = sb.tile([P, T], I32, name="dy_tile", align_bytes=64)
+
+        def load_dy_rows(queue, q):
+            row0 = 32 * q + DY_ROW
+            queue.dma_start(dy_plane[:].bitcast(I32)[row0 : row0 + 4, :], dy_scales[0, 4 * q : 4 * q + 4, :].bitcast(I32))
+
+        nc.sync.dma_start(w2_plane[:].bitcast(I32)[0:4, :, :], w2t_scales[0, 0].rearrange("(q r) c -> r q c", r=4).bitcast(I32))
         for q in range(QUADRANTS):
-            queue = nc.scalar if q == 0 else nc.sync
-            queue.dma_start(w2_plane[:].bitcast(I32)[32 * q : 32 * q + 8, :], w2t_scales[0:2, 0, 4 * q : 4 * q + 4, :].bitcast(I32))
+            load_dy_rows(nc.scalar if q < 2 else nc.sync, q)
+        nc.sync.dma_start(dy_tile[:], dy_words[0].rearrange("p t d -> p (t d)").bitcast(I32))
+        nc.sync.dma_start(w2_first[:], w2t_words[0, 0].rearrange("p i d -> p (i d)").bitcast(I32))
+        g2_first = sb.tile([P, C], F32, name="g2_first")
+        nc.sync.dma_start(g2_first[:], gate2[:, 0:C])
         w2_rest = sb.tile([P, E - 1, W], I32, name="w2_rest", align_bytes=64)
         nc.sync.dma_start(w2_rest[:], w2t_words[1:E, 0].rearrange("e p i d -> p e (i d)").bitcast(I32))
-        g2_first = held.tile([P, C], F32, name="g2_first", offset=0, align_bytes=64)
-        nc.sync.dma_start(g2_first[:], gate2[:, 0:C])
         for q in range(QUADRANTS):
-            nc.sync.dma_start(w2_plane_last[:].bitcast(I32)[32 * q : 32 * q + 4, :], w2t_scales[2, 0, 4 * q : 4 * q + 4, :].bitcast(I32))
-        g2 = sb.tile([P, T], F32, name="g2")
-        nc.sync.dma_start(g2[:], gate2)
+            nc.sync.dma_start(
+                w2_plane_rest[:].bitcast(I32)[32 * q + 4 : 32 * q + 12, :], w2t_scales[1:E, 0, 4 * q : 4 * q + 4, :].bitcast(I32)
+            )
+        g2_rest = sb.tile([P, 2 * C], F32, name="g2_rest")
+        nc.sync.dma_start(g2_rest[:], gate2[:, C:T])
         a_rows = a.rearrange("(p t) j -> p t j", t=PACK)
-        a_first = sb.tile([P, T], F32, name="a_first", tag="dc_0")
-        nc.sync.dma_start(a_first[:], a_rows[:, 0, :])
-        a_rest = sb.tile([P, PACK - 1, T], F32, name="a_rest", tag="a_rest")
-        nc.sync.dma_start(a_rest[:], a_rows[:, 1:PACK, :])
+        a_late = sb.tile([P, PACK, HALF], F32, name="a_late")
+        nc.sync.dma_start(a_late[:], a_rows[:, :, HALF:T])
         g1 = sb.tile([P, T], F32, name="g1")
         nc.sync.dma_start(g1[:], gate1)
-        list1 = sb.tile([P, T // 16], U16, name="list1")
-        nc.sync.dma_start(list1[:], offs)
+        a_early = sb.tile([P, PACK, HALF], F32, name="a_early")
+        nc.sync.dma_start(a_early[:], a_rows[:, :, 0:HALF])
         for q in range(QUADRANTS):
-            load_scale_rows(nc.sync, w1_plane, w1t_scales, q)
+            nc.sync.dma_start(
+                w1_plane[:].bitcast(I32)[32 * q : 32 * q + 4, :, :],
+                w1t_scales[:, 0, 4 * q : 4 * q + 4, :].rearrange("e r i -> r e i").bitcast(I32),
+            )
         w1 = sb.tile([P, E, 2 * W], U8, name="w1", align_bytes=64)
         nc.sync.dma_start(w1[:].bitcast(I32), w1t_words[:, 0].rearrange("e p b -> p e b").bitcast(I32))
+        list1 = sb.tile([P, T // 16], U16, name="list1")
+        nc.sync.dma_start(list1[:], offs)
 
-        w2 = []
-        w2_scale = []
-
-        def sort_words(e, source):
-            ordered = sb.tile([P, W], U32, name="w2_%d" % e, align_bytes=64)
-            nc.scalar.copy(
-                ordered[:].rearrange("p (t m) -> p m t", t=PACK),
-                source.bitcast(U32).rearrange("p (m t) -> p m t", t=PACK),
-            )
-            w2.append(ordered)
-
-        def sort_scales(plane, ordered):
+        def sort_scales(plane, name):
+            ordered = sb.tile([P, W], U8, name=name, align_bytes=64)
             nc.vector.tensor_copy(
-                ordered[:].rearrange("p (t m) -> p t m", t=PACK),
-                plane[:].rearrange("p (m t) -> p t m", t=PACK),
+                ordered[:].rearrange("p (t m) -> p t m", t=PACK), plane.rearrange("p (m t) -> p t m", t=PACK)
             )
             return ordered
 
-        sort_words(0, w2_first[:])
-        for e in range(1, E):
-            sort_words(e, w2_rest[:, e - 1, :])
+        def gather_bytes(picked, lo, hi):
+            nc.vector.tensor_copy(picked, dy_plane[:].indirect(entries(list2, lo, hi)))
 
-        scales_head = sb.tile([P, 2 * C], U8, name="scales_head", align_bytes=64)
-        nc.vector.tensor_copy(scales_head[:], dy_plane[:].indirect(entries(list2, 0, 2 * C)))
-        words = {}
+        def gather_words(picked, lo, hi):
+            nc.vector.tensor_copy(picked, dy_tile[:].bitcast(U32).indirect(entries(list2, lo, hi)))
 
-        def gather_words(e, picked):
-            words[e] = picked
-            nc.vector.tensor_copy(picked[:], dy_tile[:].bitcast(U32).indirect(entries(list2, e * C, (e + 1) * C)))
+        def second_layer(acc, weights, weight_scales, t, words, scales):
+            nc.tensor.matmul_mx(
+                out=acc,
+                lhsT=weights[:, t * P : (t + 1) * P].bitcast(FP8X4),
+                lhsT_scale=weight_scales[:, t * P : (t + 1) * P],
+                rhs=words.bitcast(FP8X4),
+                rhs_scale=scales,
+                start=True,
+                stop=True,
+            )
 
-        scales = {0: scales_head[:, 0:C], 1: scales_head[:, C : 2 * C]}
-        dc = {t: sb.tile([P, WINDOW], F32, name="dc_%d" % t) for t in range(1, PACK)}
-
-        def second_layer(t, e0, e1, number):
-            acc = bank(number)
-            for e in range(e0, e1):
-                nc.tensor.matmul_mx(
-                    out=acc[:, (e - e0) * C : (e - e0 + 1) * C],
-                    lhsT=w2[e][:, t * P : (t + 1) * P].bitcast(FP8X4),
-                    lhsT_scale=w2_scale[e][:, t * P : (t + 1) * P],
-                    rhs=words[e][:].bitcast(FP8X4),
-                    rhs_scale=scales[e],
-                    start=True,
-                    stop=True,
-                )
-            return acc[:, 0 : (e1 - e0) * C]
-
-        def gated(acc, gate, into):
+        def gated(into, acc, gate):
             nc.vector.scalar_tensor_tensor(into, acc, 2.0, gate, MULT, MULT)
 
         def scalar_scatter(window, lst, lo, hi, values):
             nc.scalar.activation(window[:].indirect(entries(lst, lo, hi)), values, COPY)
 
-        lead = {t: sb.tile([P, C], F32, name="lead_%d" % t) for t in range(1, PACK)}
-        rest = {t: sb.tile([P, 2 * C], F32, name="rest_%d" % t, tag="rest_%d" % t) for t in range(1, PACK)}
-        whole = sb.tile([P, T], F32, name="whole")
+        def vector_scatter(window, lst, lo, hi, values):
+            nc.vector.tensor_copy(window[:].indirect(entries(lst, lo, hi)), values)
 
-        for e in range(2):
-            gather_words(e, sb.tile([P, C], U32, name="words_%d" % e, align_bytes=64))
-        both = sort_scales(w2_plane, sb.tile([P, W], U8, name="w2_scale", align_bytes=64))
-        w2_scale.extend((both[:], both[4:P, :]))
-        first = {t: second_layer(t, 0, 1, t) for t in (1, 2, 3, 0)}
-        for t in (1, 2):
-            gated(first[t], g2_first[:], lead[t][:])
-            scalar_scatter(dc[t], list2, 0, C, lead[t][:])
-        gather_words(2, held.tile([P, C], U32, name="words_2", offset=3 * C, align_bytes=64))
-        scales_tail = held.tile([P, C], U8, name="scales_tail", offset=0, align_bytes=64)
-        nc.vector.tensor_copy(scales_tail[:], dy_plane[:].indirect(entries(list2, 2 * C, T)))
-        scales[2] = scales_tail[:]
-        w2_scale.append(sort_scales(w2_plane_last, sb.tile([P, W], U8, name="w2_scale_last", align_bytes=64))[:])
-        gated(first[3], g2[:, 0:C], lead[3][:])
-        gated(first[0], g2[:, 0:C], whole[:, 0:C])
-        scalar_scatter(dc[3], list2, 0, C, lead[3][:])
-        later = {t: second_layer(t, 1, 3, number) for t, number in ((1, 4), (2, 5), (3, 6), (0, 7))}
-        for t in (1, 2, 3):
-            gated(later[t], g2[:, C:T], rest[t][:])
-            for e in (1, 2):
-                scalar_scatter(dc[t], list2, e * C, (e + 1) * C, rest[t][:, (e - 1) * C : e * C])
-        gated(later[0], g2[:, C:T], whole[:, C:T])
+        by_plane = w2_first[:].bitcast(U32).rearrange("p (m t) -> p m t", t=PACK)
+        w2_lead = sb.tile([P, P], U32, name="w2_lead", align_bytes=64)
+        nc.scalar.copy(w2_lead[:], by_plane[:, :, 0])
+        w2_head = held.tile([P, W], U32, name="w2_head", offset=0, align_bytes=64)
+        nc.scalar.copy(w2_head[:].rearrange("p (t m) -> p m t", t=PACK)[:, :, 1:], by_plane[:, :, 1:])
+        for q in range(1, QUADRANTS):
+            nc.vector.tensor_copy(w2_plane[:].bitcast(I32)[32 * q : 32 * q + 4, 0, :], w2_plane[:].bitcast(I32)[0:4, q, :])
+        scales_a = sb.tile([P, P], U8, name="scales_a", align_bytes=64)
+        gather_bytes(scales_a[:], 0, P)
+        w2_scale_head = sort_scales(w2_plane[:, 0, :], "w2_scale_head")
+        words_a = held.tile([P, P], U32, name="words_a", offset=8 * W, align_bytes=64)
+        gather_words(words_a[:], 0, P)
+        scales_b = held.tile([P, P], U8, name="scales_b", offset=4 * W, align_bytes=64)
+        gather_bytes(scales_b[:], P, C)
+        words_b = held.tile([P, P], U32, name="words_b", offset=5 * W, align_bytes=64)
+        gather_words(words_b[:], P, C)
 
+        dc = [sb.tile([P, WINDOW], F32, name="dc_%d" % t) for t in range(PACK)]
+        acc_lead, acc_a, acc_b = bank(0), bank(1), bank(2)
+        second_layer(acc_lead[:, 0:P], w2_lead, w2_scale_head, 0, words_a[:], scales_a[DY_ROW:P, :])
+        for t in range(1, PACK):
+            second_layer(acc_a[:, (t - 1) * P : t * P], w2_head, w2_scale_head, t, words_a[:], scales_a[DY_ROW:P, :])
+        for t in range(PACK):
+            second_layer(acc_b[:, t * P : (t + 1) * P], w2_head if t else w2_lead, w2_scale_head, t, words_b[:], scales_b[DY_ROW:P, :])
+        lead = sb.tile([P, P], F32, name="lead")
+        gated(lead[:], acc_lead[:, 0:P], g2_first[:, 0:P])
+        scalar_scatter(dc[0], list2, 0, P, lead[:])
+        block_a = sb.tile([P, PACK - 1, P], F32, name="block_a")
+        gated(
+            block_a[:],
+            acc_a[:, 0 : 3 * P].rearrange("p (t j) -> p t j", t=3),
+            g2_first[:, 0:P].unsqueeze(1).to_broadcast([P, 3, P]),
+        )
+        for t in range(1, PACK):
+            scalar_scatter(dc[t], list2, 0, P, block_a[:, t - 1, :])
+        block_b = sb.tile([P, PACK * P + 2 * C], F32, name="block_b")
+        gated(
+            block_b[:, 0 : PACK * P].rearrange("p (t j) -> p t j", t=PACK),
+            acc_b[:].rearrange("p (t j) -> p t j", t=PACK),
+            g2_first[:, P:C].unsqueeze(1).to_broadcast([P, PACK, P]),
+        )
+        for t in range(PACK - 1):
+            scalar_scatter(dc[t], list2, P, C, block_b[:, t * P : (t + 1) * P])
+
+        scales_rest = held.tile([P, 2 * C], U8, name="scales_rest", offset=5 * W, align_bytes=64)
+        gather_bytes(scales_rest[:], C, T)
+        w2_tail = held.tile([P, E - 1, W], I32, name="w2_tail", offset=8 * W, align_bytes=64)
+        nc.vector.tensor_copy(
+            w2_tail[:].rearrange("p e (t m) -> p e m t", t=PACK), w2_rest[:].rearrange("p e (m t) -> p e m t", t=PACK)
+        )
+        w2_scale_rest = sort_scales(w2_plane_rest[:], "w2_scale_rest")
+        words_rest = {}
+        for e in (1, 2):
+            words_rest[e] = held.tile([P, C], U32, name="words_%d" % e, offset=(e - 1) * 4 * C, align_bytes=64)
+            gather_words(words_rest[e][:], e * C, (e + 1) * C)
+
+        def later_sums(pieces, number):
+            acc = bank(number)
+            for x, (t, e) in enumerate(pieces):
+                second_layer(
+                    acc[:, x * C : (x + 1) * C],
+                    w2_tail[:, e - 1, :],
+                    w2_scale_rest[4 * e : P, :],
+                    t,
+                    words_rest[e][:],
+                    scales_rest[DY_ROW:P, (e - 1) * C : e * C],
+                )
+            return acc
+
+        def one_gate(e):
+            return g2_rest[:, (e - 1) * C : e * C].unsqueeze(1).to_broadcast([P, 2, C])
+
+        both_gates = g2_rest[:].rearrange("p (e j) -> p e j", e=2)
+        for number, pieces, gate in (
+            (3, ((0, 1), (1, 1)), one_gate(1)),
+            (4, ((2, 1), (0, 2)), both_gates),
+            (5, ((3, 1), (3, 2)), both_gates),
+            (6, ((1, 2), (2, 2)), one_gate(2)),
+        ):
+            acc = later_sums(pieces, number)[:].rearrange("p (x j) -> p x j", x=2)
+            if number == 5:
+                gated(block_b[:, PACK * P :].rearrange("p (x j) -> p x j", x=2), acc, gate)
+            else:
+                values = sb.tile([P, 2, C], F32, name="rest_%d" % number, tag="rest_%d" % number)
+                gated(values[:], acc, gate)
+                for x, (t, e) in enumerate(pieces):
+                    scalar_scatter(dc[t], list2, e * C, (e + 1) * C, values[:, x, :])
+        slope = sb.tile([P, PACK, HALF], F32, name="slope")
+        nc.vector.tensor_scalar(slope[:], a_late[:], 0.0, None, MAX)
         factor = sb.tile([P, PACK, HALF], F32, name="factor")
-        da = [sb.tile([P, PACK, hi - lo], F32, name="da_%d" % lo) for lo, hi in RUNS[:2]]
+        for t in range(PACK):
+            nc.gpsimd.tensor_tensor(factor[:, t, :], slope[:, t, :], g1[:, HALF:T], MULT)
+        vector_scatter(dc[3], list2, P, T, block_b[:, 3 * P :])
 
-        def gather(t, run, lo, hi):
-            first = RUNS[run][0]
-            nc.vector.tensor_tensor(
-                da[run][:, t, lo - first : hi - first], dc[t][:].indirect(entries(list1, lo, hi)), factor[:, t, lo:hi], MULT
+        first = sb.tile([P, PACK, P], F32, name="first")
+        middle = sb.tile([P, PACK, C], F32, name="middle")
+
+        def gather(into, t, lo, hi):
+            nc.vector.tensor_tensor(into, dc[t][:].indirect(entries(list1, lo, hi)), g1[:, lo:hi], MULT)
+
+        def weave(h, values, lo, hi):
+            nc.vector.scalar_tensor_tensor(
+                h, a_early[:, :, lo:hi].rearrange("p t j -> p j t"), 0.0, values.rearrange("p t j -> p j t"), MAX, MULT
             )
 
-        woven = {}
+        def quantise(h, name):
+            width = h.shape[1]
+            codes = sb.tile([P, width], U32, name="codes_" + name, tag="codes_" + name, align_bytes=64)
+            plane = sb.tile([P, width], U8, name="plane_" + name, tag="plane_" + name, align_bytes=64)
+            nc.vector.quantize_mx(out=codes[:].bitcast(FP8X4), scales=plane[:], in_=h[:].rearrange("p j t -> p (j t)"))
+            return codes, plane
 
-        def weave(run):
-            lo, hi = RUNS[run]
-            h = sb.tile([P, hi - lo, PACK], BF16, name="h_%d" % run, align_bytes=64)
-            nc.vector.tensor_copy(
-                h[:].rearrange("p (c i) t -> p c t i", i=PACK), da[run][:].rearrange("p t (c i) -> p c t i", i=PACK)
-            )
-            woven[run] = h
-
-        quantised = {}
-
-        def quantise(run):
-            lo, hi = RUNS[run]
-            codes = sb.tile([P, hi - lo], U32, name="codes_%d" % lo, tag="codes_%d" % lo, align_bytes=64)
-            plane = sb.tile([P, hi - lo], U8, name="plane_%d" % lo, align_bytes=64)
-            nc.vector.quantize_mx(out=codes[:].bitcast(FP8X4), scales=plane[:], in_=woven[run][:].rearrange("p j t -> p (j t)"))
-            for y0, y1 in cut(lo, hi, (C, 2 * C)):
-                quantised[y0] = (codes[:, y0 - lo : y1 - lo], plane[:, y0 - lo : y1 - lo])
-
-        def first_layer(run, row_tiles, number):
-            lo, hi = RUNS[run]
-            width = hi - lo
+        def first_layer(quantised, lo, row_tiles, number):
+            codes, plane = quantised
+            width = codes.shape[1]
             acc = bank(number)
             for x, kb in enumerate(row_tiles):
-                for x0, x1 in cut(lo, hi, (C, 2 * C)):
+                for x0, x1 in cut(lo, lo + width, (C, 2 * C)):
                     e = x0 // C
                     nc.tensor.matmul_mx(
                         out=acc[:, x * width + x0 - lo : x * width + x1 - lo],
                         lhsT=w1[:, e, 2 * kb * P : 2 * (kb + 1) * P].bitcast(FP4X4),
                         lhsT_scale=w1_plane[:, e, kb * P : (kb + 1) * P],
-                        rhs=quantised[x0][0].bitcast(FP8X4),
-                        rhs_scale=quantised[x0][1],
+                        rhs=codes[:, x0 - lo : x1 - lo].bitcast(FP8X4),
+                        rhs_scale=plane[:, x0 - lo : x1 - lo],
                         start=True,
                         stop=True,
                     )
             return acc[:, 0 : len(row_tiles) * width]
-
-        dx = [sb.tile([P, WINDOW], F32, name="dx_%d" % kb) for kb in range(PACK)]
-
-        def store(kb):
-            nc.sync.dma_start(out[kb * P : (kb + 1) * P, :], dx[kb][:, 0:T])
 
         def copy_out(acc, name):
             sums = sb.tile([P, acc.shape[1]], F32, name=name)
             nc.vector.tensor_copy(sums[:], acc)
             return sums
 
-        slope = sb.tile([P, PACK, HALF], F32, name="slope")
-        nc.vector.tensor_scalar(slope[:, 0, :], a_first[:, HALF:T], 0.0, None, MAX)
-        nc.vector.tensor_scalar(slope[:, 1, :], a_rest[:, 0, HALF:T], 0.0, None, MAX)
-        nc.vector.tensor_scalar(slope[:, 2:, :], a_rest[:, 1:, HALF:T], 0.0, None, MAX)
-        nc.vector.scalar_tensor_tensor(factor[:, 0, :], a_first[:, 0:HALF], 0.0, g1[:, 0:HALF], MAX, MULT)
-        nc.vector.scalar_tensor_tensor(
-            factor[:, 1:, :], a_rest[:, :, 0:HALF], 0.0, g1[:, 0:HALF].unsqueeze(1).to_broadcast([P, PACK - 1, HALF]), MAX, MULT
-        )
-        factor_late = sb.tile([P, PACK, HALF], F32, name="factor_late", tag="a_rest")
-        for t in range(PACK):
-            nc.gpsimd.tensor_tensor(factor_late[:, t, :], slope[:, t, :], g1[:, HALF:T], MULT)
-        dc[0] = sb.tile([P, WINDOW], F32, name="dc_0", tag="dc_0")
-        nc.vector.tensor_copy(dc[0][:].indirect(list2[:]), whole[:])
-        for t in (1, 2, 0):
-            for run in range(2):
-                gather(t, run, *RUNS[run])
-        picked = sb.tile([P, PACK, HALF], F32, name="picked", tag="rest_3")
-        for t, lo in ((1, HALF + P), (2, HALF), (0, HALF), (3, HALF)):
+        dx = [sb.tile([P, WINDOW], F32, name="dx_%d" % kb) for kb in range(PACK)]
+
+        def store(kb):
+            nc.sync.dma_start(out[kb * P : (kb + 1) * P, :], dx[kb][:, 0:T])
+
+        def weave_late(h, lo, hi):
+            nc.vector.tensor_tensor(
+                h[:, lo:hi, :].rearrange("p (c i) t -> p c t i", i=PACK),
+                picked[:, :, lo:hi].rearrange("p t (c i) -> p c t i", i=PACK),
+                factor[:, :, lo:hi].rearrange("p t (c i) -> p c t i", i=PACK),
+                MULT,
+            )
+
+        for t in (3, 0, 1):
+            gather(first[:, t, :], t, 0, P)
+            gather(middle[:, t, :], t, P, HALF)
+        picked = sb.tile([P, PACK, HALF], F32, name="picked", tag="rest_6")
+        for t, lo in ((3, HALF + P), (0, HALF), (1, HALF), (2, HALF)):
             nc.scalar.activation(picked[:, t, lo - HALF :], dc[t][:].indirect(entries(list1, lo, T)), COPY)
-        for run in range(2):
-            gather(3, run, *RUNS[run])
-        for run in range(2):
-            weave(run)
-        for run in range(2):
-            quantise(run)
-        nc.vector.tensor_copy(picked[:, 1, 0:P], dc[1][:].indirect(entries(list1, HALF, HALF + P)))
-        sums = copy_out(first_layer(0, (1,), 0), "s0_1")
+        gather(first[:, 2, :], 2, 0, P)
+        gather(middle[:, 2, :], 2, P, HALF)
+        h0 = sb.tile([P, P, PACK], BF16, name="h0", tag="h0", align_bytes=64)
+        weave(h0[:], first[:], 0, P)
+        nc.vector.tensor_copy(picked[:, 3, 0:P], dc[3][:].indirect(entries(list1, HALF, HALF + P)))
+        q0 = quantise(h0, "0")
+        h1 = sb.tile([P, C, PACK], BF16, name="h1", tag="h0", align_bytes=64)
+        weave(h1[:, 0:P, :], middle[:, :, 0:P], P, C)
+        sums = copy_out(first_layer(q0, 0, (1,), 7), "s0_lead")
         scalar_scatter(dx[1], list1, 0, P, sums[:])
-        sums = copy_out(first_layer(0, (0, 2, 3), 1), "s0_023")
+        weave(h1[:, P:C, :], middle[:, :, P:C], C, HALF)
+        sums = copy_out(first_layer(q0, 0, (0, 2, 3), 0), "s0_rest")
         for x, kb in enumerate((0, 2, 3)):
             scalar_scatter(dx[kb], list1, 0, P, sums[:, x * P : (x + 1) * P])
-        sums = copy_out(first_layer(1, (2, 3), 3), "s1_23")
-        for kb in (2, 3):
-            scalar_scatter(dx[kb], list1, P, HALF, sums[:, (kb - 2) * C : (kb - 1) * C])
-        woven[2] = sb.tile([P, HALF, PACK], BF16, name="h_2", tag="codes_0", align_bytes=64)
-        nc.vector.tensor_tensor(
-            woven[2][:].rearrange("p (c i) t -> p c t i", i=PACK),
-            picked[:].rearrange("p t (c i) -> p c t i", i=PACK),
-            factor_late[:].rearrange("p t (c i) -> p c t i", i=PACK),
-            MULT,
-        )
-        shared = sb.tile([P, T - P], F32, name="shared")
-        nc.vector.tensor_copy(shared[:, 0:C], first_layer(1, (1,), 4))
-        scalar_scatter(dx[1], list1, P, SPLIT, shared[:, 0 : SPLIT - P])
-        middle = copy_out(first_layer(1, (0,), 5), "s1_0")
-        quantise(2)
-        nc.vector.tensor_copy(dx[0][:].indirect(entries(list1, P, HALF)), middle[:])
-        tails = {kb: copy_out(first_layer(2, (kb,), number), "s2_%d" % kb) for kb, number in ((0, 1), (2, 6), (3, 7))}
-        nc.vector.tensor_copy(shared[:, C : T - P], first_layer(2, (1,), 0))
-        nc.vector.tensor_copy(dx[0][:].indirect(entries(list1, HALF, T)), tails[0][:])
+        q1 = quantise(h1, "1")
+        h2 = sb.tile([P, HALF, PACK], BF16, name="h2", tag="plane_0", align_bytes=64)
+        weave_late(h2, 0, P)
+        s1_12 = copy_out(first_layer(q1, P, (1, 2), 1), "s1_12")
+        for x, kb in enumerate((1, 2)):
+            scalar_scatter(dx[kb], list1, P, HALF, s1_12[:, x * C : (x + 1) * C])
+        weave_late(h2, P, HALF)
+        s1_30 = copy_out(first_layer(q1, P, (3, 0), 2), "s1_30")
+        scalar_scatter(dx[3], list1, P, HALF, s1_30[:, 0:C])
+        q2 = quantise(h2, "2")
+        vector_scatter(dx[0], list1, P, HALF, s1_30[:, C : 2 * C])
+        tails = {kb: copy_out(first_layer(q2, HALF, (kb,), number), "s2_%d" % kb) for kb, number in ((0, 3), (2, 4), (3, 5), (1, 6))}
+        vector_scatter(dx[0], list1, HALF, T, tails[0][:])
         store(0)
         scalar_scatter(dx[2], list1, HALF, T, tails[2][:])
         store(2)
-        nc.vector.tensor_copy(dx[1][:].indirect(entries(list1, SPLIT, T)), shared[:, SPLIT - P : T - P])
+        vector_scatter(dx[1], list1, HALF, T, tails[1][:])
         store(1)
         scalar_scatter(dx[3], list1, HALF, T, tails[3][:])
         store(3)

@@ -48,11 +48,11 @@ def tile_moe_seb_relu2_kernel(
             return lst[:, lo // 16 : hi // 16]
 
         dy_plane = sb.tile([P, T], U8, name="dy_plane", align_bytes=64)
-        w2_plane = held.tile([P, QUADRANTS, W], U8, name="w2_plane", offset=4 * W, align_bytes=64)
-        w2_plane_rest = sb.tile([P, W], U8, name="w2_plane_rest", align_bytes=64)
+        w2_plane = held.tile([P, W], U8, name="w2_plane", offset=4 * W, align_bytes=64)
+        w2_plane_rest = held.tile([P, W], U8, name="w2_plane_rest", offset=16 * W, align_bytes=64)
         w1_plane = sb.tile([P, E, W], U8, name="w1_plane", align_bytes=64)
-        nc.gpsimd.memset(w2_plane[:].bitcast(I32)[:, 0, :], 0)
-        nc.vector.memset(dy_plane[:].bitcast(I32), 0)
+        nc.gpsimd.memset(dy_plane[:].bitcast(I32), 0)
+        nc.vector.memset(w2_plane[:].bitcast(I32), 0)
         nc.vector.memset(w2_plane_rest[:].bitcast(I32), 0)
         nc.vector.memset(w1_plane[:].bitcast(I32), 0)
 
@@ -65,18 +65,22 @@ def tile_moe_seb_relu2_kernel(
             row0 = 32 * q + DY_ROW
             queue.dma_start(dy_plane[:].bitcast(I32)[row0 : row0 + 4, :], dy_scales[0, 4 * q : 4 * q + 4, :].bitcast(I32))
 
-        nc.sync.dma_start(w2_plane[:].bitcast(I32)[0:4, :, :], w2t_scales[0, 0].rearrange("(q r) c -> r q c", r=4).bitcast(I32))
         for q in range(QUADRANTS):
             load_dy_rows(nc.scalar if q < 2 else nc.sync, q)
         nc.sync.dma_start(dy_tile[:], dy_words[0].rearrange("p t d -> p (t d)").bitcast(I32))
         nc.sync.dma_start(w2_first[:], w2t_words[0, 0].rearrange("p i d -> p (i d)").bitcast(I32))
-        g2_first = sb.tile([P, C], F32, name="g2_first")
+        for q in range(QUADRANTS):
+            queue = nc.scalar if q == 0 else nc.sync
+            queue.dma_start(w2_plane[:].bitcast(I32)[32 * q : 32 * q + 8, :], w2t_scales[0:2, 0, 4 * q : 4 * q + 4, :].bitcast(I32))
+        w2_second = sb.tile([P, W], I32, name="w2_second", align_bytes=64)
+        nc.sync.dma_start(w2_second[:], w2t_words[1, 0].rearrange("p i d -> p (i d)").bitcast(I32))
+        g2_first = held.tile([P, C], F32, name="g2_first", offset=20 * W, align_bytes=64)
         nc.sync.dma_start(g2_first[:], gate2[:, 0:C])
-        w2_rest = sb.tile([P, E - 1, W], I32, name="w2_rest", align_bytes=64)
-        nc.sync.dma_start(w2_rest[:], w2t_words[1:E, 0].rearrange("e p i d -> p e (i d)").bitcast(I32))
+        w2_third = sb.tile([P, W], I32, name="w2_third", align_bytes=64)
+        nc.sync.dma_start(w2_third[:], w2t_words[2, 0].rearrange("p i d -> p (i d)").bitcast(I32))
         for q in range(QUADRANTS):
             nc.sync.dma_start(
-                w2_plane_rest[:].bitcast(I32)[32 * q + 4 : 32 * q + 12, :], w2t_scales[1:E, 0, 4 * q : 4 * q + 4, :].bitcast(I32)
+                w2_plane_rest[:].bitcast(I32)[32 * q : 32 * q + 4, :], w2t_scales[2, 0, 4 * q : 4 * q + 4, :].bitcast(I32)
             )
         g2_rest = sb.tile([P, 2 * C], F32, name="g2_rest")
         nc.sync.dma_start(g2_rest[:], gate2[:, C:T])
@@ -97,8 +101,7 @@ def tile_moe_seb_relu2_kernel(
         list1 = sb.tile([P, T // 16], U16, name="list1")
         nc.sync.dma_start(list1[:], offs)
 
-        def sort_scales(plane, name):
-            ordered = sb.tile([P, W], U8, name=name, align_bytes=64)
+        def sort_scales(plane, ordered):
             nc.vector.tensor_copy(
                 ordered[:].rearrange("p (t m) -> p t m", t=PACK), plane.rearrange("p (m t) -> p t m", t=PACK)
             )
@@ -135,68 +138,61 @@ def tile_moe_seb_relu2_kernel(
         nc.scalar.copy(w2_lead[:], by_plane[:, :, 0])
         w2_head = held.tile([P, W], U32, name="w2_head", offset=0, align_bytes=64)
         nc.scalar.copy(w2_head[:].rearrange("p (t m) -> p m t", t=PACK)[:, :, 1:], by_plane[:, :, 1:])
-        for q in range(1, QUADRANTS):
-            nc.vector.tensor_copy(w2_plane[:].bitcast(I32)[32 * q : 32 * q + 4, 0, :], w2_plane[:].bitcast(I32)[0:4, q, :])
-        scales_a = sb.tile([P, P], U8, name="scales_a", align_bytes=64)
-        gather_bytes(scales_a[:], 0, P)
-        w2_scale_head = sort_scales(w2_plane[:, 0, :], "w2_scale_head")
+        w2_tail = {1: sb.tile([P, W], U32, name="w2_tail_1", align_bytes=64)}
+        nc.scalar.copy(
+            w2_tail[1][:].rearrange("p (t m) -> p m t", t=PACK), w2_second[:].bitcast(U32).rearrange("p (m t) -> p m t", t=PACK)
+        )
+        scales_head = sb.tile([P, HALF], U8, name="scales_head", align_bytes=64)
+        gather_bytes(scales_head[:], 0, HALF)
         words_a = held.tile([P, P], U32, name="words_a", offset=8 * W, align_bytes=64)
         gather_words(words_a[:], 0, P)
-        scales_b = held.tile([P, P], U8, name="scales_b", offset=4 * W, align_bytes=64)
-        gather_bytes(scales_b[:], P, C)
-        words_b = held.tile([P, P], U32, name="words_b", offset=5 * W, align_bytes=64)
+        words_b = held.tile([P, P], U32, name="words_b", offset=7 * W, align_bytes=64)
         gather_words(words_b[:], P, C)
+        w2_scale_head = sort_scales(w2_plane[:], sb.tile([P, W], U8, name="w2_scale_head", align_bytes=64))
+        words_rest = {1: held.tile([P, C], U32, name="words_1", offset=4 * W, align_bytes=64)}
+        gather_words(words_rest[1][:], C, 2 * C)
 
         dc = [sb.tile([P, WINDOW], F32, name="dc_%d" % t) for t in range(PACK)]
         acc_lead, acc_a, acc_b = bank(0), bank(1), bank(2)
-        second_layer(acc_lead[:, 0:P], w2_lead, w2_scale_head, 0, words_a[:], scales_a[DY_ROW:P, :])
+        second_layer(acc_lead[:, 0:P], w2_lead, w2_scale_head, 0, words_a[:], scales_head[DY_ROW:P, 0:P])
         for t in range(1, PACK):
-            second_layer(acc_a[:, (t - 1) * P : t * P], w2_head, w2_scale_head, t, words_a[:], scales_a[DY_ROW:P, :])
+            second_layer(acc_a[:, (t - 1) * P : t * P], w2_head, w2_scale_head, t, words_a[:], scales_head[DY_ROW:P, 0:P])
         for t in range(PACK):
-            second_layer(acc_b[:, t * P : (t + 1) * P], w2_head if t else w2_lead, w2_scale_head, t, words_b[:], scales_b[DY_ROW:P, :])
+            second_layer(acc_b[:, (t + 1) % PACK * P : ((t + 1) % PACK + 1) * P], w2_head if t else w2_lead, w2_scale_head, t, words_b[:], scales_head[DY_ROW:P, P:C])
         lead = sb.tile([P, P], F32, name="lead")
         gated(lead[:], acc_lead[:, 0:P], g2_first[:, 0:P])
         scalar_scatter(dc[0], list2, 0, P, lead[:])
-        block_a = sb.tile([P, PACK - 1, P], F32, name="block_a")
+        step = P + 2 * C
+        early = sb.tile([P, 3 * P + PACK * step], F32, name="early")
         gated(
-            block_a[:],
+            early[:, 0 : 3 * P].rearrange("p (t j) -> p t j", t=3),
             acc_a[:, 0 : 3 * P].rearrange("p (t j) -> p t j", t=3),
             g2_first[:, 0:P].unsqueeze(1).to_broadcast([P, 3, P]),
         )
-        for t in range(1, PACK):
-            scalar_scatter(dc[t], list2, 0, P, block_a[:, t - 1, :])
-        block_b = sb.tile([P, PACK * P + 2 * C], F32, name="block_b")
+        for t in (1, 2):
+            scalar_scatter(dc[t], list2, 0, P, early[:, (t - 1) * P : t * P])
+        second = early[:, 3 * P :].rearrange("p (x j) -> p x j", x=PACK)
         gated(
-            block_b[:, 0 : PACK * P].rearrange("p (t j) -> p t j", t=PACK),
-            acc_b[:].rearrange("p (t j) -> p t j", t=PACK),
+            second[:, :, 0:P],
+            acc_b[:].rearrange("p (x j) -> p x j", x=PACK),
             g2_first[:, P:C].unsqueeze(1).to_broadcast([P, PACK, P]),
         )
         for t in range(PACK - 1):
-            scalar_scatter(dc[t], list2, P, C, block_b[:, t * P : (t + 1) * P])
+            scalar_scatter(dc[t], list2, P, C, second[:, t + 1, 0:P])
 
-        scales_rest = held.tile([P, 2 * C], U8, name="scales_rest", offset=5 * W, align_bytes=64)
-        gather_bytes(scales_rest[:], C, T)
-        w2_tail = held.tile([P, E - 1, W], I32, name="w2_tail", offset=8 * W, align_bytes=64)
-        nc.vector.tensor_copy(
-            w2_tail[:].rearrange("p e (t m) -> p e m t", t=PACK), w2_rest[:].rearrange("p e (m t) -> p e m t", t=PACK)
-        )
-        w2_scale_rest = sort_scales(w2_plane_rest[:], "w2_scale_rest")
-        words_rest = {}
-        for e in (1, 2):
-            words_rest[e] = held.tile([P, C], U32, name="words_%d" % e, offset=(e - 1) * 4 * C, align_bytes=64)
-            gather_words(words_rest[e][:], e * C, (e + 1) * C)
+        scales_tail = held.tile([P, HALF], U8, name="scales_tail", offset=7 * W, align_bytes=64)
+        gather_bytes(scales_tail[:], HALF, T)
+        w2_scale_rest = sort_scales(w2_plane_rest[:], held.tile([P, W], U8, name="w2_scale_rest", offset=20 * W, align_bytes=64))
 
         def later_sums(pieces, number):
             acc = bank(number)
             for x, (t, e) in enumerate(pieces):
-                second_layer(
-                    acc[:, x * C : (x + 1) * C],
-                    w2_tail[:, e - 1, :],
-                    w2_scale_rest[4 * e : P, :],
-                    t,
-                    words_rest[e][:],
-                    scales_rest[DY_ROW:P, (e - 1) * C : e * C],
-                )
+                for lo, hi in cut(e * C, (e + 1) * C, (HALF,)):
+                    scales = scales_head[DY_ROW:P, lo:hi] if lo < HALF else scales_tail[DY_ROW:P, lo - HALF : hi - HALF]
+                    cols = slice(lo - e * C, hi - e * C)
+                    second_layer(
+                        acc[:, x * C : (x + 1) * C][:, cols], w2_tail[e], w2_scale_head[4:P, :] if e == 1 else w2_scale_rest, t, words_rest[e][:, cols], scales
+                    )
             return acc
 
         def one_gate(e):
@@ -209,20 +205,26 @@ def tile_moe_seb_relu2_kernel(
             (5, ((3, 1), (3, 2)), both_gates),
             (6, ((1, 2), (2, 2)), one_gate(2)),
         ):
+            if number == 4:
+                w2_tail[2] = held.tile([P, W], I32, name="w2_tail_2", offset=8 * W, align_bytes=64)
+                nc.vector.tensor_copy(
+                    w2_tail[2][:].rearrange("p (t m) -> p m t", t=PACK), w2_third[:].rearrange("p (m t) -> p m t", t=PACK)
+                )
+                words_rest[2] = held.tile([P, C], U32, name="words_2", offset=16 * W + C, align_bytes=64)
+                gather_words(words_rest[2][:], 2 * C, T)
             acc = later_sums(pieces, number)[:].rearrange("p (x j) -> p x j", x=2)
             if number == 5:
-                gated(block_b[:, PACK * P :].rearrange("p (x j) -> p x j", x=2), acc, gate)
+                gated(second[:, 0, P:].rearrange("p (x j) -> p x j", x=2), acc, gate)
             else:
                 values = sb.tile([P, 2, C], F32, name="rest_%d" % number, tag="rest_%d" % number)
                 gated(values[:], acc, gate)
                 for x, (t, e) in enumerate(pieces):
                     scalar_scatter(dc[t], list2, e * C, (e + 1) * C, values[:, x, :])
-        slope = sb.tile([P, PACK, HALF], F32, name="slope")
-        nc.vector.tensor_scalar(slope[:], a_late[:], 0.0, None, MAX)
         factor = sb.tile([P, PACK, HALF], F32, name="factor")
-        for t in range(PACK):
-            nc.gpsimd.tensor_tensor(factor[:, t, :], slope[:, t, :], g1[:, HALF:T], MULT)
-        vector_scatter(dc[3], list2, P, T, block_b[:, 3 * P :])
+        nc.vector.scalar_tensor_tensor(
+            factor[:], a_late[:], 0.0, g1[:, HALF:T].unsqueeze(1).to_broadcast([P, PACK, HALF]), MAX, MULT
+        )
+        vector_scatter(dc[3], list2, 0, T, early[:, 2 * P : 2 * P + T])
 
         first = sb.tile([P, PACK, P], F32, name="first")
         middle = sb.tile([P, PACK, C], F32, name="middle")

@@ -82,13 +82,14 @@ def tile_moe_seb_relu2_kernel(
             nc.sync.dma_start(
                 w2_plane_rest[:].bitcast(I32)[32 * q : 32 * q + 4, :], w2t_scales[2, 0, 4 * q : 4 * q + 4, :].bitcast(I32)
             )
-        g2_rest = sb.tile([P, 2 * C], F32, name="g2_rest")
-        nc.sync.dma_start(g2_rest[:], gate2[:, C:T])
         a_rows = a.rearrange("(p t) j -> p t j", t=PACK)
-        a_late = sb.tile([P, PACK, HALF], F32, name="a_late")
-        nc.sync.dma_start(a_late[:], a_rows[:, :, HALF:T])
+        a_late = [sb.tile([P, 2, HALF], F32, name="a_late_%d" % x) for x in range(2)]
+        nc.sync.dma_start(a_late[0][:], a_rows[:, 0:2, HALF:T])
         g1 = sb.tile([P, T], F32, name="g1")
         nc.sync.dma_start(g1[:], gate1)
+        g2_rest = sb.tile([P, 2 * C], F32, name="g2_rest")
+        nc.sync.dma_start(g2_rest[:], gate2[:, C:T])
+        nc.sync.dma_start(a_late[1][:], a_rows[:, 2:, HALF:T])
         a_early = sb.tile([P, PACK, HALF], F32, name="a_early")
         nc.sync.dma_start(a_early[:], a_rows[:, :, 0:HALF])
         for q in range(QUADRANTS):
@@ -198,6 +199,16 @@ def tile_moe_seb_relu2_kernel(
         def one_gate(e):
             return g2_rest[:, (e - 1) * C : e * C].unsqueeze(1).to_broadcast([P, 2, C])
 
+        w2_tail[2] = held.tile([P, W], I32, name="w2_tail_2", offset=8 * W, align_bytes=64)
+        nc.vector.tensor_copy(
+            w2_tail[2][:].rearrange("p (t m) -> p m t", t=PACK), w2_third[:].rearrange("p (m t) -> p m t", t=PACK)
+        )
+        words_rest[2] = held.tile([P, C], U32, name="words_2", offset=16 * W + C, align_bytes=64)
+        gather_words(words_rest[2][:], 2 * C, T)
+        factor = sb.tile([P, PACK, HALF], F32, name="factor")
+        slope = sb.tile([P, 2, HALF], F32, name="slope")
+        nc.vector.tensor_scalar(slope[:], a_late[0][:], 0.0, None, MAX)
+        nc.gpsimd.tensor_tensor(factor[:, 0:2, :], slope[:], g1[:, HALF:T].unsqueeze(1).to_broadcast([P, 2, HALF]), MULT)
         both_gates = g2_rest[:].rearrange("p (e j) -> p e j", e=2)
         for number, pieces, gate in (
             (3, ((0, 1), (1, 1)), one_gate(1)),
@@ -205,13 +216,6 @@ def tile_moe_seb_relu2_kernel(
             (5, ((3, 1), (3, 2)), both_gates),
             (6, ((1, 2), (2, 2)), one_gate(2)),
         ):
-            if number == 4:
-                w2_tail[2] = held.tile([P, W], I32, name="w2_tail_2", offset=8 * W, align_bytes=64)
-                nc.vector.tensor_copy(
-                    w2_tail[2][:].rearrange("p (t m) -> p m t", t=PACK), w2_third[:].rearrange("p (m t) -> p m t", t=PACK)
-                )
-                words_rest[2] = held.tile([P, C], U32, name="words_2", offset=16 * W + C, align_bytes=64)
-                gather_words(words_rest[2][:], 2 * C, T)
             acc = later_sums(pieces, number)[:].rearrange("p (x j) -> p x j", x=2)
             if number == 5:
                 gated(second[:, 0, P:].rearrange("p (x j) -> p x j", x=2), acc, gate)
@@ -220,9 +224,8 @@ def tile_moe_seb_relu2_kernel(
                 gated(values[:], acc, gate)
                 for x, (t, e) in enumerate(pieces):
                     scalar_scatter(dc[t], list2, e * C, (e + 1) * C, values[:, x, :])
-        factor = sb.tile([P, PACK, HALF], F32, name="factor")
         nc.vector.scalar_tensor_tensor(
-            factor[:], a_late[:], 0.0, g1[:, HALF:T].unsqueeze(1).to_broadcast([P, PACK, HALF]), MAX, MULT
+            factor[:, 2:, :], a_late[1][:], 0.0, g1[:, HALF:T].unsqueeze(1).to_broadcast([P, 2, HALF]), MAX, MULT
         )
         vector_scatter(dc[3], list2, 0, T, early[:, 2 * P : 2 * P + T])
 

@@ -286,7 +286,7 @@ def tile_moe_seb_relu2_kernel(
         for t in (3, 0, 1):
             gather(first[:, t, :], t, 0, P)
             gather(middle[:, t, :], t, P, HALF)
-        picked = sb.tile([P, PACK, HALF], F32, name="picked", tag="rest_6")
+        picked = sb.tile([P, PACK, HALF], F32, name="picked")
         for t, lo in ((3, HALF + P), (0, HALF), (1, HALF), (2, HALF)):
             nc.scalar.activation(picked[:, t, lo - HALF :], dc[t][:].indirect(entries(list1, lo, T)), COPY)
         gather(first[:, 2, :], 2, 0, P)
@@ -297,7 +297,8 @@ def tile_moe_seb_relu2_kernel(
         q0 = quantise(h0, "0")
         h1 = sb.tile([P, C, PACK], BF16, name="h1", tag="h0", align_bytes=64)
         weave(h1[:, 0:P, :], middle[:, :, 0:P], P, C)
-        sums = copy_out(first_layer(q0, 0, (1,), 7), "s0_lead")
+        sums = sb.tile([P, P], F32, name="s0_lead")
+        nc.scalar.copy(sums[:], first_layer(q0, 0, (1,), 7))
         scalar_scatter(dx[1], list1, 0, P, sums[:])
         weave(h1[:, P:C, :], middle[:, :, P:C], C, HALF)
         sums = copy_out(first_layer(q0, 0, (0, 2, 3), 0), "s0_rest")

@@ -297,12 +297,13 @@ def tile_moe_seb_relu2_kernel(
         q0 = quantise(h0, "0")
         h1 = sb.tile([P, C, PACK], BF16, name="h1", tag="h0", align_bytes=64)
         weave(h1[:, 0:P, :], middle[:, :, 0:P], P, C)
-        sums = sb.tile([P, P], F32, name="s0_lead")
-        nc.scalar.copy(sums[:], first_layer(q0, 0, (1,), 7))
-        scalar_scatter(dx[1], list1, 0, P, sums[:])
+        sums = sb.tile([P, C], F32, name="s0_lead")
+        nc.scalar.copy(sums[:], first_layer(q0, 0, (1, 0), 7))
+        for x, kb in enumerate((1, 0)):
+            scalar_scatter(dx[kb], list1, 0, P, sums[:, x * P : (x + 1) * P])
         weave(h1[:, P:C, :], middle[:, :, P:C], C, HALF)
-        sums = copy_out(first_layer(q0, 0, (0, 2, 3), 0), "s0_rest")
-        for x, kb in enumerate((0, 2, 3)):
+        sums = copy_out(first_layer(q0, 0, (2, 3), 0), "s0_rest")
+        for x, kb in enumerate((2, 3)):
             scalar_scatter(dx[kb], list1, 0, P, sums[:, x * P : (x + 1) * P])
         q1 = quantise(h1, "1")
         h2 = sb.tile([P, HALF, PACK], BF16, name="h2", tag="plane_0", align_bytes=64)

@@ -229,7 +229,7 @@ def tile_moe_seb_relu2_kernel(
         )
         vector_scatter(dc[3], list2, 0, T, early[:, 2 * P : 2 * P + T])
 
-        first = sb.tile([P, PACK, P], F32, name="first")
+        first = sb.tile([P, PACK, P], F32, name="first", tag="first", align_bytes=64)
         middle = sb.tile([P, PACK, C], F32, name="middle")
 
         def gather(into, t, lo, hi):
@@ -291,17 +291,16 @@ def tile_moe_seb_relu2_kernel(
             nc.scalar.activation(picked[:, t, lo - HALF :], dc[t][:].indirect(entries(list1, lo, T)), COPY)
         gather(first[:, 2, :], 2, 0, P)
         gather(middle[:, 2, :], 2, P, HALF)
-        h0 = sb.tile([P, P, PACK], BF16, name="h0", tag="h0", align_bytes=64)
+        h0 = sb.tile([P, P, PACK], BF16, name="h0", align_bytes=64)
         weave(h0[:], first[:], 0, P)
         nc.vector.tensor_copy(picked[:, 3, 0:P], dc[3][:].indirect(entries(list1, HALF, HALF + P)))
         q0 = quantise(h0, "0")
-        h1 = sb.tile([P, C, PACK], BF16, name="h1", tag="h0", align_bytes=64)
-        weave(h1[:, 0:P, :], middle[:, :, 0:P], P, C)
+        h1 = sb.tile([P, C, PACK], BF16, name="h1", tag="first", align_bytes=64)
+        weave(h1[:], middle[:], P, HALF)
         sums = sb.tile([P, C], F32, name="s0_lead")
         nc.scalar.copy(sums[:], first_layer(q0, 0, (1, 0), 7))
         for x, kb in enumerate((1, 0)):
             scalar_scatter(dx[kb], list1, 0, P, sums[:, x * P : (x + 1) * P])
-        weave(h1[:, P:C, :], middle[:, :, P:C], C, HALF)
         sums = copy_out(first_layer(q0, 0, (2, 3), 0), "s0_rest")
         for x, kb in enumerate((2, 3)):
             scalar_scatter(dx[kb], list1, 0, P, sums[:, x * P : (x + 1) * P])

@@ -74,8 +74,8 @@ def tile_moe_seb_relu2_kernel(
             queue.dma_start(w2_plane[:].bitcast(I32)[32 * q : 32 * q + 8, :], w2t_scales[0:2, 0, 4 * q : 4 * q + 4, :].bitcast(I32))
         w2_second = sb.tile([P, W], I32, name="w2_second", align_bytes=64)
         nc.sync.dma_start(w2_second[:], w2t_words[1, 0].rearrange("p i d -> p (i d)").bitcast(I32))
-        g2_first = held.tile([P, C], F32, name="g2_first", offset=20 * W, align_bytes=64)
-        nc.sync.dma_start(g2_first[:], gate2[:, 0:C])
+        g2 = sb.tile([P, T], F32, name="g2")
+        nc.sync.dma_start(g2[:, 0:HALF], gate2[:, 0:HALF])
         w2_third = sb.tile([P, W], I32, name="w2_third", align_bytes=64)
         nc.sync.dma_start(w2_third[:], w2t_words[2, 0].rearrange("p i d -> p (i d)").bitcast(I32))
         for q in range(QUADRANTS):
@@ -86,10 +86,10 @@ def tile_moe_seb_relu2_kernel(
         a_late = [sb.tile([P, 2, HALF], F32, name="a_late_%d" % x) for x in range(2)]
         nc.sync.dma_start(a_late[0][:], a_rows[:, 0:2, HALF:T])
         g1 = sb.tile([P, T], F32, name="g1")
-        nc.sync.dma_start(g1[:], gate1)
-        g2_rest = sb.tile([P, 2 * C], F32, name="g2_rest")
-        nc.sync.dma_start(g2_rest[:], gate2[:, C:T])
+        nc.sync.dma_start(g1[:, HALF:T], gate1[:, HALF:T])
+        nc.sync.dma_start(g2[:, HALF:T], gate2[:, HALF:T])
         nc.sync.dma_start(a_late[1][:], a_rows[:, 2:, HALF:T])
+        nc.sync.dma_start(g1[:, 0:HALF], gate1[:, 0:HALF])
         a_early = sb.tile([P, PACK, HALF], F32, name="a_early")
         nc.sync.dma_start(a_early[:], a_rows[:, :, 0:HALF])
         for q in range(QUADRANTS):
@@ -139,95 +139,84 @@ def tile_moe_seb_relu2_kernel(
         nc.scalar.copy(w2_lead[:], by_plane[:, :, 0])
         w2_head = held.tile([P, W], U32, name="w2_head", offset=0, align_bytes=64)
         nc.scalar.copy(w2_head[:].rearrange("p (t m) -> p m t", t=PACK)[:, :, 1:], by_plane[:, :, 1:])
-        w2_tail = {1: sb.tile([P, W], U32, name="w2_tail_1", align_bytes=64)}
+        w2_sorted = {0: w2_head, 1: sb.tile([P, W], U32, name="w2_sorted_1", align_bytes=64)}
         nc.scalar.copy(
-            w2_tail[1][:].rearrange("p (t m) -> p m t", t=PACK), w2_second[:].bitcast(U32).rearrange("p (m t) -> p m t", t=PACK)
+            w2_sorted[1][:].rearrange("p (t m) -> p m t", t=PACK), w2_second[:].bitcast(U32).rearrange("p (m t) -> p m t", t=PACK)
         )
         scales_head = sb.tile([P, HALF], U8, name="scales_head", align_bytes=64)
         gather_bytes(scales_head[:], 0, HALF)
-        words_a = held.tile([P, P], U32, name="words_a", offset=8 * W, align_bytes=64)
-        gather_words(words_a[:], 0, P)
-        words_b = held.tile([P, P], U32, name="words_b", offset=7 * W, align_bytes=64)
-        gather_words(words_b[:], P, C)
+        words = {0: held.tile([P, C], U32, name="words_0", offset=8 * W, align_bytes=64)}
+        gather_words(words[0][:, 0:P], 0, P)
+        gather_words(words[0][:, P:C], P, C)
         w2_scale_head = sort_scales(w2_plane[:], sb.tile([P, W], U8, name="w2_scale_head", align_bytes=64))
-        words_rest = {1: held.tile([P, C], U32, name="words_1", offset=4 * W, align_bytes=64)}
-        gather_words(words_rest[1][:], C, 2 * C)
+        w2_scales = {0: w2_scale_head[:], 1: w2_scale_head[4:P, :]}
+        words[1] = held.tile([P, C], U32, name="words_1", offset=4 * W, align_bytes=64)
+        gather_words(words[1][:], C, 2 * C)
+        dy_picked = {0: scales_head}
+
+        def sums_of(pieces, number):
+            acc = bank(number)
+            at = 0
+            for t, lo, hi in pieces:
+                for x0, x1 in cut(lo, hi, (C, HALF, 2 * C)):
+                    e, half = x0 // C, x0 // HALF
+                    second_layer(
+                        acc[:, at + x0 - lo : at + x1 - lo],
+                        w2_lead if (e, t) == (0, 0) else w2_sorted[e],
+                        w2_scales[e],
+                        t,
+                        words[e][:, x0 - e * C : x1 - e * C],
+                        dy_picked[half][DY_ROW:P, x0 - half * HALF : x1 - half * HALF],
+                    )
+                at += hi - lo
+            return acc[:, 0:at]
 
         dc = [sb.tile([P, WINDOW], F32, name="dc_%d" % t) for t in range(PACK)]
-        acc_lead, acc_a, acc_b = bank(0), bank(1), bank(2)
-        second_layer(acc_lead[:, 0:P], w2_lead, w2_scale_head, 0, words_a[:], scales_head[DY_ROW:P, 0:P])
-        for t in range(1, PACK):
-            second_layer(acc_a[:, (t - 1) * P : t * P], w2_head, w2_scale_head, t, words_a[:], scales_head[DY_ROW:P, 0:P])
-        for t in range(PACK):
-            second_layer(acc_b[:, (t + 1) % PACK * P : ((t + 1) % PACK + 1) * P], w2_head if t else w2_lead, w2_scale_head, t, words_b[:], scales_head[DY_ROW:P, P:C])
-        lead = sb.tile([P, P], F32, name="lead")
-        gated(lead[:], acc_lead[:, 0:P], g2_first[:, 0:P])
-        scalar_scatter(dc[0], list2, 0, P, lead[:])
-        step = P + 2 * C
-        early = sb.tile([P, 3 * P + PACK * step], F32, name="early")
-        gated(
-            early[:, 0 : 3 * P].rearrange("p (t j) -> p t j", t=3),
-            acc_a[:, 0 : 3 * P].rearrange("p (t j) -> p t j", t=3),
-            g2_first[:, 0:P].unsqueeze(1).to_broadcast([P, 3, P]),
-        )
-        for t in (1, 2):
-            scalar_scatter(dc[t], list2, 0, P, early[:, (t - 1) * P : t * P])
-        second = early[:, 3 * P :].rearrange("p (x j) -> p x j", x=PACK)
-        gated(
-            second[:, :, 0:P],
-            acc_b[:].rearrange("p (x j) -> p x j", x=PACK),
-            g2_first[:, P:C].unsqueeze(1).to_broadcast([P, PACK, P]),
-        )
-        for t in range(PACK - 1):
-            scalar_scatter(dc[t], list2, P, C, second[:, t + 1, 0:P])
 
-        scales_tail = held.tile([P, HALF], U8, name="scales_tail", offset=7 * W, align_bytes=64)
-        gather_bytes(scales_tail[:], HALF, T)
-        w2_scale_rest = sort_scales(w2_plane_rest[:], held.tile([P, W], U8, name="w2_scale_rest", offset=20 * W, align_bytes=64))
+        def products(t, lo, hi, number, gate):
+            values = sb.tile([P, hi - lo], F32, name="values_%d_%d" % (t, lo), tag="values_%d_%d" % (t, lo), align_bytes=64)
+            gated(values[:], sums_of(((t, lo, hi),), number), gate)
+            scalar_scatter(dc[t], list2, lo, hi, values[:])
 
-        def later_sums(pieces, number):
-            acc = bank(number)
-            for x, (t, e) in enumerate(pieces):
-                for lo, hi in cut(e * C, (e + 1) * C, (HALF,)):
-                    scales = scales_head[DY_ROW:P, lo:hi] if lo < HALF else scales_tail[DY_ROW:P, lo - HALF : hi - HALF]
-                    cols = slice(lo - e * C, hi - e * C)
-                    second_layer(
-                        acc[:, x * C : (x + 1) * C][:, cols], w2_tail[e], w2_scale_head[4:P, :] if e == 1 else w2_scale_rest, t, words_rest[e][:, cols], scales
-                    )
-            return acc
+        def paired(into, pieces, number, e):
+            gated(
+                into.rearrange("p (x j) -> p x j", x=2),
+                sums_of(pieces, number).rearrange("p (x j) -> p x j", x=2),
+                g2[:, e * C : (e + 1) * C].unsqueeze(1).to_broadcast([P, 2, C]),
+            )
 
-        def one_gate(e):
-            return g2_rest[:, (e - 1) * C : e * C].unsqueeze(1).to_broadcast([P, 2, C])
-
-        w2_tail[2] = held.tile([P, W], I32, name="w2_tail_2", offset=8 * W, align_bytes=64)
+        for t, hi in ((0, P), (1, C), (2, C)):
+            products(t, 0, hi, t, g2[:, 0:hi])
+        dy_picked[1] = sb.tile([P, HALF], U8, name="scales_tail", tag="values_0_0", align_bytes=64)
+        gather_bytes(dy_picked[1][:], HALF, T)
+        products(0, P, HALF, 3, g2[:, P:HALF])
+        w2_scales[2] = sort_scales(w2_plane_rest[:], sb.tile([P, W], U8, name="w2_scale_rest", align_bytes=64))[:]
+        w2_sorted[2] = held.tile([P, W], I32, name="w2_sorted_2", offset=8 * W, align_bytes=64)
         nc.vector.tensor_copy(
-            w2_tail[2][:].rearrange("p (t m) -> p m t", t=PACK), w2_third[:].rearrange("p (m t) -> p m t", t=PACK)
+            w2_sorted[2][:].rearrange("p (t m) -> p m t", t=PACK), w2_third[:].rearrange("p (m t) -> p m t", t=PACK)
         )
-        words_rest[2] = held.tile([P, C], U32, name="words_2", offset=16 * W + C, align_bytes=64)
-        gather_words(words_rest[2][:], 2 * C, T)
+        words[2] = held.tile([P, C], U32, name="words_2", offset=16 * W + C, align_bytes=64)
+        gather_words(words[2][:], 2 * C, T)
         factor = sb.tile([P, PACK, HALF], F32, name="factor")
         slope = sb.tile([P, 2, HALF], F32, name="slope")
         nc.vector.tensor_scalar(slope[:], a_late[0][:], 0.0, None, MAX)
         nc.gpsimd.tensor_tensor(factor[:, 0:2, :], slope[:], g1[:, HALF:T].unsqueeze(1).to_broadcast([P, 2, HALF]), MULT)
-        both_gates = g2_rest[:].rearrange("p (e j) -> p e j", e=2)
-        for number, pieces, gate in (
-            (3, ((0, 1), (1, 1)), one_gate(1)),
-            (4, ((2, 1), (0, 2)), both_gates),
-            (5, ((3, 1), (3, 2)), both_gates),
-            (6, ((1, 2), (2, 2)), one_gate(2)),
-        ):
-            acc = later_sums(pieces, number)[:].rearrange("p (x j) -> p x j", x=2)
-            if number == 5:
-                gated(second[:, 0, P:].rearrange("p (x j) -> p x j", x=2), acc, gate)
-            else:
-                values = sb.tile([P, 2, C], F32, name="rest_%d" % number, tag="rest_%d" % number)
-                gated(values[:], acc, gate)
-                for x, (t, e) in enumerate(pieces):
-                    scalar_scatter(dc[t], list2, e * C, (e + 1) * C, values[:, x, :])
+        def pair_for_scalar(e, number):
+            values = sb.tile([P, 2 * C], F32, name="pair_%d" % e)
+            paired(values[:], [(t, e * C, (e + 1) * C) for t in (1, 2)], number, e)
+            for x, t in enumerate((1, 2)):
+                scalar_scatter(dc[t], list2, e * C, (e + 1) * C, values[:, x * C : (x + 1) * C])
+
+        pair_for_scalar(1, 4)
+        products(0, HALF, T, 5, g2[:, HALF:T])
+        whole = sb.tile([P, T], F32, name="whole")
+        for lo, hi, number in ((0, 2 * C, 6), (2 * C, T, 7)):
+            gated(whole[:, lo:hi], sums_of(((3, lo, hi),), number), g2[:, lo:hi])
+        pair_for_scalar(2, 0)
         nc.vector.scalar_tensor_tensor(
             factor[:, 2:, :], a_late[1][:], 0.0, g1[:, HALF:T].unsqueeze(1).to_broadcast([P, 2, HALF]), MAX, MULT
         )
-        vector_scatter(dc[3], list2, 0, T, early[:, 2 * P : 2 * P + T])
+        vector_scatter(dc[3], list2, 0, T, whole[:])
 
         first = sb.tile([P, PACK, P], F32, name="first", tag="first", align_bytes=64)
         middle = sb.tile([P, PACK, C], F32, name="middle")

@@ -21,7 +21,7 @@ E = 3
 C = 256
 W = 512
 QUADRANTS = 4
-WINDOW = 1024
+SHIFT = 96
 HALF = T // 2
 FLOPS = 2 * 2 * W * W * T
 DY_ROW = 4
@@ -48,8 +48,8 @@ def tile_moe_seb_relu2_kernel(
             return lst[:, lo // 16 : hi // 16]
 
         dy_plane = sb.tile([P, T], U8, name="dy_plane", align_bytes=64)
-        w2_plane = held.tile([P, W], U8, name="w2_plane", offset=4 * W, align_bytes=64)
-        w2_plane_rest = held.tile([P, W], U8, name="w2_plane_rest", offset=16 * W, align_bytes=64)
+        w2_plane = held.tile([P, W], U8, name="w2_plane", offset=0, align_bytes=64)
+        w2_plane_rest = sb.tile([P, W], U8, name="w2_plane_rest", align_bytes=64)
         w1_plane = sb.tile([P, E, W], U8, name="w1_plane", align_bytes=64)
         nc.gpsimd.memset(dy_plane[:].bitcast(I32), 0)
         nc.vector.memset(w2_plane[:].bitcast(I32), 0)
@@ -58,38 +58,36 @@ def tile_moe_seb_relu2_kernel(
 
         list2 = sb.tile([P, T // 16], U16, name="list2")
         nc.sync.dma_start(list2[:], offs2)
-        w2_first = sb.tile([P, W], I32, name="w2_first", align_bytes=64)
         dy_tile = sb.tile([P, T], I32, name="dy_tile", align_bytes=64)
-
-        def load_dy_rows(queue, q):
-            row0 = 32 * q + DY_ROW
-            queue.dma_start(dy_plane[:].bitcast(I32)[row0 : row0 + 4, :], dy_scales[0, 4 * q : 4 * q + 4, :].bitcast(I32))
-
         for q in range(QUADRANTS):
-            load_dy_rows(nc.scalar if q < 2 else nc.sync, q)
+            row0 = 32 * q + DY_ROW
+            queue = nc.scalar if q < 2 else nc.sync
+            queue.dma_start(dy_plane[:].bitcast(I32)[row0 : row0 + 4, :], dy_scales[0, 4 * q : 4 * q + 4, :].bitcast(I32))
         nc.sync.dma_start(dy_tile[:], dy_words[0].rearrange("p t d -> p (t d)").bitcast(I32))
-        nc.sync.dma_start(w2_first[:], w2t_words[0, 0].rearrange("p i d -> p (i d)").bitcast(I32))
+
+        def load_w2(e):
+            raw = sb.tile([P, W], I32, name="w2_raw_%d" % e, align_bytes=64)
+            nc.sync.dma_start(raw[:], w2t_words[e, 0].rearrange("p i d -> p (i d)").bitcast(I32))
+            return raw[:].bitcast(U32).rearrange("p (m t) -> p m t", t=PACK)
+
+        w2_first = load_w2(0)
         for q in range(QUADRANTS):
             queue = nc.scalar if q == 0 else nc.sync
             queue.dma_start(w2_plane[:].bitcast(I32)[32 * q : 32 * q + 8, :], w2t_scales[0:2, 0, 4 * q : 4 * q + 4, :].bitcast(I32))
-        w2_second = sb.tile([P, W], I32, name="w2_second", align_bytes=64)
-        nc.sync.dma_start(w2_second[:], w2t_words[1, 0].rearrange("p i d -> p (i d)").bitcast(I32))
+        w2_second = load_w2(1)
         g2 = sb.tile([P, T], F32, name="g2")
         nc.sync.dma_start(g2[:, 0:HALF], gate2[:, 0:HALF])
-        w2_third = sb.tile([P, W], I32, name="w2_third", align_bytes=64)
-        nc.sync.dma_start(w2_third[:], w2t_words[2, 0].rearrange("p i d -> p (i d)").bitcast(I32))
+        a_rows = a.rearrange("(p t) j -> p t j", t=PACK)
+        a_late = held.tile([P, PACK, HALF], F32, name="a_late", offset=2560, align_bytes=64)
+        nc.sync.dma_start(a_late[:], a_rows[:, :, HALF:T])
+        nc.sync.dma_start(g2[:, HALF:T], gate2[:, HALF:T])
+        w2_third = load_w2(2)
         for q in range(QUADRANTS):
             nc.sync.dma_start(
                 w2_plane_rest[:].bitcast(I32)[32 * q : 32 * q + 4, :], w2t_scales[2, 0, 4 * q : 4 * q + 4, :].bitcast(I32)
             )
-        a_rows = a.rearrange("(p t) j -> p t j", t=PACK)
-        a_late = [sb.tile([P, 2, HALF], F32, name="a_late_%d" % x) for x in range(2)]
-        nc.sync.dma_start(a_late[0][:], a_rows[:, 0:2, HALF:T])
         g1 = sb.tile([P, T], F32, name="g1")
-        nc.sync.dma_start(g1[:, HALF:T], gate1[:, HALF:T])
-        nc.sync.dma_start(g2[:, HALF:T], gate2[:, HALF:T])
-        nc.sync.dma_start(a_late[1][:], a_rows[:, 2:, HALF:T])
-        nc.sync.dma_start(g1[:, 0:HALF], gate1[:, 0:HALF])
+        nc.sync.dma_start(g1[:], gate1)
         a_early = sb.tile([P, PACK, HALF], F32, name="a_early")
         nc.sync.dma_start(a_early[:], a_rows[:, :, 0:HALF])
         for q in range(QUADRANTS):
@@ -102,10 +100,8 @@ def tile_moe_seb_relu2_kernel(
         list1 = sb.tile([P, T // 16], U16, name="list1")
         nc.sync.dma_start(list1[:], offs)
 
-        def sort_scales(plane, ordered):
-            nc.vector.tensor_copy(
-                ordered[:].rearrange("p (t m) -> p t m", t=PACK), plane.rearrange("p (m t) -> p t m", t=PACK)
-            )
+        def sort_scales(engine, plane, ordered):
+            engine.tensor_copy(ordered[:].rearrange("p (t m) -> p t m", t=PACK), plane[:].rearrange("p (m t) -> p t m", t=PACK))
             return ordered
 
         def gather_bytes(picked, lo, hi):
@@ -134,23 +130,19 @@ def tile_moe_seb_relu2_kernel(
         def vector_scatter(window, lst, lo, hi, values):
             nc.vector.tensor_copy(window[:].indirect(entries(lst, lo, hi)), values)
 
-        by_plane = w2_first[:].bitcast(U32).rearrange("p (m t) -> p m t", t=PACK)
         w2_lead = sb.tile([P, P], U32, name="w2_lead", align_bytes=64)
-        nc.scalar.copy(w2_lead[:], by_plane[:, :, 0])
-        w2_head = held.tile([P, W], U32, name="w2_head", offset=0, align_bytes=64)
-        nc.scalar.copy(w2_head[:].rearrange("p (t m) -> p m t", t=PACK)[:, :, 1:], by_plane[:, :, 1:])
-        w2_sorted = {0: w2_head, 1: sb.tile([P, W], U32, name="w2_sorted_1", align_bytes=64)}
-        nc.scalar.copy(
-            w2_sorted[1][:].rearrange("p (t m) -> p m t", t=PACK), w2_second[:].bitcast(U32).rearrange("p (m t) -> p m t", t=PACK)
-        )
+        nc.scalar.copy(w2_lead[:], w2_first[:, :, 0])
+        w2_sorted = {e: sb.tile([P, W], U32, name="w2_sorted_%d" % e, align_bytes=64) for e in range(2)}
+        nc.scalar.copy(w2_sorted[0][:].rearrange("p (t m) -> p m t", t=PACK)[:, :, 1:], w2_first[:, :, 1:])
+        nc.scalar.copy(w2_sorted[1][:].rearrange("p (t m) -> p m t", t=PACK), w2_second)
         scales_head = sb.tile([P, HALF], U8, name="scales_head", align_bytes=64)
         gather_bytes(scales_head[:], 0, HALF)
-        words = {0: held.tile([P, C], U32, name="words_0", offset=8 * W, align_bytes=64)}
+        words = {0: sb.tile([P, C], U32, name="words_0", align_bytes=64)}
         gather_words(words[0][:, 0:P], 0, P)
         gather_words(words[0][:, P:C], P, C)
-        w2_scale_head = sort_scales(w2_plane[:], sb.tile([P, W], U8, name="w2_scale_head", align_bytes=64))
+        w2_scale_head = sort_scales(nc.vector, w2_plane, sb.tile([P, W], U8, name="w2_scale_head", align_bytes=64))
         w2_scales = {0: w2_scale_head[:], 1: w2_scale_head[4:P, :]}
-        words[1] = held.tile([P, C], U32, name="words_1", offset=4 * W, align_bytes=64)
+        words[1] = held.tile([P, C], U32, name="words_1", offset=0, align_bytes=64)
         gather_words(words[1][:], C, 2 * C)
         dy_picked = {0: scales_head}
 
@@ -171,52 +163,51 @@ def tile_moe_seb_relu2_kernel(
                 at += hi - lo
             return acc[:, 0:at]
 
-        dc = [sb.tile([P, WINDOW], F32, name="dc_%d" % t) for t in range(PACK)]
+        dc = [sb.tile([P, T], F32, name="dc_%d" % t) for t in range(PACK)]
 
-        def products(t, lo, hi, number, gate):
-            values = sb.tile([P, hi - lo], F32, name="values_%d_%d" % (t, lo), tag="values_%d_%d" % (t, lo), align_bytes=64)
-            gated(values[:], sums_of(((t, lo, hi),), number), gate)
-            scalar_scatter(dc[t], list2, lo, hi, values[:])
+        def products(values, t, lo, hi, number, stop):
+            gated(values[:], sums_of(((t, lo, hi),), number), g2[:, lo:hi])
+            scalar_scatter(dc[t], list2, lo, stop, values[:, 0 : stop - lo])
 
-        def paired(into, pieces, number, e):
-            gated(
-                into.rearrange("p (x j) -> p x j", x=2),
-                sums_of(pieces, number).rearrange("p (x j) -> p x j", x=2),
-                g2[:, e * C : (e + 1) * C].unsqueeze(1).to_broadcast([P, 2, C]),
-            )
-
-        for t, hi in ((0, P), (1, C), (2, C)):
-            products(t, 0, hi, t, g2[:, 0:hi])
-        dy_picked[1] = sb.tile([P, HALF], U8, name="scales_tail", tag="values_0_0", align_bytes=64)
-        gather_bytes(dy_picked[1][:], HALF, T)
-        products(0, P, HALF, 3, g2[:, P:HALF])
-        w2_scales[2] = sort_scales(w2_plane_rest[:], sb.tile([P, W], U8, name="w2_scale_rest", align_bytes=64))[:]
-        w2_sorted[2] = held.tile([P, W], I32, name="w2_sorted_2", offset=8 * W, align_bytes=64)
-        nc.vector.tensor_copy(
-            w2_sorted[2][:].rearrange("p (t m) -> p m t", t=PACK), w2_third[:].rearrange("p (m t) -> p m t", t=PACK)
-        )
-        words[2] = held.tile([P, C], U32, name="words_2", offset=16 * W + C, align_bytes=64)
-        gather_words(words[2][:], 2 * C, T)
-        factor = sb.tile([P, PACK, HALF], F32, name="factor")
-        slope = sb.tile([P, 2, HALF], F32, name="slope")
-        nc.vector.tensor_scalar(slope[:], a_late[0][:], 0.0, None, MAX)
-        nc.gpsimd.tensor_tensor(factor[:, 0:2, :], slope[:], g1[:, HALF:T].unsqueeze(1).to_broadcast([P, 2, HALF]), MULT)
         def pair_for_scalar(e, number):
             values = sb.tile([P, 2 * C], F32, name="pair_%d" % e)
-            paired(values[:], [(t, e * C, (e + 1) * C) for t in (1, 2)], number, e)
+            gated(
+                values[:].rearrange("p (x j) -> p x j", x=2),
+                sums_of([(t, e * C, (e + 1) * C) for t in (1, 2)], number).rearrange("p (x j) -> p x j", x=2),
+                g2[:, e * C : (e + 1) * C].unsqueeze(1).to_broadcast([P, 2, C]),
+            )
             for x, t in enumerate((1, 2)):
                 scalar_scatter(dc[t], list2, e * C, (e + 1) * C, values[:, x * C : (x + 1) * C])
 
-        pair_for_scalar(1, 4)
-        products(0, HALF, T, 5, g2[:, HALF:T])
+        products(held.tile([P, P], F32, name="lead", offset=1024, align_bytes=64), 0, 0, P, 0, P)
+        for t in (1, 2):
+            products(sb.tile([P, C], F32, name="values_%d" % t), t, 0, C, t, C)
+        products(sb.tile([P, C], F32, name="values_0"), 0, P, HALF, 3, HALF)
+        dy_picked[1] = held.tile([P, HALF], U8, name="scales_tail", offset=1024, align_bytes=64)
+        gather_bytes(dy_picked[1][:], HALF, T)
+        words[2] = held.tile([P, C], U32, name="words_2", offset=1024 + HALF, align_bytes=64)
+        gather_words(words[2][:], 2 * C, T)
+        slope = sb.tile([P, PACK, HALF], F32, name="slope")
+        nc.vector.tensor_scalar(slope[:], a_late[:], 0.0, None, MAX)
+        w2_sorted[2] = held.tile([P, W], U32, name="w2_sorted_2", offset=2560, align_bytes=64)
+        nc.gpsimd.tensor_copy(w2_sorted[2][:].rearrange("p (t m) -> p t m", t=PACK), w2_third.rearrange("p m t -> p t m"))
+        w2_scales[2] = sort_scales(nc.gpsimd, w2_plane_rest, held.tile([P, W], U8, name="w2_scale_rest", offset=4608, align_bytes=64))[:]
+        factor_head = sb.tile([P, PACK, P], F32, name="factor_head", tag="factor_head", align_bytes=64)
+        factor_rest = sb.tile([P, PACK, C], F32, name="factor_rest")
+        for factor, lo, hi in ((factor_head, 0, P), (factor_rest, P, HALF)):
+            nc.gpsimd.tensor_tensor(
+                factor[:], slope[:, :, lo:hi], g1[:, HALF + lo : HALF + hi].unsqueeze(1).to_broadcast([P, PACK, hi - lo]), MULT
+            )
         whole = sb.tile([P, T], F32, name="whole")
-        for lo, hi, number in ((0, 2 * C, 6), (2 * C, T, 7)):
-            gated(whole[:, lo:hi], sums_of(((3, lo, hi),), number), g2[:, lo:hi])
+        gated(whole[:, 0 : 2 * C], sums_of(((3, 0, 2 * C),), 6), g2[:, 0 : 2 * C])
+        pair_for_scalar(1, 4)
+        vector_scatter(dc[3], list2, 0, 2 * C, whole[:, 0 : 2 * C])
+        gated(whole[:, 2 * C : T], sums_of(((3, 2 * C, T),), 7), g2[:, 2 * C : T])
+        last_values = sb.tile([P, HALF], F32, name="last_values")
+        products(last_values, 0, HALF, T, 5, T - SHIFT)
         pair_for_scalar(2, 0)
-        nc.vector.scalar_tensor_tensor(
-            factor[:, 2:, :], a_late[1][:], 0.0, g1[:, HALF:T].unsqueeze(1).to_broadcast([P, 2, HALF]), MAX, MULT
-        )
-        vector_scatter(dc[3], list2, 0, T, whole[:])
+        vector_scatter(dc[3], list2, 2 * C, T, whole[:, 2 * C : T])
+        vector_scatter(dc[0], list2, T - SHIFT, T, last_values[:, HALF - SHIFT : HALF])
 
         first = sb.tile([P, PACK, P], F32, name="first", tag="first", align_bytes=64)
         middle = sb.tile([P, PACK, C], F32, name="middle")
@@ -229,22 +220,20 @@ def tile_moe_seb_relu2_kernel(
                 h, a_early[:, :, lo:hi].rearrange("p t j -> p j t"), 0.0, values.rearrange("p t j -> p j t"), MAX, MULT
             )
 
-        def quantise(h, name):
-            width = h.shape[1]
-            codes = sb.tile([P, width], U32, name="codes_" + name, tag="codes_" + name, align_bytes=64)
-            plane = sb.tile([P, width], U8, name="plane_" + name, tag="plane_" + name, align_bytes=64)
+        def quantise(h, codes, name):
+            plane = sb.tile([P, h.shape[1]], U8, name="plane_" + name, tag="plane_" + name, align_bytes=64)
             nc.vector.quantize_mx(out=codes[:].bitcast(FP8X4), scales=plane[:], in_=h[:].rearrange("p j t -> p (j t)"))
             return codes, plane
 
-        def first_layer(quantised, lo, row_tiles, number):
+        def first_layer(quantised, lo, pieces, number):
             codes, plane = quantised
-            width = codes.shape[1]
             acc = bank(number)
-            for x, kb in enumerate(row_tiles):
-                for x0, x1 in cut(lo, lo + width, (C, 2 * C)):
+            at = 0
+            for kb, start, stop in pieces:
+                for x0, x1 in cut(start, stop, (C, 2 * C)):
                     e = x0 // C
                     nc.tensor.matmul_mx(
-                        out=acc[:, x * width + x0 - lo : x * width + x1 - lo],
+                        out=acc[:, at + x0 - start : at + x1 - start],
                         lhsT=w1[:, e, 2 * kb * P : 2 * (kb + 1) * P].bitcast(FP4X4),
                         lhsT_scale=w1_plane[:, e, kb * P : (kb + 1) * P],
                         rhs=codes[:, x0 - lo : x1 - lo].bitcast(FP8X4),
@@ -252,25 +241,16 @@ def tile_moe_seb_relu2_kernel(
                         start=True,
                         stop=True,
                     )
-            return acc[:, 0 : len(row_tiles) * width]
+                at += stop - start
+            return acc[:, 0:at]
 
         def copy_out(acc, name):
             sums = sb.tile([P, acc.shape[1]], F32, name=name)
             nc.vector.tensor_copy(sums[:], acc)
             return sums
 
-        dx = [sb.tile([P, WINDOW], F32, name="dx_%d" % kb) for kb in range(PACK)]
-
         def store(kb):
-            nc.sync.dma_start(out[kb * P : (kb + 1) * P, :], dx[kb][:, 0:T])
-
-        def weave_late(h, lo, hi):
-            nc.vector.tensor_tensor(
-                h[:, lo:hi, :].rearrange("p (c i) t -> p c t i", i=PACK),
-                picked[:, :, lo:hi].rearrange("p t (c i) -> p c t i", i=PACK),
-                factor[:, :, lo:hi].rearrange("p t (c i) -> p c t i", i=PACK),
-                MULT,
-            )
+            nc.sync.dma_start(out[kb * P : (kb + 1) * P, :], dx[kb][:])
 
         for t in (3, 0, 1):
             gather(first[:, t, :], t, 0, P)
@@ -283,28 +263,52 @@ def tile_moe_seb_relu2_kernel(
         h0 = sb.tile([P, P, PACK], BF16, name="h0", align_bytes=64)
         weave(h0[:], first[:], 0, P)
         nc.vector.tensor_copy(picked[:, 3, 0:P], dc[3][:].indirect(entries(list1, HALF, HALF + P)))
-        q0 = quantise(h0, "0")
+        q0 = quantise(h0, sb.tile([P, P], U32, name="codes_0", align_bytes=64), "0")
         h1 = sb.tile([P, C, PACK], BF16, name="h1", tag="first", align_bytes=64)
         weave(h1[:], middle[:], P, HALF)
+        dx = {kb: sb.tile([P, T], F32, name="dx_%d" % kb) for kb in (1, 2, 3)}
         sums = sb.tile([P, C], F32, name="s0_lead")
-        nc.scalar.copy(sums[:], first_layer(q0, 0, (1, 0), 7))
-        for x, kb in enumerate((1, 0)):
+        nc.scalar.copy(sums[:], first_layer(q0, 0, ((1, 0, P), (2, 0, P)), 7))
+        for x, kb in enumerate((1, 2)):
             scalar_scatter(dx[kb], list1, 0, P, sums[:, x * P : (x + 1) * P])
-        sums = copy_out(first_layer(q0, 0, (2, 3), 0), "s0_rest")
-        for x, kb in enumerate((2, 3)):
-            scalar_scatter(dx[kb], list1, 0, P, sums[:, x * P : (x + 1) * P])
-        q1 = quantise(h1, "1")
+        early = sb.tile([P, C + HALF], F32, name="early")
+        nc.vector.tensor_copy(early[:, 0:C], first_layer(q0, 0, ((3, 0, P), (0, 0, P)), 0))
+        scalar_scatter(dx[3], list1, 0, P, early[:, 0:P])
+        q1 = quantise(h1, held.tile([P, C], U32, name="codes_1", offset=8704, align_bytes=64), "1")
         h2 = sb.tile([P, HALF, PACK], BF16, name="h2", tag="plane_0", align_bytes=64)
-        weave_late(h2, 0, P)
-        s1_12 = copy_out(first_layer(q1, P, (1, 2), 1), "s1_12")
+        nc.vector.tensor_tensor(
+            h2[:, 0:P, :].rearrange("p (c i) t -> p c t i", i=PACK),
+            picked[:, :, 0:P].rearrange("p t (c i) -> p c t i", i=PACK),
+            factor_head[:].rearrange("p t (c i) -> p c t i", i=PACK),
+            MULT,
+        )
+        pairs = sb.tile([P, 2, C, 2], BF16, name="pairs", tag="factor_head", align_bytes=64)
+        nc.gpsimd.tensor_tensor(
+            pairs[:].rearrange("p u j e -> p u e j"),
+            picked[:, :, P:HALF].rearrange("p (u e) j -> p u e j", e=2),
+            factor_rest[:].rearrange("p (u e) j -> p u e j", e=2),
+            MULT,
+        )
+        s1_12 = copy_out(first_layer(q1, P, ((1, P, HALF), (2, P, HALF)), 1), "s1_12")
         for x, kb in enumerate((1, 2)):
             scalar_scatter(dx[kb], list1, P, HALF, s1_12[:, x * C : (x + 1) * C])
-        weave_late(h2, P, HALF)
-        s1_30 = copy_out(first_layer(q1, P, (3, 0), 2), "s1_30")
-        scalar_scatter(dx[3], list1, P, HALF, s1_30[:, 0:C])
-        q2 = quantise(h2, "2")
-        vector_scatter(dx[0], list1, P, HALF, s1_30[:, C : 2 * C])
-        tails = {kb: copy_out(first_layer(q2, HALF, (kb,), number), "s2_%d" % kb) for kb, number in ((0, 3), (2, 4), (3, 5), (1, 6))}
+        acc = first_layer(q1, P, ((0, P, C), (3, P, HALF), (0, C, HALF)), 2)
+        nc.vector.tensor_copy(early[:, C:], acc[:, 0:HALF])
+        scalar_scatter(dx[3], list1, P, HALF, early[:, HALF:])
+        dx[0] = held.tile([P, T], F32, name="dx_0", offset=8704, align_bytes=64)
+        vector_scatter(dx[0], list1, 0, C, early[:, P:HALF])
+        nc.vector.tensor_copy(
+            h2[:, P:HALF, :].rearrange("p j t -> p (j t)").bitcast(I32).rearrange("p (j u) -> p j u", u=2),
+            pairs[:].rearrange("p u j e -> p (u j e)").bitcast(I32).rearrange("p (u j) -> p j u", u=2),
+        )
+        filler = sb.tile([P, P], F32, name="filler", tag="factor_head", align_bytes=64)
+        nc.vector.tensor_copy(filler[:], acc[:, HALF:])
+        q2 = quantise(h2, sb.tile([P, HALF], U32, name="codes_2", align_bytes=64), "2")
+        vector_scatter(dx[0], list1, C, HALF, filler[:])
+        tails = {kb: sb.tile([P, HALF], F32, name="s2_%d" % kb) for kb in range(PACK)}
+        for kb, number in ((0, 3), (1, 4), (2, 5), (3, 6)):
+            copy = nc.vector.tensor_copy if kb < 2 else nc.scalar.copy
+            copy(tails[kb][:], first_layer(q2, HALF, ((kb, HALF, T),), number))
         vector_scatter(dx[0], list1, HALF, T, tails[0][:])
         store(0)
         scalar_scatter(dx[2], list1, HALF, T, tails[2][:])

@@ -13,6 +13,7 @@ FP4X4 = mybir.dt.float4_e2m1fn_x4
 COPY = mybir.ActivationFunctionType.Copy
 MULT = mybir.AluOpType.mult
 MAX = mybir.AluOpType.max
+MIN = mybir.AluOpType.min
 
 P = 128
 PACK = 4
@@ -21,7 +22,7 @@ E = 3
 C = 256
 W = 512
 QUADRANTS = 4
-SHIFT = 96
+SHIFT = 128
 HALF = T // 2
 FLOPS = 2 * 2 * W * W * T
 DY_ROW = 4
@@ -78,14 +79,14 @@ def tile_moe_seb_relu2_kernel(
         g2 = sb.tile([P, T], F32, name="g2")
         nc.sync.dma_start(g2[:, 0:HALF], gate2[:, 0:HALF])
         a_rows = a.rearrange("(p t) j -> p t j", t=PACK)
-        a_late = held.tile([P, PACK, HALF], F32, name="a_late", offset=2560, align_bytes=64)
-        nc.sync.dma_start(a_late[:], a_rows[:, :, HALF:T])
-        nc.sync.dma_start(g2[:, HALF:T], gate2[:, HALF:T])
         w2_third = load_w2(2)
+        nc.sync.dma_start(g2[:, HALF:T], gate2[:, HALF:T])
         for q in range(QUADRANTS):
             nc.sync.dma_start(
                 w2_plane_rest[:].bitcast(I32)[32 * q : 32 * q + 4, :], w2t_scales[2, 0, 4 * q : 4 * q + 4, :].bitcast(I32)
             )
+        a_late = sb.tile([P, PACK, HALF], F32, name="a_late")
+        nc.sync.dma_start(a_late[:], a_rows[:, :, HALF:T])
         g1 = sb.tile([P, T], F32, name="g1")
         nc.sync.dma_start(g1[:], gate1)
         a_early = sb.tile([P, PACK, HALF], F32, name="a_early")
@@ -165,33 +166,34 @@ def tile_moe_seb_relu2_kernel(
 
         dc = [sb.tile([P, T], F32, name="dc_%d" % t) for t in range(PACK)]
 
-        def products(values, t, lo, hi, number, stop):
+        def products(values, t, lo, hi, number):
             gated(values[:], sums_of(((t, lo, hi),), number), g2[:, lo:hi])
-            scalar_scatter(dc[t], list2, lo, stop, values[:, 0 : stop - lo])
+            return values
 
-        def pair_for_scalar(e, number):
-            values = sb.tile([P, 2 * C], F32, name="pair_%d" % e)
+        def paired(e, number):
+            values = sb.tile([P, 2, C], F32, name="pair_%d" % e)
             gated(
-                values[:].rearrange("p (x j) -> p x j", x=2),
+                values[:],
                 sums_of([(t, e * C, (e + 1) * C) for t in (1, 2)], number).rearrange("p (x j) -> p x j", x=2),
                 g2[:, e * C : (e + 1) * C].unsqueeze(1).to_broadcast([P, 2, C]),
             )
-            for x, t in enumerate((1, 2)):
-                scalar_scatter(dc[t], list2, e * C, (e + 1) * C, values[:, x * C : (x + 1) * C])
+            return values
 
-        products(held.tile([P, P], F32, name="lead", offset=1024, align_bytes=64), 0, 0, P, 0, P)
-        for t in (1, 2):
-            products(sb.tile([P, C], F32, name="values_%d" % t), t, 0, C, t, C)
-        products(sb.tile([P, C], F32, name="values_0"), 0, P, HALF, 3, HALF)
+        lead = held.tile([P, P], F32, name="lead", offset=1024, align_bytes=64)
+        scalar_scatter(dc[0], list2, 0, P, products(lead, 0, 0, P, 0)[:])
+        second = held.tile([P, C], F32, name="second", offset=2560, align_bytes=64)
+        scalar_scatter(dc[1], list2, 0, C, products(second, 1, 0, C, 1)[:])
+        scalar_scatter(dc[2], list2, 0, C, products(sb.tile([P, C], F32, name="third"), 2, 0, C, 2)[:])
+        scalar_scatter(dc[0], list2, P, HALF, products(sb.tile([P, C], F32, name="fourth"), 0, P, HALF, 3)[:])
         dy_picked[1] = held.tile([P, HALF], U8, name="scales_tail", offset=1024, align_bytes=64)
         gather_bytes(dy_picked[1][:], HALF, T)
         words[2] = held.tile([P, C], U32, name="words_2", offset=1024 + HALF, align_bytes=64)
         gather_words(words[2][:], 2 * C, T)
-        slope = sb.tile([P, PACK, HALF], F32, name="slope")
-        nc.vector.tensor_scalar(slope[:], a_late[:], 0.0, None, MAX)
         w2_sorted[2] = held.tile([P, W], U32, name="w2_sorted_2", offset=2560, align_bytes=64)
         nc.gpsimd.tensor_copy(w2_sorted[2][:].rearrange("p (t m) -> p t m", t=PACK), w2_third.rearrange("p m t -> p t m"))
-        w2_scales[2] = sort_scales(nc.gpsimd, w2_plane_rest, held.tile([P, W], U8, name="w2_scale_rest", offset=4608, align_bytes=64))[:]
+        w2_scales[2] = sort_scales(nc.gpsimd, w2_plane_rest, sb.tile([P, W], U8, name="w2_scale_rest", align_bytes=64))[:]
+        slope = sb.tile([P, PACK, HALF], F32, name="slope")
+        nc.gpsimd.tensor_scalar(slope[:], a_late[:], float("inf"), 0.0, MIN, MAX)
         factor_head = sb.tile([P, PACK, P], F32, name="factor_head", tag="factor_head", align_bytes=64)
         factor_rest = sb.tile([P, PACK, C], F32, name="factor_rest")
         for factor, lo, hi in ((factor_head, 0, P), (factor_rest, P, HALF)):
@@ -199,15 +201,19 @@ def tile_moe_seb_relu2_kernel(
                 factor[:], slope[:, :, lo:hi], g1[:, HALF + lo : HALF + hi].unsqueeze(1).to_broadcast([P, PACK, hi - lo]), MULT
             )
         whole = sb.tile([P, T], F32, name="whole")
-        gated(whole[:, 0 : 2 * C], sums_of(((3, 0, 2 * C),), 6), g2[:, 0 : 2 * C])
-        pair_for_scalar(1, 4)
+        products(whole[:, 0 : 2 * C], 3, 0, 2 * C, 6)
+        values = paired(1, 4)
+        for x, t in enumerate((1, 2)):
+            scalar_scatter(dc[t], list2, C, 2 * C, values[:, x, :])
         vector_scatter(dc[3], list2, 0, 2 * C, whole[:, 0 : 2 * C])
-        gated(whole[:, 2 * C : T], sums_of(((3, 2 * C, T),), 7), g2[:, 2 * C : T])
-        last_values = sb.tile([P, HALF], F32, name="last_values")
-        products(last_values, 0, HALF, T, 5, T - SHIFT)
-        pair_for_scalar(2, 0)
+        values = paired(2, 0)
+        last = products(sb.tile([P, HALF], F32, name="last"), 0, HALF, T, 5)
+        products(whole[:, 2 * C : T], 3, 2 * C, T, 7)
+        vector_scatter(dc[0], list2, HALF, HALF + SHIFT, last[:, 0:SHIFT])
         vector_scatter(dc[3], list2, 2 * C, T, whole[:, 2 * C : T])
-        vector_scatter(dc[0], list2, T - SHIFT, T, last_values[:, HALF - SHIFT : HALF])
+        for x, t in enumerate((1, 2)):
+            scalar_scatter(dc[t], list2, 2 * C, T, values[:, x, :])
+        scalar_scatter(dc[0], list2, HALF + SHIFT, T, last[:, SHIFT:HALF])
 
         first = sb.tile([P, PACK, P], F32, name="first", tag="first", align_bytes=64)
         middle = sb.tile([P, PACK, C], F32, name="middle")
@@ -252,14 +258,14 @@ def tile_moe_seb_relu2_kernel(
         def store(kb):
             nc.sync.dma_start(out[kb * P : (kb + 1) * P, :], dx[kb][:])
 
-        for t in (3, 0, 1):
+        for t in (1, 3, 2):
             gather(first[:, t, :], t, 0, P)
             gather(middle[:, t, :], t, P, HALF)
         picked = sb.tile([P, PACK, HALF], F32, name="picked")
-        for t, lo in ((3, HALF + P), (0, HALF), (1, HALF), (2, HALF)):
+        for t, lo in ((3, HALF + P), (1, HALF), (2, HALF), (0, HALF)):
             nc.scalar.activation(picked[:, t, lo - HALF :], dc[t][:].indirect(entries(list1, lo, T)), COPY)
-        gather(first[:, 2, :], 2, 0, P)
-        gather(middle[:, 2, :], 2, P, HALF)
+        gather(first[:, 0, :], 0, 0, P)
+        gather(middle[:, 0, :], 0, P, HALF)
         h0 = sb.tile([P, P, PACK], BF16, name="h0", align_bytes=64)
         weave(h0[:], first[:], 0, P)
         nc.vector.tensor_copy(picked[:, 3, 0:P], dc[3][:].indirect(entries(list1, HALF, HALF + P)))

@@ -22,7 +22,7 @@ E = 3
 C = 256
 W = 512
 QUADRANTS = 4
-SHIFT = 128
+SHIFT = 224
 HALF = T // 2
 FLOPS = 2 * 2 * W * W * T
 DY_ROW = 4
@@ -85,12 +85,12 @@ def tile_moe_seb_relu2_kernel(
             nc.sync.dma_start(
                 w2_plane_rest[:].bitcast(I32)[32 * q : 32 * q + 4, :], w2t_scales[2, 0, 4 * q : 4 * q + 4, :].bitcast(I32)
             )
-        a_late = sb.tile([P, PACK, HALF], F32, name="a_late")
-        nc.sync.dma_start(a_late[:], a_rows[:, :, HALF:T])
+        a_late = sb.tile([P, PACK, 2 * C], F32, name="a_late")
+        nc.sync.dma_start(a_late[:], a_rows[:, :, C:T])
         g1 = sb.tile([P, T], F32, name="g1")
         nc.sync.dma_start(g1[:], gate1)
-        a_early = sb.tile([P, PACK, HALF], F32, name="a_early")
-        nc.sync.dma_start(a_early[:], a_rows[:, :, 0:HALF])
+        a_early = sb.tile([P, PACK, C], F32, name="a_early")
+        nc.sync.dma_start(a_early[:], a_rows[:, :, 0:C])
         for q in range(QUADRANTS):
             nc.sync.dma_start(
                 w1_plane[:].bitcast(I32)[32 * q : 32 * q + 4, :, :],
@@ -192,13 +192,12 @@ def tile_moe_seb_relu2_kernel(
         w2_sorted[2] = held.tile([P, W], U32, name="w2_sorted_2", offset=2560, align_bytes=64)
         nc.gpsimd.tensor_copy(w2_sorted[2][:].rearrange("p (t m) -> p t m", t=PACK), w2_third.rearrange("p m t -> p t m"))
         w2_scales[2] = sort_scales(nc.gpsimd, w2_plane_rest, sb.tile([P, W], U8, name="w2_scale_rest", align_bytes=64))[:]
-        slope = sb.tile([P, PACK, HALF], F32, name="slope")
+        slope = sb.tile([P, PACK, 2 * C], F32, name="slope")
         nc.gpsimd.tensor_scalar(slope[:], a_late[:], float("inf"), 0.0, MIN, MAX)
-        factor_head = sb.tile([P, PACK, P], F32, name="factor_head", tag="factor_head", align_bytes=64)
-        factor_rest = sb.tile([P, PACK, C], F32, name="factor_rest")
-        for factor, lo, hi in ((factor_head, 0, P), (factor_rest, P, HALF)):
+        factor = {e: sb.tile([P, PACK, C], F32, name="factor_%d" % e) for e in (1, 2)}
+        for e in (1, 2):
             nc.gpsimd.tensor_tensor(
-                factor[:], slope[:, :, lo:hi], g1[:, HALF + lo : HALF + hi].unsqueeze(1).to_broadcast([P, PACK, hi - lo]), MULT
+                factor[e][:], slope[:, :, (e - 1) * C : e * C], g1[:, e * C : (e + 1) * C].unsqueeze(1).to_broadcast([P, PACK, C]), MULT
             )
         whole = sb.tile([P, T], F32, name="whole")
         products(whole[:, 0 : 2 * C], 3, 0, 2 * C, 6)
@@ -215,111 +214,110 @@ def tile_moe_seb_relu2_kernel(
             scalar_scatter(dc[t], list2, 2 * C, T, values[:, x, :])
         scalar_scatter(dc[0], list2, HALF + SHIFT, T, last[:, SHIFT:HALF])
 
-        first = sb.tile([P, PACK, P], F32, name="first", tag="first", align_bytes=64)
-        middle = sb.tile([P, PACK, C], F32, name="middle")
-
         def gather(into, t, lo, hi):
             nc.vector.tensor_tensor(into, dc[t][:].indirect(entries(list1, lo, hi)), g1[:, lo:hi], MULT)
 
-        def weave(h, values, lo, hi):
-            nc.vector.scalar_tensor_tensor(
-                h, a_early[:, :, lo:hi].rearrange("p t j -> p j t"), 0.0, values.rearrange("p t j -> p j t"), MAX, MULT
-            )
+        def quantise(h, codes, plane):
+            nc.vector.quantize_mx(out=codes.bitcast(FP8X4), scales=plane, in_=h.rearrange("p j t -> p (j t)"))
 
-        def quantise(h, codes, name):
-            plane = sb.tile([P, h.shape[1]], U8, name="plane_" + name, tag="plane_" + name, align_bytes=64)
-            nc.vector.quantize_mx(out=codes[:].bitcast(FP8X4), scales=plane[:], in_=h[:].rearrange("p j t -> p (j t)"))
-            return codes, plane
+        codes = [sb.tile([P, C], U32, name="codes_%d" % e, align_bytes=64) for e in range(E)]
+        planes = [sb.tile([P, C], U8, name="plane_%d" % e, align_bytes=64) for e in range(E)]
 
-        def first_layer(quantised, lo, pieces, number):
-            codes, plane = quantised
+        def first_layer(e, row_tiles, number):
             acc = bank(number)
-            at = 0
-            for kb, start, stop in pieces:
-                for x0, x1 in cut(start, stop, (C, 2 * C)):
-                    e = x0 // C
-                    nc.tensor.matmul_mx(
-                        out=acc[:, at + x0 - start : at + x1 - start],
-                        lhsT=w1[:, e, 2 * kb * P : 2 * (kb + 1) * P].bitcast(FP4X4),
-                        lhsT_scale=w1_plane[:, e, kb * P : (kb + 1) * P],
-                        rhs=codes[:, x0 - lo : x1 - lo].bitcast(FP8X4),
-                        rhs_scale=plane[:, x0 - lo : x1 - lo],
-                        start=True,
-                        stop=True,
-                    )
-                at += stop - start
-            return acc[:, 0:at]
+            for x, kb in enumerate(row_tiles):
+                nc.tensor.matmul_mx(
+                    out=acc[:, x * C : (x + 1) * C],
+                    lhsT=w1[:, e, 2 * kb * P : 2 * (kb + 1) * P].bitcast(FP4X4),
+                    lhsT_scale=w1_plane[:, e, kb * P : (kb + 1) * P],
+                    rhs=codes[e][:].bitcast(FP8X4),
+                    rhs_scale=planes[e][:],
+                    start=True,
+                    stop=True,
+                )
+            return acc
 
-        def copy_out(acc, name):
-            sums = sb.tile([P, acc.shape[1]], F32, name=name)
-            nc.vector.tensor_copy(sums[:], acc)
+        def copy_out(copy, acc, name, tag=None):
+            sums = sb.tile([P, acc.shape[1]], F32, name=name, tag=tag or name, align_bytes=64)
+            copy(sums[:], acc)
             return sums
+
+        def multiply(picked, e, tag):
+            pairs = sb.tile([P, 2, C, 2], BF16, name="pairs_%d" % e, tag=tag, align_bytes=64)
+            nc.gpsimd.tensor_tensor(
+                pairs[:].rearrange("p u j e -> p u e j"),
+                picked[:].rearrange("p (u e) j -> p u e j", e=2),
+                factor[e][:].rearrange("p (u e) j -> p u e j", e=2),
+                MULT,
+            )
+            return pairs
+
+        def weave_words(pairs, name):
+            h = sb.tile([P, C, PACK], BF16, name=name, tag=name, align_bytes=64)
+            nc.vector.tensor_copy(
+                h[:].rearrange("p j t -> p (j t)").bitcast(I32).rearrange("p (j u) -> p j u", u=2),
+                pairs[:].rearrange("p u j e -> p (u j e)").bitcast(I32).rearrange("p (u j) -> p j u", u=2),
+            )
+            return h
+
+        dx = [sb.tile([P, T], F32, name="dx_%d" % kb) for kb in range(PACK)]
 
         def store(kb):
             nc.sync.dma_start(out[kb * P : (kb + 1) * P, :], dx[kb][:])
 
+        first = sb.tile([P, PACK, C], F32, name="first", tag="first", align_bytes=64)
         for t in (1, 3, 2):
-            gather(first[:, t, :], t, 0, P)
-            gather(middle[:, t, :], t, P, HALF)
-        picked = sb.tile([P, PACK, HALF], F32, name="picked")
-        for t, lo in ((3, HALF + P), (1, HALF), (2, HALF), (0, HALF)):
-            nc.scalar.activation(picked[:, t, lo - HALF :], dc[t][:].indirect(entries(list1, lo, T)), COPY)
-        gather(first[:, 0, :], 0, 0, P)
-        gather(middle[:, 0, :], 0, P, HALF)
-        h0 = sb.tile([P, P, PACK], BF16, name="h0", align_bytes=64)
-        weave(h0[:], first[:], 0, P)
-        nc.vector.tensor_copy(picked[:, 3, 0:P], dc[3][:].indirect(entries(list1, HALF, HALF + P)))
-        q0 = quantise(h0, sb.tile([P, P], U32, name="codes_0", align_bytes=64), "0")
-        h1 = sb.tile([P, C, PACK], BF16, name="h1", tag="first", align_bytes=64)
-        weave(h1[:], middle[:], P, HALF)
-        dx = {kb: sb.tile([P, T], F32, name="dx_%d" % kb) for kb in (1, 2, 3)}
-        sums = sb.tile([P, C], F32, name="s0_lead")
-        nc.scalar.copy(sums[:], first_layer(q0, 0, ((1, 0, P), (2, 0, P)), 7))
-        for x, kb in enumerate((1, 2)):
-            scalar_scatter(dx[kb], list1, 0, P, sums[:, x * P : (x + 1) * P])
-        early = sb.tile([P, C + HALF], F32, name="early")
-        nc.vector.tensor_copy(early[:, 0:C], first_layer(q0, 0, ((3, 0, P), (0, 0, P)), 0))
-        scalar_scatter(dx[3], list1, 0, P, early[:, 0:P])
-        q1 = quantise(h1, held.tile([P, C], U32, name="codes_1", offset=8704, align_bytes=64), "1")
-        h2 = sb.tile([P, HALF, PACK], BF16, name="h2", tag="plane_0", align_bytes=64)
-        nc.vector.tensor_tensor(
-            h2[:, 0:P, :].rearrange("p (c i) t -> p c t i", i=PACK),
-            picked[:, :, 0:P].rearrange("p t (c i) -> p c t i", i=PACK),
-            factor_head[:].rearrange("p t (c i) -> p c t i", i=PACK),
-            MULT,
-        )
-        pairs = sb.tile([P, 2, C, 2], BF16, name="pairs", tag="factor_head", align_bytes=64)
-        nc.gpsimd.tensor_tensor(
-            pairs[:].rearrange("p u j e -> p u e j"),
-            picked[:, :, P:HALF].rearrange("p (u e) j -> p u e j", e=2),
-            factor_rest[:].rearrange("p (u e) j -> p u e j", e=2),
-            MULT,
-        )
-        s1_12 = copy_out(first_layer(q1, P, ((1, P, HALF), (2, P, HALF)), 1), "s1_12")
-        for x, kb in enumerate((1, 2)):
-            scalar_scatter(dx[kb], list1, P, HALF, s1_12[:, x * C : (x + 1) * C])
-        acc = first_layer(q1, P, ((0, P, C), (3, P, HALF), (0, C, HALF)), 2)
-        nc.vector.tensor_copy(early[:, C:], acc[:, 0:HALF])
-        scalar_scatter(dx[3], list1, P, HALF, early[:, HALF:])
-        dx[0] = held.tile([P, T], F32, name="dx_0", offset=8704, align_bytes=64)
-        vector_scatter(dx[0], list1, 0, C, early[:, P:HALF])
-        nc.vector.tensor_copy(
-            h2[:, P:HALF, :].rearrange("p j t -> p (j t)").bitcast(I32).rearrange("p (j u) -> p j u", u=2),
-            pairs[:].rearrange("p u j e -> p (u j e)").bitcast(I32).rearrange("p (u j) -> p j u", u=2),
-        )
-        filler = sb.tile([P, P], F32, name="filler", tag="factor_head", align_bytes=64)
-        nc.vector.tensor_copy(filler[:], acc[:, HALF:])
-        q2 = quantise(h2, sb.tile([P, HALF], U32, name="codes_2", align_bytes=64), "2")
-        vector_scatter(dx[0], list1, C, HALF, filler[:])
-        tails = {kb: sb.tile([P, HALF], F32, name="s2_%d" % kb) for kb in range(PACK)}
-        for kb, number in ((0, 3), (1, 4), (2, 5), (3, 6)):
-            copy = nc.vector.tensor_copy if kb < 2 else nc.scalar.copy
-            copy(tails[kb][:], first_layer(q2, HALF, ((kb, HALF, T),), number))
-        vector_scatter(dx[0], list1, HALF, T, tails[0][:])
-        store(0)
-        scalar_scatter(dx[2], list1, HALF, T, tails[2][:])
-        store(2)
-        vector_scatter(dx[1], list1, HALF, T, tails[1][:])
-        store(1)
-        scalar_scatter(dx[3], list1, HALF, T, tails[3][:])
-        store(3)
+            gather(first[:, t, :], t, 0, C)
+        picked_1 = sb.tile([P, PACK, C], F32, name="picked_1")
+        for t in (1, 3, 2, 0):
+            nc.scalar.activation(picked_1[:, t, :], dc[t][:].indirect(entries(list1, C, 2 * C)), COPY)
+        h0 = sb.tile([P, C, PACK], BF16, name="h0", tag="h0", align_bytes=64)
+        for lo in (0, P):
+            gather(first[:, 0, lo : lo + P], 0, lo, lo + P)
+        for lo in (0, P):
+            nc.vector.scalar_tensor_tensor(
+                h0[:, lo : lo + P, :],
+                a_early[:, :, lo : lo + P].rearrange("p t j -> p j t"),
+                0.0,
+                first[:, :, lo : lo + P].rearrange("p t j -> p j t"),
+                MAX,
+                MULT,
+            )
+        for lo in (0, P):
+            quantise(h0[:, lo : lo + P, :], codes[0][:, lo : lo + P], planes[0][:, lo : lo + P])
+        picked_2 = sb.tile([P, PACK, C], F32, name="picked_2", tag="first", align_bytes=64)
+        nc.vector.tensor_copy(picked_2[:, 0, :], dc[0][:].indirect(entries(list1, 2 * C, T)))
+        for t in (1, 3, 2):
+            nc.scalar.activation(picked_2[:, t, :], dc[t][:].indirect(entries(list1, 2 * C, T)), COPY)
+        pairs = multiply(picked_1, 1, "h0")
+        acc = first_layer(0, (1, 0), 0)
+        s0_low = copy_out(nc.vector.tensor_copy, acc[:, 0:HALF], "s0_low")
+        s0_high = copy_out(nc.vector.tensor_copy, first_layer(0, (2, 3), 7)[:], "s0_high")
+        scalar_scatter(dx[1], list1, 0, C, s0_low[:, 0:C])
+        for x, kb in enumerate((2, 3)):
+            scalar_scatter(dx[kb], list1, 0, C, s0_high[:, x * C : (x + 1) * C])
+        vector_scatter(dx[0], list1, 0, P, s0_low[:, C:HALF])
+        h1 = weave_words(pairs, "h1")
+        s0_rest = copy_out(nc.vector.tensor_copy, acc[:, HALF:W], "s0_rest", "h0")
+        quantise(h1[:], codes[1][:], planes[1][:])
+        pairs = multiply(picked_2, 2, "h1")
+        vector_scatter(dx[0], list1, P, C, s0_rest[:])
+        acc = first_layer(1, (0, 1), 1)
+        s1_0 = copy_out(nc.vector.tensor_copy, acc[:, 0:C], "s1_0")
+        s1_high = copy_out(nc.vector.tensor_copy, first_layer(1, (2, 3), 2)[:], "s1_high")
+        for x, kb in enumerate((2, 3)):
+            scalar_scatter(dx[kb], list1, C, 2 * C, s1_high[:, x * C : (x + 1) * C])
+        vector_scatter(dx[0], list1, C, 2 * C, s1_0[:])
+        h2 = weave_words(pairs, "h2")
+        s1_1 = copy_out(nc.vector.tensor_copy, acc[:, C:W], "s1_1", "h1")
+        quantise(h2[:], codes[2][:], planes[2][:])
+        vector_scatter(dx[1], list1, C, HALF, s1_1[:, 0:P])
+        scalar_scatter(dx[1], list1, HALF, 2 * C, s1_1[:, P:C])
+        tails = [
+            copy_out(nc.vector.tensor_copy if kb < 2 else nc.scalar.copy, first_layer(2, (kb,), 3 + kb)[:, 0:C], "s2_%d" % kb)
+            for kb in range(PACK)
+        ]
+        for kb in (0, 2, 1, 3):
+            scatter = vector_scatter if kb < 2 else scalar_scatter
+            scatter(dx[kb], list1, 2 * C, T, tails[kb][:])
+            store(kb)

@@ -49,7 +49,7 @@ def tile_moe_seb_relu2_kernel(
             return lst[:, lo // 16 : hi // 16]
 
         dy_plane = sb.tile([P, T], U8, name="dy_plane", align_bytes=64)
-        w2_plane = held.tile([P, W], U8, name="w2_plane", offset=0, align_bytes=64)
+        w2_plane = sb.tile([P, W], U8, name="w2_plane", align_bytes=64)
         w2_plane_rest = sb.tile([P, W], U8, name="w2_plane_rest", align_bytes=64)
         w1_plane = sb.tile([P, E, W], U8, name="w1_plane", align_bytes=64)
         nc.gpsimd.memset(dy_plane[:].bitcast(I32), 0)
@@ -75,9 +75,9 @@ def tile_moe_seb_relu2_kernel(
         for q in range(QUADRANTS):
             queue = nc.scalar if q == 0 else nc.sync
             queue.dma_start(w2_plane[:].bitcast(I32)[32 * q : 32 * q + 8, :], w2t_scales[0:2, 0, 4 * q : 4 * q + 4, :].bitcast(I32))
-        w2_second = load_w2(1)
         g2 = sb.tile([P, T], F32, name="g2")
         nc.sync.dma_start(g2[:, 0:HALF], gate2[:, 0:HALF])
+        w2_second = load_w2(1)
         a_rows = a.rearrange("(p t) j -> p t j", t=PACK)
         w2_third = load_w2(2)
         nc.sync.dma_start(g2[:, HALF:T], gate2[:, HALF:T])
@@ -135,15 +135,19 @@ def tile_moe_seb_relu2_kernel(
         nc.scalar.copy(w2_lead[:], w2_first[:, :, 0])
         w2_sorted = {e: sb.tile([P, W], U32, name="w2_sorted_%d" % e, align_bytes=64) for e in range(2)}
         nc.scalar.copy(w2_sorted[0][:].rearrange("p (t m) -> p m t", t=PACK)[:, :, 1:], w2_first[:, :, 1:])
-        nc.scalar.copy(w2_sorted[1][:].rearrange("p (t m) -> p m t", t=PACK), w2_second)
         scales_head = sb.tile([P, HALF], U8, name="scales_head", align_bytes=64)
         gather_bytes(scales_head[:], 0, HALF)
         words = {0: sb.tile([P, C], U32, name="words_0", align_bytes=64)}
         gather_words(words[0][:, 0:P], 0, P)
         gather_words(words[0][:, P:C], P, C)
-        w2_scale_head = sort_scales(nc.vector, w2_plane, sb.tile([P, W], U8, name="w2_scale_head", align_bytes=64))
+        by_plane = w2_plane[:].rearrange("p (m t) -> p t m", t=PACK)
+        scale_lead = sb.tile([P, P], U8, name="scale_lead", align_bytes=64)
+        nc.gpsimd.tensor_copy(scale_lead[:], by_plane[:, 0, :])
+        w2_scale_head = sb.tile([P, W], U8, name="w2_scale_head", align_bytes=64)
+        nc.gpsimd.tensor_copy(w2_scale_head[:].rearrange("p (t m) -> p t m", t=PACK)[:, 1:, :], by_plane[:, 1:, :])
+        nc.gpsimd.tensor_copy(w2_sorted[1][:].rearrange("p (t m) -> p t m", t=PACK), w2_second.rearrange("p m t -> p t m"))
         w2_scales = {0: w2_scale_head[:], 1: w2_scale_head[4:P, :]}
-        words[1] = held.tile([P, C], U32, name="words_1", offset=0, align_bytes=64)
+        words[1] = sb.tile([P, C], U32, name="words_1", align_bytes=64)
         gather_words(words[1][:], C, 2 * C)
         dy_picked = {0: scales_head}
 
@@ -156,7 +160,7 @@ def tile_moe_seb_relu2_kernel(
                     second_layer(
                         acc[:, at + x0 - lo : at + x1 - lo],
                         w2_lead if (e, t) == (0, 0) else w2_sorted[e],
-                        w2_scales[e],
+                        scale_lead[4 * e : P, :] if t == 0 and e < 2 else w2_scales[e],
                         t,
                         words[e][:, x0 - e * C : x1 - e * C],
                         dy_picked[half][DY_ROW:P, x0 - half * HALF : x1 - half * HALF],
@@ -164,7 +168,7 @@ def tile_moe_seb_relu2_kernel(
                 at += hi - lo
             return acc[:, 0:at]
 
-        dc = [sb.tile([P, T], F32, name="dc_%d" % t) for t in range(PACK)]
+        dc = [sb.tile([P, 4 * C], F32, name="dc_%d" % t) for t in range(PACK)]
 
         def products(values, t, lo, hi, number):
             gated(values[:], sums_of(((t, lo, hi),), number), g2[:, lo:hi])
@@ -181,7 +185,7 @@ def tile_moe_seb_relu2_kernel(
 
         lead = held.tile([P, P], F32, name="lead", offset=1024, align_bytes=64)
         scalar_scatter(dc[0], list2, 0, P, products(lead, 0, 0, P, 0)[:])
-        second = held.tile([P, C], F32, name="second", offset=2560, align_bytes=64)
+        second = sb.tile([P, C], F32, name="second")
         scalar_scatter(dc[1], list2, 0, C, products(second, 1, 0, C, 1)[:])
         scalar_scatter(dc[2], list2, 0, C, products(sb.tile([P, C], F32, name="third"), 2, 0, C, 2)[:])
         scalar_scatter(dc[0], list2, P, HALF, products(sb.tile([P, C], F32, name="fourth"), 0, P, HALF, 3)[:])
@@ -189,7 +193,7 @@ def tile_moe_seb_relu2_kernel(
         gather_bytes(dy_picked[1][:], HALF, T)
         words[2] = held.tile([P, C], U32, name="words_2", offset=1024 + HALF, align_bytes=64)
         gather_words(words[2][:], 2 * C, T)
-        w2_sorted[2] = held.tile([P, W], U32, name="w2_sorted_2", offset=2560, align_bytes=64)
+        w2_sorted[2] = sb.tile([P, W], U32, name="w2_sorted_2", align_bytes=64)
         nc.gpsimd.tensor_copy(w2_sorted[2][:].rearrange("p (t m) -> p t m", t=PACK), w2_third.rearrange("p m t -> p t m"))
         w2_scales[2] = sort_scales(nc.gpsimd, w2_plane_rest, sb.tile([P, W], U8, name="w2_scale_rest", align_bytes=64))[:]
         slope = sb.tile([P, PACK, 2 * C], F32, name="slope")
@@ -200,16 +204,15 @@ def tile_moe_seb_relu2_kernel(
                 factor[e][:], slope[:, :, (e - 1) * C : e * C], g1[:, e * C : (e + 1) * C].unsqueeze(1).to_broadcast([P, PACK, C]), MULT
             )
         whole = sb.tile([P, T], F32, name="whole")
-        products(whole[:, 0 : 2 * C], 3, 0, 2 * C, 6)
         values = paired(1, 4)
         for x, t in enumerate((1, 2)):
             scalar_scatter(dc[t], list2, C, 2 * C, values[:, x, :])
-        vector_scatter(dc[3], list2, 0, 2 * C, whole[:, 0 : 2 * C])
-        values = paired(2, 0)
-        last = products(sb.tile([P, HALF], F32, name="last"), 0, HALF, T, 5)
+        products(whole[:, 0 : 2 * C], 3, 0, 2 * C, 6)
         products(whole[:, 2 * C : T], 3, 2 * C, T, 7)
+        last = products(sb.tile([P, HALF], F32, name="last"), 0, HALF, T, 5)
+        values = paired(2, 0)
+        vector_scatter(dc[3], list2, 0, T, whole[:])
         vector_scatter(dc[0], list2, HALF, HALF + SHIFT, last[:, 0:SHIFT])
-        vector_scatter(dc[3], list2, 2 * C, T, whole[:, 2 * C : T])
         for x, t in enumerate((1, 2)):
             scalar_scatter(dc[t], list2, 2 * C, T, values[:, x, :])
         scalar_scatter(dc[0], list2, HALF + SHIFT, T, last[:, SHIFT:HALF])

@@ -168,7 +168,7 @@ def tile_moe_seb_relu2_kernel(
                 at += hi - lo
             return acc[:, 0:at]
 
-        dc = [sb.tile([P, 4 * C], F32, name="dc_%d" % t) for t in range(PACK)]
+        dc = [sb.tile([P, T], F32, name="dc_%d" % t) for t in range(PACK)]
 
         def products(values, t, lo, hi, number):
             gated(values[:], sums_of(((t, lo, hi),), number), g2[:, lo:hi])
@@ -204,15 +204,16 @@ def tile_moe_seb_relu2_kernel(
                 factor[e][:], slope[:, :, (e - 1) * C : e * C], g1[:, e * C : (e + 1) * C].unsqueeze(1).to_broadcast([P, PACK, C]), MULT
             )
         whole = sb.tile([P, T], F32, name="whole")
+        products(whole[:, 0 : 2 * C], 3, 0, 2 * C, 6)
         values = paired(1, 4)
         for x, t in enumerate((1, 2)):
             scalar_scatter(dc[t], list2, C, 2 * C, values[:, x, :])
-        products(whole[:, 0 : 2 * C], 3, 0, 2 * C, 6)
-        products(whole[:, 2 * C : T], 3, 2 * C, T, 7)
-        last = products(sb.tile([P, HALF], F32, name="last"), 0, HALF, T, 5)
+        vector_scatter(dc[3], list2, 0, 2 * C, whole[:, 0 : 2 * C])
         values = paired(2, 0)
-        vector_scatter(dc[3], list2, 0, T, whole[:])
+        last = products(sb.tile([P, HALF], F32, name="last"), 0, HALF, T, 5)
+        products(whole[:, 2 * C : T], 3, 2 * C, T, 7)
         vector_scatter(dc[0], list2, HALF, HALF + SHIFT, last[:, 0:SHIFT])
+        vector_scatter(dc[3], list2, 2 * C, T, whole[:, 2 * C : T])
         for x, t in enumerate((1, 2)):
             scalar_scatter(dc[t], list2, 2 * C, T, values[:, x, :])
         scalar_scatter(dc[0], list2, HALF + SHIFT, T, last[:, SHIFT:HALF])
@@ -226,18 +227,19 @@ def tile_moe_seb_relu2_kernel(
         codes = [sb.tile([P, C], U32, name="codes_%d" % e, align_bytes=64) for e in range(E)]
         planes = [sb.tile([P, C], U8, name="plane_%d" % e, align_bytes=64) for e in range(E)]
 
-        def first_layer(e, row_tiles, number):
+        def first_layer(e, row_tiles, number, width=C):
             acc = bank(number)
-            for x, kb in enumerate(row_tiles):
-                nc.tensor.matmul_mx(
-                    out=acc[:, x * C : (x + 1) * C],
-                    lhsT=w1[:, e, 2 * kb * P : 2 * (kb + 1) * P].bitcast(FP4X4),
-                    lhsT_scale=w1_plane[:, e, kb * P : (kb + 1) * P],
-                    rhs=codes[e][:].bitcast(FP8X4),
-                    rhs_scale=planes[e][:],
-                    start=True,
-                    stop=True,
-                )
+            for lo in range(0, C, width):
+                for x, kb in enumerate(row_tiles):
+                    nc.tensor.matmul_mx(
+                        out=acc[:, x * C + lo : x * C + lo + width],
+                        lhsT=w1[:, e, 2 * kb * P : 2 * (kb + 1) * P].bitcast(FP4X4),
+                        lhsT_scale=w1_plane[:, e, kb * P : (kb + 1) * P],
+                        rhs=codes[e][:, lo : lo + width].bitcast(FP8X4),
+                        rhs_scale=planes[e][:, lo : lo + width],
+                        start=True,
+                        stop=True,
+                    )
             return acc
 
         def copy_out(copy, acc, name, tag=None):
@@ -293,7 +295,7 @@ def tile_moe_seb_relu2_kernel(
         for t in (1, 3, 2):
             nc.scalar.activation(picked_2[:, t, :], dc[t][:].indirect(entries(list1, 2 * C, T)), COPY)
         pairs = multiply(picked_1, 1, "h0")
-        acc = first_layer(0, (1, 0), 0)
+        acc = first_layer(0, (1, 0), 0, P)
         s0_low = copy_out(nc.vector.tensor_copy, acc[:, 0:HALF], "s0_low")
         s0_high = copy_out(nc.vector.tensor_copy, first_layer(0, (2, 3), 7)[:], "s0_high")
         scalar_scatter(dx[1], list1, 0, C, s0_low[:, 0:C])
@@ -305,19 +307,18 @@ def tile_moe_seb_relu2_kernel(
         quantise(h1[:], codes[1][:], planes[1][:])
         pairs = multiply(picked_2, 2, "h1")
         vector_scatter(dx[0], list1, P, C, s0_rest[:])
-        acc = first_layer(1, (0, 1), 1)
-        s1_0 = copy_out(nc.vector.tensor_copy, acc[:, 0:C], "s1_0")
+        s1_0 = copy_out(nc.vector.tensor_copy, first_layer(1, (0,), 1)[:, 0:C], "s1_0")
         s1_high = copy_out(nc.vector.tensor_copy, first_layer(1, (2, 3), 2)[:], "s1_high")
         for x, kb in enumerate((2, 3)):
             scalar_scatter(dx[kb], list1, C, 2 * C, s1_high[:, x * C : (x + 1) * C])
         vector_scatter(dx[0], list1, C, 2 * C, s1_0[:])
         h2 = weave_words(pairs, "h2")
-        s1_1 = copy_out(nc.vector.tensor_copy, acc[:, C:W], "s1_1", "h1")
+        s1_1 = copy_out(nc.vector.tensor_copy, first_layer(1, (1,), 3)[:, 0:C], "s1_1", "h1")
         quantise(h2[:], codes[2][:], planes[2][:])
         vector_scatter(dx[1], list1, C, HALF, s1_1[:, 0:P])
         scalar_scatter(dx[1], list1, HALF, 2 * C, s1_1[:, P:C])
         tails = [
-            copy_out(nc.vector.tensor_copy if kb < 2 else nc.scalar.copy, first_layer(2, (kb,), 3 + kb)[:, 0:C], "s2_%d" % kb)
+            copy_out(nc.vector.tensor_copy if kb < 2 else nc.scalar.copy, first_layer(2, (kb,), 4 + kb)[:, 0:C], "s2_%d" % kb)
             for kb in range(PACK)
         ]
         for kb in (0, 2, 1, 3):

from contextlib import ExitStack

import concourse.mybir as mybir

F32 = mybir.dt.float32
BF16 = mybir.dt.bfloat16
I32 = mybir.dt.int32
U32 = mybir.dt.uint32
U16 = mybir.dt.uint16
U8 = mybir.dt.uint8
FP8X4 = mybir.dt.float8_e4m3fn_x4
FP4X4 = mybir.dt.float4_e2m1fn_x4
COPY = mybir.ActivationFunctionType.Copy
MULT = mybir.AluOpType.mult
MAX = mybir.AluOpType.max
MIN = mybir.AluOpType.min

P = 128
PACK = 4
T = 768
E = 3
C = 256
W = 512
QUADRANTS = 4
SHIFT = 224
HALF = T // 2
FLOPS = 2 * 2 * W * W * T
DY_ROW = 4


def cut(lo, hi, marks):
    edges = [lo] + [m for m in marks if lo < m < hi] + [hi]
    return list(zip(edges[:-1], edges[1:]))


def tile_moe_seb_relu2_kernel(
    tc, dy_words, dy_scales, w2t_words, w2t_scales, w1t_words, w1t_scales, a, gate1, gate2, offs, offs2, out
):
    nc = tc.nc
    with ExitStack() as ctx:
        sb = ctx.enter_context(tc.tile_pool(name="sb", bufs=1))
        held = ctx.enter_context(tc.tile_pool(name="held", bufs=1))
        ps = ctx.enter_context(tc.psum_pool(name="ps", bufs=1))

        def bank(number):
            return ps.tile([P, W], F32, name="bank%d" % number, tag="bank%d" % number)

        def entries(lst, lo, hi):
            return lst[:, lo // 16 : hi // 16]

        dy_plane = sb.tile([P, T], U8, name="dy_plane", align_bytes=64)
        w2_plane = sb.tile([P, W], U8, name="w2_plane", align_bytes=64)
        w2_plane_rest = sb.tile([P, W], U8, name="w2_plane_rest", align_bytes=64)
        w1_plane = sb.tile([P, E, W], U8, name="w1_plane", align_bytes=64)
        nc.gpsimd.memset(dy_plane[:].bitcast(I32), 0)
        nc.vector.memset(w2_plane[:].bitcast(I32), 0)
        nc.vector.memset(w2_plane_rest[:].bitcast(I32), 0)
        nc.vector.memset(w1_plane[:].bitcast(I32), 0)

        list2 = sb.tile([P, T // 16], U16, name="list2")
        nc.sync.dma_start(list2[:], offs2)
        dy_tile = sb.tile([P, T], I32, name="dy_tile", align_bytes=64)
        for q in range(QUADRANTS):
            row0 = 32 * q + DY_ROW
            queue = nc.scalar if q < 2 else nc.sync
            queue.dma_start(dy_plane[:].bitcast(I32)[row0 : row0 + 4, :], dy_scales[0, 4 * q : 4 * q + 4, :].bitcast(I32))
        nc.sync.dma_start(dy_tile[:], dy_words[0].rearrange("p t d -> p (t d)").bitcast(I32))

        def load_w2(e):
            raw = sb.tile([P, W], I32, name="w2_raw_%d" % e, align_bytes=64)
            nc.sync.dma_start(raw[:], w2t_words[e, 0].rearrange("p i d -> p (i d)").bitcast(I32))
            return raw[:].bitcast(U32).rearrange("p (m t) -> p m t", t=PACK)

        w2_first = load_w2(0)
        for q in range(QUADRANTS):
            queue = nc.scalar if q == 0 else nc.sync
            queue.dma_start(w2_plane[:].bitcast(I32)[32 * q : 32 * q + 8, :], w2t_scales[0:2, 0, 4 * q : 4 * q + 4, :].bitcast(I32))
        g2 = sb.tile([P, T], F32, name="g2")
        nc.sync.dma_start(g2[:, 0:HALF], gate2[:, 0:HALF])
        w2_second = load_w2(1)
        a_rows = a.rearrange("(p t) j -> p t j", t=PACK)
        w2_third = load_w2(2)
        nc.sync.dma_start(g2[:, HALF:T], gate2[:, HALF:T])
        for q in range(QUADRANTS):
            nc.sync.dma_start(
                w2_plane_rest[:].bitcast(I32)[32 * q : 32 * q + 4, :], w2t_scales[2, 0, 4 * q : 4 * q + 4, :].bitcast(I32)
            )
        a_late = sb.tile([P, PACK, 2 * C], F32, name="a_late")
        nc.sync.dma_start(a_late[:], a_rows[:, :, C:T])
        g1 = sb.tile([P, T], F32, name="g1")
        nc.sync.dma_start(g1[:], gate1)
        a_early = sb.tile([P, PACK, C], F32, name="a_early")
        nc.sync.dma_start(a_early[:], a_rows[:, :, 0:C])
        for q in range(QUADRANTS):
            nc.sync.dma_start(
                w1_plane[:].bitcast(I32)[32 * q : 32 * q + 4, :, :],
                w1t_scales[:, 0, 4 * q : 4 * q + 4, :].rearrange("e r i -> r e i").bitcast(I32),
            )
        w1 = sb.tile([P, E, 2 * W], U8, name="w1", align_bytes=64)
        nc.sync.dma_start(w1[:].bitcast(I32), w1t_words[:, 0].rearrange("e p b -> p e b").bitcast(I32))
        list1 = sb.tile([P, T // 16], U16, name="list1")
        nc.sync.dma_start(list1[:], offs)

        def sort_scales(engine, plane, ordered):
            engine.tensor_copy(ordered[:].rearrange("p (t m) -> p t m", t=PACK), plane[:].rearrange("p (m t) -> p t m", t=PACK))
            return ordered

        def gather_bytes(picked, lo, hi):
            nc.vector.tensor_copy(picked, dy_plane[:].indirect(entries(list2, lo, hi)))

        def gather_words(picked, lo, hi):
            nc.vector.tensor_copy(picked, dy_tile[:].bitcast(U32).indirect(entries(list2, lo, hi)))

        def second_layer(acc, weights, weight_scales, t, words, scales):
            nc.tensor.matmul_mx(
                out=acc,
                lhsT=weights[:, t * P : (t + 1) * P].bitcast(FP8X4),
                lhsT_scale=weight_scales[:, t * P : (t + 1) * P],
                rhs=words.bitcast(FP8X4),
                rhs_scale=scales,
                start=True,
                stop=True,
            )

        def gated(into, acc, gate):
            nc.vector.scalar_tensor_tensor(into, acc, 2.0, gate, MULT, MULT)

        def scalar_scatter(window, lst, lo, hi, values):
            nc.scalar.activation(window[:].indirect(entries(lst, lo, hi)), values, COPY)

        def vector_scatter(window, lst, lo, hi, values):
            nc.vector.tensor_copy(window[:].indirect(entries(lst, lo, hi)), values)

        w2_lead = sb.tile([P, P], U32, name="w2_lead", align_bytes=64)
        nc.scalar.copy(w2_lead[:], w2_first[:, :, 0])
        w2_sorted = {e: sb.tile([P, W], U32, name="w2_sorted_%d" % e, align_bytes=64) for e in range(2)}
        nc.scalar.copy(w2_sorted[0][:].rearrange("p (t m) -> p m t", t=PACK)[:, :, 1:], w2_first[:, :, 1:])
        scales_head = sb.tile([P, HALF], U8, name="scales_head", align_bytes=64)
        gather_bytes(scales_head[:], 0, HALF)
        words = {0: sb.tile([P, C], U32, name="words_0", align_bytes=64)}
        gather_words(words[0][:, 0:P], 0, P)
        gather_words(words[0][:, P:C], P, C)
        by_plane = w2_plane[:].rearrange("p (m t) -> p t m", t=PACK)
        scale_lead = sb.tile([P, P], U8, name="scale_lead", align_bytes=64)
        nc.gpsimd.tensor_copy(scale_lead[:], by_plane[:, 0, :])
        w2_scale_head = sb.tile([P, W], U8, name="w2_scale_head", align_bytes=64)
        nc.gpsimd.tensor_copy(w2_scale_head[:].rearrange("p (t m) -> p t m", t=PACK)[:, 1:, :], by_plane[:, 1:, :])
        nc.gpsimd.tensor_copy(w2_sorted[1][:].rearrange("p (t m) -> p t m", t=PACK), w2_second.rearrange("p m t -> p t m"))
        w2_scales = {0: w2_scale_head[:], 1: w2_scale_head[4:P, :]}
        words[1] = sb.tile([P, C], U32, name="words_1", align_bytes=64)
        gather_words(words[1][:], C, 2 * C)
        dy_picked = {0: scales_head}

        def sums_of(pieces, number):
            acc = bank(number)
            at = 0
            for t, lo, hi in pieces:
                for x0, x1 in cut(lo, hi, (C, HALF, 2 * C)):
                    e, half = x0 // C, x0 // HALF
                    second_layer(
                        acc[:, at + x0 - lo : at + x1 - lo],
                        w2_lead if (e, t) == (0, 0) else w2_sorted[e],
                        scale_lead[4 * e : P, :] if t == 0 and e < 2 else w2_scales[e],
                        t,
                        words[e][:, x0 - e * C : x1 - e * C],
                        dy_picked[half][DY_ROW:P, x0 - half * HALF : x1 - half * HALF],
                    )
                at += hi - lo
            return acc[:, 0:at]

        dc = [sb.tile([P, T], F32, name="dc_%d" % t) for t in range(PACK)]

        def products(values, t, lo, hi, number):
            gated(values[:], sums_of(((t, lo, hi),), number), g2[:, lo:hi])
            return values

        def paired(e, number):
            values = sb.tile([P, 2, C], F32, name="pair_%d" % e)
            gated(
                values[:],
                sums_of([(t, e * C, (e + 1) * C) for t in (1, 2)], number).rearrange("p (x j) -> p x j", x=2),
                g2[:, e * C : (e + 1) * C].unsqueeze(1).to_broadcast([P, 2, C]),
            )
            return values

        lead = held.tile([P, P], F32, name="lead", offset=1024, align_bytes=64)
        scalar_scatter(dc[0], list2, 0, P, products(lead, 0, 0, P, 0)[:])
        second = sb.tile([P, C], F32, name="second")
        scalar_scatter(dc[1], list2, 0, C, products(second, 1, 0, C, 1)[:])
        scalar_scatter(dc[2], list2, 0, C, products(sb.tile([P, C], F32, name="third"), 2, 0, C, 2)[:])
        scalar_scatter(dc[0], list2, P, HALF, products(sb.tile([P, C], F32, name="fourth"), 0, P, HALF, 3)[:])
        dy_picked[1] = held.tile([P, HALF], U8, name="scales_tail", offset=1024, align_bytes=64)
        gather_bytes(dy_picked[1][:], HALF, T)
        words[2] = held.tile([P, C], U32, name="words_2", offset=1024 + HALF, align_bytes=64)
        gather_words(words[2][:], 2 * C, T)
        w2_sorted[2] = sb.tile([P, W], U32, name="w2_sorted_2", align_bytes=64)
        nc.gpsimd.tensor_copy(w2_sorted[2][:].rearrange("p (t m) -> p t m", t=PACK), w2_third.rearrange("p m t -> p t m"))
        w2_scales[2] = sort_scales(nc.gpsimd, w2_plane_rest, sb.tile([P, W], U8, name="w2_scale_rest", align_bytes=64))[:]
        slope = sb.tile([P, PACK, 2 * C], F32, name="slope")
        nc.gpsimd.tensor_scalar(slope[:], a_late[:], float("inf"), 0.0, MIN, MAX)
        factor = {e: sb.tile([P, PACK, C], F32, name="factor_%d" % e) for e in (1, 2)}
        for e in (1, 2):
            nc.gpsimd.tensor_tensor(
                factor[e][:], slope[:, :, (e - 1) * C : e * C], g1[:, e * C : (e + 1) * C].unsqueeze(1).to_broadcast([P, PACK, C]), MULT
            )
        whole = sb.tile([P, T], F32, name="whole")
        products(whole[:, 0 : 2 * C], 3, 0, 2 * C, 6)
        values = paired(1, 4)
        for x, t in enumerate((1, 2)):
            scalar_scatter(dc[t], list2, C, 2 * C, values[:, x, :])
        vector_scatter(dc[3], list2, 0, 2 * C, whole[:, 0 : 2 * C])
        values = paired(2, 0)
        last = products(sb.tile([P, HALF], F32, name="last"), 0, HALF, T, 5)
        products(whole[:, 2 * C : T], 3, 2 * C, T, 7)
        vector_scatter(dc[0], list2, HALF, HALF + SHIFT, last[:, 0:SHIFT])
        vector_scatter(dc[3], list2, 2 * C, T, whole[:, 2 * C : T])
        for x, t in enumerate((1, 2)):
            scalar_scatter(dc[t], list2, 2 * C, T, values[:, x, :])
        scalar_scatter(dc[0], list2, HALF + SHIFT, T, last[:, SHIFT:HALF])

        def gather(into, t, lo, hi):
            nc.vector.tensor_tensor(into, dc[t][:].indirect(entries(list1, lo, hi)), g1[:, lo:hi], MULT)

        def quantise(h, codes, plane):
            nc.vector.quantize_mx(out=codes.bitcast(FP8X4), scales=plane, in_=h.rearrange("p j t -> p (j t)"))

        codes = [sb.tile([P, C], U32, name="codes_%d" % e, align_bytes=64) for e in range(E)]
        planes = [sb.tile([P, C], U8, name="plane_%d" % e, align_bytes=64) for e in range(E)]

        def first_layer(e, row_tiles, number, width=C):
            acc = bank(number)
            for lo in range(0, C, width):
                for x, kb in enumerate(row_tiles):
                    nc.tensor.matmul_mx(
                        out=acc[:, x * C + lo : x * C + lo + width],
                        lhsT=w1[:, e, 2 * kb * P : 2 * (kb + 1) * P].bitcast(FP4X4),
                        lhsT_scale=w1_plane[:, e, kb * P : (kb + 1) * P],
                        rhs=codes[e][:, lo : lo + width].bitcast(FP8X4),
                        rhs_scale=planes[e][:, lo : lo + width],
                        start=True,
                        stop=True,
                    )
            return acc

        def copy_out(copy, acc, name, tag=None):
            sums = sb.tile([P, acc.shape[1]], F32, name=name, tag=tag or name, align_bytes=64)
            copy(sums[:], acc)
            return sums

        def multiply(picked, e, tag):
            pairs = sb.tile([P, 2, C, 2], BF16, name="pairs_%d" % e, tag=tag, align_bytes=64)
            nc.gpsimd.tensor_tensor(
                pairs[:].rearrange("p u j e -> p u e j"),
                picked[:].rearrange("p (u e) j -> p u e j", e=2),
                factor[e][:].rearrange("p (u e) j -> p u e j", e=2),
                MULT,
            )
            return pairs

        def weave_words(pairs, name):
            h = sb.tile([P, C, PACK], BF16, name=name, tag=name, align_bytes=64)
            nc.vector.tensor_copy(
                h[:].rearrange("p j t -> p (j t)").bitcast(I32).rearrange("p (j u) -> p j u", u=2),
                pairs[:].rearrange("p u j e -> p (u j e)").bitcast(I32).rearrange("p (u j) -> p j u", u=2),
            )
            return h

        dx = [sb.tile([P, T], F32, name="dx_%d" % kb) for kb in range(PACK)]

        def store(kb):
            nc.sync.dma_start(out[kb * P : (kb + 1) * P, :], dx[kb][:])

        first = sb.tile([P, PACK, C], F32, name="first", tag="first", align_bytes=64)
        for t in (1, 3, 2):
            gather(first[:, t, :], t, 0, C)
        picked_1 = sb.tile([P, PACK, C], F32, name="picked_1")
        for t in (1, 3, 2, 0):
            nc.scalar.activation(picked_1[:, t, :], dc[t][:].indirect(entries(list1, C, 2 * C)), COPY)
        h0 = sb.tile([P, C, PACK], BF16, name="h0", tag="h0", align_bytes=64)
        for lo in (0, P):
            gather(first[:, 0, lo : lo + P], 0, lo, lo + P)
        for lo in (0, P):
            nc.vector.scalar_tensor_tensor(
                h0[:, lo : lo + P, :],
                a_early[:, :, lo : lo + P].rearrange("p t j -> p j t"),
                0.0,
                first[:, :, lo : lo + P].rearrange("p t j -> p j t"),
                MAX,
                MULT,
            )
        for lo in (0, P):
            quantise(h0[:, lo : lo + P, :], codes[0][:, lo : lo + P], planes[0][:, lo : lo + P])
        picked_2 = sb.tile([P, PACK, C], F32, name="picked_2", tag="first", align_bytes=64)
        nc.vector.tensor_copy(picked_2[:, 0, :], dc[0][:].indirect(entries(list1, 2 * C, T)))
        for t in (1, 3, 2):
            nc.scalar.activation(picked_2[:, t, :], dc[t][:].indirect(entries(list1, 2 * C, T)), COPY)
        pairs = multiply(picked_1, 1, "h0")
        acc = first_layer(0, (1, 0), 0, P)
        s0_low = copy_out(nc.vector.tensor_copy, acc[:, 0:HALF], "s0_low")
        s0_high = copy_out(nc.vector.tensor_copy, first_layer(0, (2, 3), 7)[:], "s0_high")
        scalar_scatter(dx[1], list1, 0, C, s0_low[:, 0:C])
        for x, kb in enumerate((2, 3)):
            scalar_scatter(dx[kb], list1, 0, C, s0_high[:, x * C : (x + 1) * C])
        vector_scatter(dx[0], list1, 0, P, s0_low[:, C:HALF])
        h1 = weave_words(pairs, "h1")
        s0_rest = copy_out(nc.vector.tensor_copy, acc[:, HALF:W], "s0_rest", "h0")
        quantise(h1[:], codes[1][:], planes[1][:])
        pairs = multiply(picked_2, 2, "h1")
        vector_scatter(dx[0], list1, P, C, s0_rest[:])
        s1_0 = copy_out(nc.vector.tensor_copy, first_layer(1, (0,), 1)[:, 0:C], "s1_0")
        s1_high = copy_out(nc.vector.tensor_copy, first_layer(1, (2, 3), 2)[:], "s1_high")
        for x, kb in enumerate((2, 3)):
            scalar_scatter(dx[kb], list1, C, 2 * C, s1_high[:, x * C : (x + 1) * C])
        vector_scatter(dx[0], list1, C, 2 * C, s1_0[:])
        h2 = weave_words(pairs, "h2")
        s1_1 = copy_out(nc.vector.tensor_copy, first_layer(1, (1,), 3)[:, 0:C], "s1_1", "h1")
        quantise(h2[:], codes[2][:], planes[2][:])
        vector_scatter(dx[1], list1, C, HALF, s1_1[:, 0:P])
        scalar_scatter(dx[1], list1, HALF, 2 * C, s1_1[:, P:C])
        tails = [
            copy_out(nc.vector.tensor_copy if kb < 2 else nc.scalar.copy, first_layer(2, (kb,), 4 + kb)[:, 0:C], "s2_%d" % kb)
            for kb in range(PACK)
        ]
        for kb in (0, 2, 1, 3):
            scatter = vector_scatter if kb < 2 else scalar_scatter
            scatter(dx[kb], list1, 2 * C, T, tails[kb][:])
            store(kb)
